import numpy as np, ml_dtypes
CORES = [35,38,43,46]
N = 4
BF = ml_dtypes.bfloat16
def gentries(a):
    return np.ascontiguousarray(a.reshape(8, 16, -1).transpose(0, 2, 1)).reshape(8, -1)
def gtable(e):
    e = np.asarray(e); return np.ascontiguousarray(e.reshape(8, -1, 16).transpose(0, 2, 1)).reshape(128, -1).astype(np.int32)
W, K, Q, ST, EV = 4096, 256, 2, 6, 2
def parts(rng):
    return {"turn": np.argsort(rng.random((8, W)), axis=1), "tw": rng.integers(0, 256, (8, 16, W)), "img": rng.integers(0, W, (N, 8, K, 16)),
            "ent": rng.integers(0, W, (N, 8, Q, W)), "elen": rng.integers(0, 25, (N, 8, W)), "own": rng.integers(0, W, (N, 8, Q, K)), "olen": rng.integers(0, 25, (N, 8, K))}
def flock(rng, img, share):
    c = np.where(rng.random((N, 8, K)) < share, rng.integers(0, K, (N, 8, K)), np.arange(K))
    o = np.argsort(rng.random(img.shape), axis=3)
    return np.take_along_axis(np.take_along_axis(img, c[..., None], 2), o, 3)
def pack(p):
    return {"turn": np.tile(p["turn"][None], (N, 1, 1)).astype(np.int32), "twist": np.tile(p["tw"].reshape(1, 128, W), (N, 1, 1)).astype(np.float32).astype(BF),
            "img": np.stack([gtable(a.reshape(8, 16 * K)) for a in p["img"]]), "ent": p["ent"].reshape(N, 8, Q * W).astype(np.int32), "elen": p["elen"].astype(np.int32),
            "own": p["own"].reshape(N, 8, Q * K).astype(np.int32), "olen": p["olen"].astype(np.int32)}
def setup_inputs(rng):
    p = parts(rng); p["img"] = flock(rng, p["img"], 0.4)
    return pack(p)
def setup_inputs_crowd(rng):
    p = parts(rng); base = rng.integers(0, W, (N, 8, 3, 16)); c = rng.integers(0, 3, (N, 8, K)); c[:, ::2] = 0
    p["img"] = np.take_along_axis(base, c[..., None], 2)
    p["olen"] = 5 + rng.integers(0, 2, (N, 8, K)) * rng.integers(0, 2, (N, 8, 1)); p["elen"] = rng.integers(0, 60, (N, 8, W))
    x = np.arange(W); j = np.arange(K)
    p["elen"][:, 2::2] = rng.integers(2000, 4096, (N, 3, W))
    p["olen"][:, 2] = 3 * (K - 1 - j) + int(rng.integers(0, 100)); p["olen"][:, 6] = 3 * j + int(rng.integers(0, 100))
    two = np.argsort(rng.random((N, W)), axis=1)[:, :8 * K].reshape(N, K // 2, 16)
    p["img"][:, 4] = two[:, rng.permutation(K) % (K // 2)]; p["olen"][:, 4] = rng.integers(0, 4, (N, K))
    n = K // ST; hop = W // (ST * Q); odd = 2 * int(rng.integers(1, W // 2)) + 1; o = (x * odd + int(rng.integers(0, W))) % W
    p["turn"][5] = (x + hop * odd) % W
    s = rng.permutation(K); a = np.minimum(j // n, ST - 1)[s]; i = (j % n)[s]
    p["img"][:, 5] = np.repeat(o[(i - a * Q * hop) % W][:, None], 16, axis=1)
    p["olen"][:, 5] = 3000 - 400 * a + rng.integers(0, 200, (N, K))
    p["elen"][:, 5] = 0; p["elen"][:, 5, o[:n]] = rng.integers(3500, 4096, (N, n))
    return pack(p)
def setup_inputs_ends(rng):
    p = parts(rng); v = np.array([0, 1, W // 2, W - 1]); e = np.array([0, 1, 4094, 4095]); x = np.arange(W)
    p["turn"][0] = x; p["turn"][1] = x[::-1]; p["turn"][2] = (x + 1) % W
    p["tw"][3] = 0; p["tw"][4] = 255 * rng.integers(0, 2, (16, W)); p["tw"][5] = 255
    p["img"][:, ::2] = rng.choice(v, (N, 4, K, 16)); p["img"][:, 1] = np.repeat(p["img"][:, 1, :, :1], 16, axis=2)
    p["ent"][:, 1:5] = rng.choice(v, (N, 4, Q, W)); p["own"][:, 1:5] = rng.choice(v, (N, 4, Q, K))
    p["elen"] = rng.choice(e, (N, 8, W)); p["olen"] = rng.choice(e, (N, 8, K)); p["olen"][int(rng.integers(0, N))] = 4095
    return pack(p)
def setup_inputs_full(rng):
    p = parts(rng); hop = W // (ST * Q); x = np.arange(W); j = np.arange(K)
    for g in range(8):
        c = int(rng.integers(1, W))
        if g < 4:
            o = (16 * np.argsort(rng.random((16, W // 16)), axis=1) + rng.permutation(16)[:, None]).reshape(W)
            p["ent"][:, g] = c; p["own"][:, g] = c
        else:
            o = (x * (2 * int(rng.integers(1, W // 2)) + 1) + int(rng.integers(0, W))) % W
        sig = np.zeros(W, np.int64); sig[o] = o[(x + hop) % W]
        p["turn"][g, (x + c) % W] = (sig + c) % W
        n = K if g % 2 else min(2 * K, Q * hop); z = np.argsort(rng.random((N, n)), axis=1)
        pts = o[np.stack([z[:, :K], z[:, np.where(K + j < n, K + j, j)]], axis=2)]
        p["img"][:, g] = np.take_along_axis(pts, np.argsort(rng.random((N, K, 16)), axis=2) % 2, 2)
        p["elen"][:, g, o] = 100 * (np.minimum(x // (Q * hop), ST - 1) + 1) + rng.integers(0, 50, (N, W)); p["olen"][:, g] = rng.integers(0, 50, (N, K))
    return pack(p)
def setup_inputs_spread(rng):
    p = parts(rng)
    p["tw"] = np.minimum((np.exp2(8 * rng.random((8, 1, W))) * rng.random((8, 16, W))).astype(np.int64), 255)
    p["img"] = flock(rng, np.minimum((W * rng.random((N, 8, K, 16)) ** 3).astype(np.int64), W - 1), 0.3)
    p["ent"] = np.minimum((W * rng.random((N, 8, Q, W)) ** 2).astype(np.int64), W - 1)
    p["elen"] = np.minimum(np.exp2(12 * rng.random((N, 8, W))).astype(np.int64), 4095); p["olen"] = np.minimum(np.exp2(12 * rng.random((N, 8, K))).astype(np.int64) - 1, 4095)
    return pack(p)
def setup_inputs_ties(rng):
    p = parts(rng); o = np.argsort(rng.random((8, 16, W)), axis=1)
    p["tw"] = o % 2 * 128; p["tw"][1] = o[1]; p["tw"][5] = o[5]; p["tw"][3::4] = rng.integers(0, 4, (2, 16, W))
    p["img"] = flock(rng, p["img"], 0.7)
    low = rng.permutation(np.array([0, 0, 0, 252, 1020, 2048, 3000, 4088])).reshape(1, 8, 1)
    p["elen"] = low + rng.integers(3, 6, (N, 8, W)); p["olen"] = low + rng.integers(3, 6, (N, 8, K))
    return pack(p)
def check_inputs(d):
    bad = []
    for k, hi in (("turn", W - 1), ("img", W - 1), ("ent", W - 1), ("own", W - 1), ("elen", 4095), ("olen", 4095)):
        if np.min(d[k]) < 0 or np.max(d[k]) > hi: bad.append("range of " + k)
    t = np.asarray(d["twist"]).astype(np.float32)
    if not np.all((t >= 0) & (t <= 255) & (t == np.floor(t))): bad.append("twist: whole numbers from 0 to 255")
    if not np.all(t == t[:1]): bad.append("twist alike on all ranks")
    if not np.all(np.sort(d["turn"], axis=2) == np.arange(W)): bad.append("turn: permutations")
    if not np.all(d["turn"] == d["turn"][:1]): bad.append("turn alike on all ranks")
    return bad
def reference(turn, twist, img, ent, elen, own, olen):
    pt = turn.astype(np.int64); tw = twist.astype(np.float32).astype(np.int64).reshape(N, 8, 16, W)
    b = np.stack([gentries(a) for a in img]).astype(np.int64)
    f = np.take_along_axis(tw, b[:, :, None, :], 3)
    e = ent.astype(np.int64).reshape(N, 8, Q, W); l = elen.astype(np.int64); o = own.astype(np.int64).reshape(N, 8, Q, K); m = olen.astype(np.int64)
    ri = np.arange(N).reshape(N, 1, 1); gi = np.arange(8).reshape(1, 8, 1); big = 2 ** 40
    for step in range(1, ST + 1):
        d = np.argmax(np.add.reduce(f, axis=2).reshape(N, 8, K, 16), axis=3)
        w = np.take_along_axis(b.reshape(N, 8, K, 16), d[..., None], 3)[..., 0]
        a = np.take_along_axis(e, w[:, :, None, :], 3); al = np.take_along_axis(l, w, 2)
        for q in range(Q):
            s = np.repeat(a[:, :, q], 16, axis=2); u = (b + s) & (W - 1)
            f = (f + np.take_along_axis(tw, u[:, :, None, :], 3)) & 255
            b = (np.take_along_axis(pt, u, 2) - s) & (W - 1)
        key = np.where(m < al, m * K + np.arange(K), big); best = np.full((N, 8, W), big)
        np.minimum.at(best, (ri, gi, w), key)
        won = (m < al) & (key == np.take_along_axis(best, w, 2))
        r1, g1, j1 = np.nonzero(won); x1 = w[r1, g1, j1]
        e[r1, g1, :, x1] = o[r1, g1, :, j1]; l[r1, g1, x1] = m[r1, g1, j1]
        m = np.where(won, al, m) + Q; o = a
        if step % EV == 0: e = np.roll(e, 1, axis=0); l = np.roll(l, 1, axis=0)
    return {"yimg": np.ascontiguousarray(b.reshape(N, 8, K, 16).transpose(0, 1, 3, 2)).reshape(N, 128, K).astype(np.float32), "yf": f.reshape(N, 128, 16 * K).astype(np.float32).astype(BF),
            "yent": e.reshape(N, 8, Q * W).astype(np.float32), "yelen": l.astype(np.float32)}

@@ -1,0 +1,548 @@
+from concourse.mybir import AluOpType as Al, AxisListType, ActivationFunctionType as Af
+
+F, B, H16, I, U = "float32", "bfloat16", "float16", "int32", "uint16"
+NP = 4
+NZD = 4
+ZO = 7
+X0A = 4
+ESA = 1
+HA, BV, YV, RA, RF = 1, 8, 0, 4, 4
+CV, CA, CP, CQ, SY, GC = 0.06, 0.08, 0.0005, 0.05, 0.1, 1.55
+LOOK, BIAS, WB = 0.0, 1.0, 0.0
+CB = {'acn6': -0.5, 'vcj3': 2, 'acn9': 2, 'ay1.': -1.0, 'pT0': 0.5, 'vWn': 1, 'vWm0': 2, 'vWz1': -1, 'vcf': -1, 'vm': -0.5, 'vcmp': -1, 'voU0': 0.5, 've15': 1, 'gsnd': 2, 'vWm1': 2, 'gA8': 2, 'vcpv': -1, 'vbit': -1.5, 'scI0': 0.5, 'vwi0': 0.5, 'acn8': -1.0, 'aRb1': 1, 'pP3': -1, 'vdE0': -1, 'vMz': 1, 'gtf0': -2, 'vES1': -1, 'vt1': -1, 'pP1': 1, 'vnn1': -1.5, 'vRm0': -2, 'vH3': 0.5, 'acn5': -0.5, 'voS1': -1, 'vdE1': 0.5, 'acn3': 0.5, 'pZ0': -1.5, 'pP2': -2, 'vH1': 1, 'acn0': -0.5, 'aX3.': 1, 'vtab': -2, 'vnn0': 2, 'vA8b': 1, 'vkb': 0.5}
+MG = 12582912.0
+
+
+def _sb(n, d):
+    return ("sbuf", [128, n], d)
+
+
+SCRATCH = {
+    "tw": _sb(4096, B), "Hw": _sb(16384, B), "bits": _sb(4096, B), "tab0": _sb(4352, F), "tab1": _sb(4352, F), "Xi": _sb(2048, B),
+    "X0": _sb(2048, H16), "X1": _sb(2048, H16), "X2": _sb(2048, H16), "G0": _sb(2048, B), "G1": _sb(2048, B), "G2": _sb(2048, B),
+    "y0": _sb(2048, B), "y1": _sb(2048, B), "fo": _sb(2048, B), "Rb0": _sb(512, B), "Rb1": _sb(512, B),
+    "imgi": _sb(256, I), "imgf": _sb(256, F), "offI": _sb(256, U), "tci": _sb(512, I), "ta": _sb(512, F), "ki": _sb(512, I), "kj": _sb(512, I), "kb16": _sb(512, B),
+    "cmpI": _sb(768, I), "cmp": _sb(768, F), "land0": _sb(768, F), "land1": _sb(768, F), "land2": _sb(768, F),
+    "lv0": _sb(256, F), "lv1": _sb(256, F), "lv2": _sb(256, F), "lo0": _sb(16, U), "lo1": _sb(16, U), "lo2": _sb(16, U),
+    "owni": _sb(256, I), "A0": _sb(256, H16), "A1": _sb(256, H16), "V0": _sb(256, F), "V1": _sb(256, F), "XR": _sb(256, H16), "XL0": _sb(256, B), "XL1": _sb(256, B),
+    "IM": _sb(128, F), "IG": _sb(128, F), "A8": ("sbuf", [128, 8, 16], F), "xi": _sb(272, F), "xj": _sb(272, I), "xk": _sb(272, I), "Plo": _sb(256, B), "Phi": _sb(16, F),
+    "pi": _sb(8, I), "col": _sb(48, F), "POW": _sb(96, F), "i8": _sb(16, F), "isl": _sb(16, F), "SL": _sb(16, B), "z16": _sb(16, F),
+    "Ib": _sb(128, B), "If": _sb(128, F), "nI": _sb(128, B), "ones": _sb(128, B),
+    "Dp0": _sb(128, B), "Dm1": _sb(128, B), "D01": _sb(128, B), "S01": _sb(128, B), "DB": _sb(128, B), "J3": _sb(128, B),
+    "BD": _sb(128, B), "bd1": _sb(128, B), "bd2": _sb(128, B), "bd3": _sb(128, B), "bd4": _sb(128, B), "BC": _sb(1024, B), "CTW": _sb(144, B),
+    "RR": _sb(32, B), "CK": _sb(256, B), "CKP": _sb(512, B), "seg": _sb(128, F), "JT": _sb(256, B), "JB": _sb(16, F), "DUM": _sb(16, F),
+    "ES0": _sb(128, F), "ES1": _sb(128, F), "Rm0": _sb(128, F), "Rm1": _sb(128, F), "nn0": _sb(128, B), "nn1": _sb(128, B),
+    "dE0": _sb(128, F), "dE1": _sb(128, F), "e15": _sb(16, F), "Wm0": _sb(128, F), "Wm1": _sb(128, F),
+    "wi": _sb(16, I), "wj": _sb(16, I), "Wz": _sb(256, F), "Wn": _sb(256, F), "MK": _sb(256, F), "ogi": _sb(16, I), "offG": _sb(16, U), "OH": _sb(8, F), "DT": _sb(16, F), "Mz": _sb(256, H16),
+    "offO0": _sb(16, U), "offO1": _sb(16, U), "offU0": _sb(256, U), "offU1": _sb(256, U), "offS0": _sb(16, U), "offS1": _sb(16, U),
+    "ui": _sb(256, I), "uj": _sb(256, I), "yi": _sb(256, F), "AT0": _sb(32, F), "AT1": _sb(32, F), "tn": _sb(192, F), "cnt": _sb(16, F), "junk": _sb(4096, B),
+    "pP": ("psum", [128, 2048], F), "pT0": ("psum", [128, 512], F), "pT1": ("psum", [128, 512], F), "pZ0": ("psum", [128, 512], F), "pZ1": ("psum", [128, 512], F),
+}
+SEMAPHORES = ["cv", "ca", "cp", "cg"] + ["d%d" % k for k in range(90)] + ["r%d" % k for k in range(9)]
+
+
+def build(T, topo, core, rank):
+    ops = []; tail = {}
+    n4 = len(T.cores)
+    nxt, prv = T.cores[(rank + 1) % n4], T.cores[(rank - 1) % n4]
+    rid, pid = topo.addr(nxt)[0], topo.addr(nxt)[1]
+    nout, nin = len(topo.engines(core, nxt)), len(topo.engines(prv, core))
+
+    def op(e, t, r, w, fn, b=(), kind="c", lat=0.0, sem=None):
+        ops.append({"e": e, "t": t, "r": list(r), "w": list(w), "b": list(b), "fn": fn, "k": kind, "lat": lat, "sem": sem})
+
+    def v(n, r, w, fn, b=()):
+        op("v", CV + max(n, 40) * 0.001, r, w, fn, b)
+
+    def gp(n, r, w, fn):
+        op("g", 0.15 + n * 0.002, r, w, fn)
+
+    def mm(r, b, lst):
+        lst = [list(x) + [True] for x in lst]
+        for x in lst:
+            if not x[3]:
+                tail[b[0]][5] = False
+            tail[b[0]] = x
+
+        def fn(q):
+            last = None
+            for o, l, x, s0, c, s1 in lst:
+                last = q.matmul(o, l, x, s0, s1)
+            return last
+        op("p", CQ + sum(m[4] for m in lst) * CP, r, [], fn, b)
+
+    def dma(e, kb, r, w, out, src):
+        op(e, 0.1, r, w, lambda q: q.dma_start(out, src), kind="d", lat=2.0 + kb / 200.0)
+
+    def send(k, kb, r, w, dst, src):
+        op("g", 0.3, r, ["snd%d" % k], lambda q, ls: q.remote_dma(dst, src, T.sem["r%d" % k], ls, pid, rid, topo.mask(core, nxt)), kind="s", lat=2.0 + kb / 80.0)
+        op("x", 0.0, ["snd%d" % k], w, None, kind="x", lat=0.5, sem=("r%d" % k, nin))
+
+    def ts(n, r, w, out, in0, s1, s2, o0, o1=None, b=()):
+        if o1 is None:
+            v(n, r, w, lambda q: q.tensor_scalar(out, in0, s1, None, o0), b)
+        else:
+            v(n, r, w, lambda q: q.tensor_scalar(out, in0, s1, s2, o0, o1), b)
+
+    def tt(n, r, w, out, x, y, o, b=()):
+        v(n, r, w, lambda q: q.tensor_tensor(out, x, y, o), b)
+
+    def cp(n, r, w, out, x, b=()):
+        v(n, r, w, lambda q: q.tensor_copy(out, x), b)
+
+    def ms(n, w, out, c, r=()):
+        v(n, r, w, lambda q: q.memset(out, c))
+
+    def act(n, r, w, out, x, f, bias=0.0, scale=1.0, b=(), acc=None):
+        op("a", CA + max(n, 40) * 0.001, r, w, lambda q: q.activation(out, x, f, bias=bias, scale=scale, accum_out=acc), b)
+
+    def iota(n, w, out, pat, base, cm, flt=True, r=()):
+        if flt:
+            gp(n, r, w, lambda q: q.iota(out, pat, base, cm, allow_small_or_imprecise_dtypes=True))
+        else:
+            gp(n, r, w, lambda q: q.iota(out, pat, base, cm))
+
+    tab = [T.tab0, T.tab1]; X = [T.X0, T.X1, T.X2, T.Xi]; G = [T.G0, T.G1, T.G2]; A = [T.A0, T.A1]; V = [T.V0, T.V1]
+    pT = [T.pT0, T.pT1]; pZ = [T.pZ0, T.pZ1]; ES = [T.ES0, T.ES1]; offO = [T.offO0, T.offO1]; offU = [T.offU0, T.offU1]; offS = [T.offS0, T.offS1]
+    AT = [T.AT0, T.AT1]; XL = [T.XL0, T.XL1]
+    PW = 2048 // NP; PL = 128 // NP
+    allp = lambda s: ["%s.%d" % (s, k) for k in range(NP)]
+
+    dma("s", 512, [], ["tw0"], T.tw[:, 0:2048], T.twist[:, 0:2048])
+    dma("a", 512, [], ["tw1"], T.tw[:, 2048:4096], T.twist[:, 2048:4096])
+    dma("s", 128, [], ["imgi"], T.imgi[:], T.img[:])
+    dma("a", 128, [], ["tc0"], T.tci[0:64, :], T.turn[:])
+    dma("s", 128, [], ["tc1"], T.tci[64:128, :], T.turn[:])
+    iota(256, ["owni"], T.owni[:], [[0, 256]], 0, 0, False)
+    for q in range(2):
+        dma("s", 128, [], ["cI%d" % q], T.cmpI[:, 256 * q:256 * q + 256], T.ent[:, 4096 * q:4096 * q + 4096])
+        dma("s", 8, ["owni"], ["ow%d" % q], T.owni[q:128:16, :], T.own[:, 256 * q:256 * q + 256])
+    dma("s", 128, [], ["cI2"], T.cmpI[:, 512:768], T.elen[:])
+    dma("s", 8, ["owni"], ["ow2"], T.owni[2:128:16, :], T.olen[:])
+
+    iota(8, ["pi0"], T.pi[:, 0:1], [[0, 1]], 0, 1, False)
+    iota(16, ["i8"], T.i8[:], [[1, 16]], 0, 0)
+    iota(128, ["IM"], T.IM[:], [[1, 128]], 0, 0)
+    iota(128, ["IG"], T.IG[:], [[16, 8], [0, 16]], 0, 0)
+    iota(128, ["A8"], T.A8[:], [[8, 8], [0, 16]], 0, 0)
+    iota(16, ["isl"], T.isl[:], [[1, 2], [16, 8]], 1, 0)
+    ms(128, ["CK"], T.CK[:], 0.0); iota(512, ["CKP0"], T.CKP[:], [[0, 512]], 0, 0); iota(512, ["CKP"], T.CKP[0:1, :], [[0, 512]], -49152, 0, r=["CKP0"])
+    ms(1, ["dE0"], T.dE0[:, 0:1], 0.0); ms(1, ["dE1"], T.dE1[:, 0:1], 0.0)
+    iota(128, ["CKa"], T.CK[0:1, 0:128], [[0, 8], [-1, 16]], 15, 0, r=["CK"])
+    ms(64, ["CKb"], T.CK[0:1, 128:256], 4096.0, r=["CK"]); ms(64, ["CKc"], T.CK[32:33, 128:256], -255.0 / 512, r=["CK"])
+    CKr = ["CKa", "CKb", "CKc"]
+    iota(256, ["xi0"], T.xi[:, 0:256], [[1, 256]], 0, 0)
+    iota(16, ["xi1"], T.xi[:, 256:272], [[256, 16]], 0, 0)
+    iota(256, ["JT"], T.JT[:], [[1, 256]], 0, 0)
+    iota(16, ["JB0"], T.JB[:], [[128, 2], [0, 8]], -6815744, 1)
+    ts(16, ["JB0"], ["JB"], T.JB[:], T.JB[:], 4096.0, None, Al.mult)
+    iota(16, ["DUM0"], T.DUM[:], [[16, 16]], 4096, 0)
+    for tb in range(2):
+        for k in range(8):
+            iota(544, ["tab%d" % tb if k == 7 else "tf%d.%d" % (tb, k)], tab[tb][:, 544 * k:544 * k + 544], [[0, 544]], 0, 0, r=["tf%d.%d" % (tb, x) for x in range(7)] if k == 7 else [])
+    names = {}
+
+    def c(nm):
+        if nm not in names:
+            names[nm] = len(names)
+        return T.col[:, names[nm]:names[nm] + 1]
+
+    def cs(nm, src, s1, s2, o0, o1=None):
+        r = ["c" + x for x in (src, s1, s2) if isinstance(x, str)]
+        ts(1, r, ["c" + nm], c(nm), c(src), c(s1) if isinstance(s1, str) else s1, c(s2) if isinstance(s2, str) else s2, o0, o1)
+
+    def cl(nm, src, sc, bi):
+        act(1, ["c" + x for x in (src, bi) if isinstance(x, str)], ["c" + nm], c(nm), c(src), Af.Identity, bias=c(bi) if isinstance(bi, str) else bi, scale=sc)
+    cp(1, ["pi0"], ["cp"], c("p"), T.pi[:, 0:1])
+    for k, (nm, sh, mk) in enumerate((("f", 0, 15), ("p64", 0, 63), ("od", 4, 1))):
+        ts(1, ["pi0"], ["pi%d" % (k + 1)], T.pi[:, k + 1:k + 2], T.pi[:, 0:1], sh, mk, Al.arith_shift_right, Al.bitwise_and)
+        cp(1, ["pi%d" % (k + 1)], ["c" + nm], c(nm), T.pi[:, k + 1:k + 2])
+    ms(16, ["P2"], T.POW[:, 32:48], 2.0); ms(16, ["P3"], T.POW[:, 48:64], 0.5); ms(16, ["z16"], T.z16[:], 0.0)
+    ts(16, ["i8", "cf"], ["M16"], T.i8[:], T.i8[:], c("f"), None, Al.is_equal)
+    v(16, ["P2", "z16"], ["P0"], lambda q: q.tensor_tensor_scan(T.POW[:, 0:16], T.POW[:, 32:48], T.z16[:], 0.5, Al.mult, Al.add))
+    v(16, ["P3", "z16"], ["P1"], lambda q: q.tensor_tensor_scan(T.POW[:, 16:32], T.POW[:, 48:64], T.z16[:], 2.0, Al.mult, Al.add))
+    for k, nm in ((0, "pw"), (1, "pv")):
+        tt(16, ["P%d" % k, "M16"], ["P%d" % (k + 4)], T.POW[:, 64 + 16 * k:80 + 16 * k], T.POW[:, 16 * k:16 * k + 16], T.i8[:], Al.mult)
+        v(16, ["P%d" % (k + 4)], ["c" + nm], lambda q, k=k, nm=nm: q.tensor_reduce(c(nm), T.POW[:, 64 + 16 * k:80 + 16 * k], AxisListType.X, Al.add))
+    cs("l12", "f", 12, 2.0 ** -8, Al.is_lt, Al.mult)
+    cs("cw", "pw", "l12", None, Al.mult)
+    cs("cw6", "cw", 1.0 / 64, None, Al.mult); cl("ncw", "cw", -1.0, 0.0)
+    cs("g16", "p", "f", None, Al.subtract)
+    G8 = T.IG[:, 0:128:16]
+    ms(72, ["CTW"], T.CTW[:], 0.0)
+    ts(8, ["IG", "cg16", "ccw", "CTW"], ["CTa"], T.CTW[:, 7:71:8], G8, c("g16"), c("cw"), Al.is_equal, Al.mult)
+    ts(8, ["IG", "cg16", "ccw6", "CTW"], ["CTb"], T.CTW[:, 71:135:8], G8, c("g16"), c("cw6"), Al.is_equal, Al.mult)
+    cp(256, ["imgi"], ["offI"], T.offI[:], T.imgi[:]); cp(256, ["imgi"], ["imgf"], T.imgf[:], T.imgi[:])
+    for k, w in enumerate((16.0, "cw", "ncw", -16.0)):
+        ts(8, ["IG", "cg16", "ccw", "cncw"], ["RR%d" % k], T.RR[:, 8 * k:8 * k + 8], G8, c("g16"), c(w) if isinstance(w, str) else w, Al.is_equal, Al.mult)
+    RR = T.RR; RRr = ["RR0", "RR1", "RR2", "RR3"]
+    for nm, d in (("m1", 1), ("m7", 7), ("m12", 12)):
+        cl(nm, "p", 1.0, -float(d))
+    cs("s01", "f", 2, None, Al.is_lt); cs("dv", "f", 4, -2.0 / 4096, Al.is_ge, Al.mult); cs("j3", "f", 3, None, Al.is_equal)
+    cl("ev", "od", -1.0, 1.0)
+    cs("a0", "f", 12, 512.0, Al.is_ge, Al.mult); cl("a", "a0", 1.0, -256.0)
+    cs("c", "f", 12, 512.0, Al.is_equal, Al.mult)
+    cs("b0", "f", 6, 512.0, Al.not_equal, Al.mult); cs("b1", "f", 13, "b0", Al.is_lt, Al.mult); cs("b", "f", 0, "b1", Al.is_gt, Al.mult)
+    cs("v0", "f", 6, 63.0, Al.is_ge, Al.mult); cs("pv6", "v0", 1.0, "pv", Al.add, Al.mult)
+    cl("pvb", "pv", 16.0, 0.0)
+    cl("ahi", "a0", 8192.0, 0.0); cl("chi", "a0", -4096.0, 0.0); cl("nhi", "a0", -8192.0, 0.0)
+    cl("al0", "dv", -512.0 * 4096 * 4096, "nhi")
+    cs("c2", "f", 2, 256.0, Al.is_equal, Al.mult); cs("c3", "c2", "j3", 4096.0, Al.add, Al.mult); cl("clo", "al0", -0.5, "c3")
+    k0 = len(names); names["se"] = k0; names["so"] = k0 + 1
+    ms(1, ["se0"], T.col[0:64, k0:k0 + 1], -1.0); ms(1, ["se1"], T.col[64:128, k0:k0 + 1], -1.0 / 64)
+    ms(1, ["so0"], T.col[0:64, k0 + 1:k0 + 2], 4096 - 0.5 + 2.0 ** -9); ms(1, ["so1"], T.col[64:128, k0 + 1:k0 + 2], 64 - 0.5 + 2.0 ** -15)
+
+    def eq(nm, src, colnm, s):
+        ts(128, [src, "c" + colnm] + (["c" + s] if isinstance(s, str) else []), [nm], T[nm][:], T[src][:], c(colnm), c(s) if isinstance(s, str) else s, Al.is_equal, Al.mult)
+
+    def scaled(nm, s):
+        act(128, ["Ib"] + (["c" + s] if isinstance(s, str) else []), [nm], T[nm][:], T.Ib[:], Af.Identity, scale=c(s) if isinstance(s, str) else s)
+    ms(48, ["A8a"], T.A8[0:64, :, 6:16], 1000.0, r=["A8"]); ms(48, ["A8b"], T.A8[64:128, :, 0:6], 1000.0, r=["A8"]); ms(48, ["A8c"], T.A8[64:128, :, 12:16], 1000.0, r=["A8"])
+    for i in range(8):
+        ts(128, ["A8a", "A8b", "A8c", "cp64"], ["BC%d" % i], T.BC[:, 128 * i:128 * i + 128], T.A8[:], float(i), c("p64"), Al.add, Al.is_equal)
+    eq("Ib", "IM", "p", 1.0)
+    scaled("bd1", "a"); eq("bd2", "IM", "m1", "b"); eq("bd3", "IG", "m12", -256.0); eq("bd4", "IM", "m7", "c")
+    tt(128, ["bd1", "bd2"], ["bd1"], T.bd1[:], T.bd1[:], T.bd2[:], Al.add); tt(128, ["bd3", "bd4"], ["bd3"], T.bd3[:], T.bd3[:], T.bd4[:], Al.add)
+    tt(128, ["bd1", "bd3"], ["BD"], T.BD[:], T.bd1[:], T.bd3[:], Al.add)
+    eq("Dp0", "IG", "p", 1.0); eq("Dm1", "IG", "m1", -1.0)
+    tt(128, ["Dp0", "Dm1"], ["D0a"], T.D01[:], T.Dm1[:], T.Dp0[:], Al.add)
+    act(128, ["D0a"], ["D01"], T.D01[:], T.D01[:], Af.Identity, scale=-1.0)
+    for nm, sc in (("If", 1.0), ("nI", -1.0), ("S01", "s01"), ("DB", "dv"), ("J3", "j3")):
+        scaled(nm, sc)
+    ts(16, ["isl", "cp"], ["SL"], T.SL[:], T.isl[:], c("p"), None, Al.is_equal)
+    iota(128, ["ones"], T.ones[:], [[0, 128]], 1, 0)
+    iota(128, ["seg0"], T.seg[:], [[0, 128]], 1, 0); ms(8, ["seg"], T.seg[:, 0:128:16], 0.0, r=["seg0"])
+    iota(256, ["MK0"], T.MK[:], [[0, 16], [1, 16]], 0, 0); ts(256, ["MK0", "cf"], ["MK"], T.MK[:], T.MK[:], c("f"), None, Al.is_equal)
+    iota(16, ["ogi"], T.ogi[:], [[1, 16]], 0, 0, False); cp(16, ["ogi"], ["offG"], T.offG[:], T.ogi[:])
+    ts(8, ["IG", "cg16"], ["OH"], T.OH[:], G8, c("g16"), None, Al.is_equal); iota(16, ["DT"], T.DT[:], [[128, 2], [0, 8]], 4096, 1)
+    ms(128, ["Mz"], T.Mz[:], 0.0)
+    ts(16, ["DUM0", "cf"], ["DUM"], T.DUM[:], T.DUM[:], c("f"), None, Al.add)
+    ts(272, ["xi0", "xi1", "cpvb"], ["xj"], T.xj[:], T.xi[:], c("pvb"), -0.5 + 2.0 ** -12, Al.mult, Al.add)
+    ts(272, ["xj"], ["xk"], T.xk[:], T.xj[:], 1, None, Al.bitwise_and)
+    ts(256, ["xk", "cal0", "cclo"], ["Plo"], T.Plo[:], T.xk[:, 0:256], c("al0"), c("clo"), Al.mult, Al.add)
+    ts(16, ["xk", "cahi", "cchi"], ["Phi"], T.Phi[:], T.xk[:, 256:272], c("ahi"), c("chi"), Al.mult, Al.add)
+    for k in range(16):
+        if k < BV:
+            ts(128, ["Plo", "Phi"], ["bits%d" % k], T.bits[:, 256 * k:256 * k + 256], T.Plo[:], T.Phi[:, k:k + 1], None, Al.add)
+        else:
+            act(256, ["Plo", "Phi"], ["bits%d" % k], T.bits[:, 256 * k:256 * k + 256], T.Plo[:], Af.Identity, bias=T.Phi[:, k:k + 1])
+    bitsr = ["bits%d" % k for k in range(16)]
+
+    Pb = lambda k: T.pP[:, 512 * k:512 * k + 512]
+    for hh in range(2):
+        mm(["tw%d" % hh, "CTa", "CTb"], ["Z0"], [(T.pZ0[:], T.CTW[:, 7 - i:135 - i], T.tw[:, 512 * i:512 * i + 512], i == 0, 512) for i in range(4 * hh, 4 * hh + 4)])
+    ts(512, ["tc0", "tc1", "se0", "se1", "so0", "so1"], ["ta"], T.ta[:], T.tci[:], c("se"), c("so"), Al.mult, Al.add)
+    tt(512, ["ta"], ["ki"], T.ki[:], T.pZ0[:], T.ta[:], Al.add, b=["Z0"])
+    ts(512, ["ki"], ["kj"], T.kj[:], T.ki[:], 63, None, Al.bitwise_and)
+    cp(512, ["kj"], ["kb16"], T.kb16[:], T.kj[:])
+    Rb = [T.Rb0, T.Rb1]
+    for i in range(8):
+        e = i % 2; sl = slice(512 * i, 512 * i + 512)
+        mm(["kb16", "BC%d" % i], ["P%d" % e], [(Pb(e), T.BC[:, 128 * i:128 * i + 128], T.kb16[:], True, 512)])
+        act(512, ["cpv6"], ["Rb%d" % e], Rb[e][:], Pb(e), Af.Identity, bias=191.515625, scale=c("pv6"), b=["P%d" % e])
+        if i % 4 < HA:
+            mm(["Rb%d" % e, "BD", "Ib", "tw%d" % (i // 4)], ["P%d" % (2 + e)], [(Pb(2 + e), T.Ib[:], T.tw[:, sl], True, 512), (Pb(2 + e), T.BD[:], Rb[e][:], False, 512)])
+            act(512, [], ["H%d" % i], T.Hw[:, sl], Pb(2 + e), Af.Copy, b=["P%d" % (2 + e)])
+        else:
+            mm(["Rb%d" % e, "BD"], ["P%d" % (2 + e)], [(Pb(2 + e), T.BD[:], Rb[e][:], True, 512)])
+            tt(512, ["tw%d" % (i // 4)], ["H%d" % i], T.Hw[:, sl], Pb(2 + e), T.tw[:, sl], Al.add, b=["P%d" % (2 + e)])
+    Hr = ["H%d" % i for i in range(8)]
+    for k in range(1, 4):
+        dma("s", 1024, Hr, ["Hx%d" % k], T.Hw[:, 4096 * k:4096 * k + 4096], T.Hw[:, 0:4096])
+    Hxr = Hr + ["Hx1", "Hx2", "Hx3"]
+
+    cp(768, ["cI0", "cI1", "cI2"], ["cmp0", "cmp1", "cmp2"], T.cmp[:], T.cmpI[:])
+
+    def unpack(src, keys, tb):
+        for q in range(3):
+            dma("s", 128, keys + ["tab%d" % tb], ["tab%d.%d" % (tb, q)], tab[tb][q:128:16, 0:4096], src[:, 256 * q:256 * q + 256])
+    tabk = lambda tb: ["tab%d" % tb] + ["tab%d.%d" % (tb, q) for q in range(3)]
+    unpack(T.cmp, ["cmp0", "cmp1", "cmp2"], 0)
+    ts(256, ["ow0", "ow1", "ow2"], ["A0.0", "A0.1"], T.A0[:], T.owni[:], 2048, None, Al.subtract)
+    tn = lambda k: T.tn[:, 16 * k:16 * k + 16]
+    m = tn(0)
+    mm(["A0.0", "A0.1", "SL"], ["Z1"], [(T.pZ1[:, 8 * h:8 * h + 8], T.A0[:, 128 * h:128 * h + 128], T.SL[:, 8:16], True, 64) for h in range(2)])
+    ts(16, [], ["m"], m, T.pZ1[:, 0:16], 2048.0, None, Al.add, b=["Z1"])
+
+    def gather(h, win, wr, off, offr, new, prev):
+        for s in range(NP):
+            o = off[:, 128 * h + PL * s:128 * h + PL * s + PL]; sl = slice(PW * s, PW * s + PW)
+            if h == 1:
+                act(PW * GC, wr + offr, ["G%d.%d" % (new, s)], G[new][:, sl], win.indirect(o), Af.Copy)
+            elif prev is not None:
+                tt(PW * GC, wr + offr + ["X%d.%d" % (prev, s)], ["X%d.%d" % (new, s)], X[new][:, sl], win.indirect(o), X[prev][:, sl], Al.add)
+            elif s < X0A:
+                act(PW * GC, wr + offr, ["X%d.%d" % (new, s)], X[new][:, sl], win.indirect(o), Af.Copy)
+            else:
+                cp(PW * GC, wr + offr, ["X%d.%d" % (new, s)], X[new][:, sl], win.indirect(o))
+
+    def addP(k):
+        for bk in range(4):
+            if k is None:
+                mm(["CKP", "Ib", "ones"], ["P%d" % bk], [(Pb(bk), T.ones[:], T.CKP[:], True, 512)])
+            else:
+                mm(["G%d.%d" % (k, bk * NP // 4), "Ib", "ones"], ["P%d" % bk], [(Pb(bk), T.Ib[:], G[k][:, 512 * bk:512 * bk + 512], False, 512)])
+
+    def tr(h, src, keys, lo, hi, rhs):
+        mm(keys + RRr, ["T%d" % h], [(pT[h][:, lo + i:hi:16], src[:, i:2048:16], rhs, False, 64) for i in range(16)])
+
+    def const(h, lo, hi):
+        mm(CKr + ["ones"], ["T%d" % h], [(pT[h][:, lo:hi], T.ones[:], T.CK[:, lo:hi], True, hi - lo)])
+
+    def escopy(h, diff):
+        if ESA >> h & 1:
+            act(128, [], ["ES%d" % h], ES[h][:], pT[h][:, 128:256], Af.Copy, b=["T%d" % h])
+        else:
+            cp(128, [], ["ES%d" % h], ES[h][:], pT[h][:, 128:256], b=["T%d" % h])
+        if diff:
+            tt(128, ["ES%d" % h], ["dE%d" % h], T["dE%d" % h][:, 1:128], ES[h][:, 0:127], pT[h][:, 129:256], Al.subtract, b=["T%d" % h])
+
+    def nterms(h, terms, turn):
+        o = pT[h][:, 256:384]
+        mm((["ES%d" % h, "If"] if turn else []) + [x for t in terms for x in (t[0], "A%d.%d" % (t[1], h))], ["T%d" % h],
+           ([(o, ES[h][:], T.If[:], True, 512)] if turn else []) + [(o, T[t[0]][:], A[t[1]][:, 128 * h:128 * h + 128], False, 128) for t in terms])
+
+    def nstage(h, add, out, key, plain):
+        o = pT[h][:, 256:384]; sl = slice(128 * h, 128 * h + 128)
+        if plain:
+            ts(128, [], [key], out[:, sl], o, MG, MG - add, Al.add, Al.subtract, b=["T%d" % h])
+        else:
+            ts(128, [], ["ui%d" % h], T.ui[:, sl], o, MG, MG - add, Al.add, Al.subtract, b=["T%d" % h])
+            ts(128, ["ui%d" % h], ["uj%d" % h], T.uj[:, sl], T.ui[:, sl], 4095, None, Al.bitwise_and)
+            cp(128, ["uj%d" % h], [key], out[:, sl], T.uj[:, sl])
+
+    def reduce256(src, sk, out, ok, ra):
+        for bk in range(4):
+            z = bk % 2; sl = slice(512 * bk, 512 * bk + 512)
+            mm([sk % (bk * NP // 4), "y0.%d" % (bk // 2), "Ib", "nI"], ["Z%d" % z], [(pZ[z][:], T.Ib[:], src[:, sl], True, 512), (pZ[z][:], T.nI[:], T.y0[:, sl], False, 512)])
+            if bk < ra:
+                act(512, [], ok(bk), out[:, sl], pZ[z][:], Af.Identity, bias=-49152.0, b=["Z%d" % z])
+            else:
+                ts(512, [], ok(bk), out[:, sl], pZ[z][:], -49152.0, None, Al.add, b=["Z%d" % z])
+
+    for h in range(2):
+        gather(h, T.tw[:], ["tw0", "tw1"], T.offI, ["offI"], 2 if h else 3, None)
+        const(h, 0, 256)
+        mm(["imgf", "If"], ["T%d" % h], [(pT[h][:, 128:256], T.imgf[:, 128 * h:128 * h + 128], T.If[:], False, 512)])
+        tr(h, G[2] if h else X[3], allp("G2" if h else "X3"), 0, 128, RR[:, 0:8])
+        escopy(h, True)
+    at = [3]
+    for n in range(1, 7):
+        cur, old = n % 2, 1 - n % 2
+        tb = ((n - 1) // 2) % 2
+        win, wr = (T.Hw[:, 0:4096], Hr) if n == 1 else (T.Hw[:], Hxr)
+        for h in range(2):
+            bk = ["T%d" % h]; Rm = T["Rm%d" % h]; nn = T["nn%d" % h]; Wm = T["Wm%d" % h]; s8 = slice(8 * h, 8 * h + 8)
+            v(128, ["seg"], ["Rm%d" % h], lambda q, Rm=Rm, h=h: q.tensor_tensor_scan(Rm[:], T.seg[:], pT[h][:, 0:128], 0.0, Al.mult, Al.max), bk)
+            tt(128, ["Rm%d" % h], ["nn%d" % h], nn[:], pT[h][:, 0:128], Rm[:], Al.is_lt, b=bk)
+            v(128, ["nn%d" % h, "dE%d" % h], ["Wm%d" % h], lambda q, Wm=Wm, nn=nn, h=h: q.tensor_tensor_scan(Wm[:], T["dE%d" % h][:], nn[:], 0.0, Al.add, Al.mult))
+            e15 = ES[h][:, 15:128:16]
+            if n > 1:
+                tt(8, ["ES%d" % h, "AT%d" % old], ["e15%d" % h], T.e15[:, s8], e15, AT[old][:, s8], Al.subtract)
+            tt(8, ["Wm%d" % h, "ES%d" % h, "e15%d" % h], ["wi%d" % h], T.wi[:, s8], Wm[:, 15:128:16], T.e15[:, s8] if n > 1 else e15, Al.add)
+            ts(8, ["wi%d" % h], ["wj%d" % h], T.wj[:, s8], T.wi[:, s8], 4095, None, Al.bitwise_and)
+            tt(200, ["wj%d" % h, "offG", "MK"], ["Wz%d" % h], T.Wz[:, 128 * h:128 * h + 128], T.wj[:, s8].indirect(T.offG[:, 0:8]), T.MK[:, 0:128], Al.mult)
+            mm(["Wz%d" % h, "OH"], bk, [(pT[h][:, 384:392], T.Wz[:, 128 * h:128 * h + 128], T.OH[:], True, 256)])
+            cp(8, [], ["oO%d.%d" % (cur, h)], offO[cur][:, s8], pT[h][:, 384:392], b=bk)
+            nterms(h, [("Dm1", old)] if n > 1 else [], True)
+            ts(200, tabk(tb) + ["oO%d.%d" % (cur, h)], ["A%d.%d" % (cur, h)], A[cur][:, 128 * h:128 * h + 128], tab[tb][:].indirect(offO[cur][:, s8]), 2048.0, None, Al.subtract)
+            nterms(h, [("Dp0", cur)], False)
+            nstage(h, 2048 if n == 1 else 4096, T.offU0, "oU0.%d" % h, n > 1)
+        oO = ["oO%d.0" % cur, "oO%d.1" % cur]; Ac = ["A%d.0" % cur, "A%d.1" % cur]; Ao = ["A%d.0" % old, "A%d.1" % old]
+        ts(16, ["m"], ["Mz"], T.Mz[:, 2:256:16], m, 4095.0, 2048.0, Al.min, Al.subtract)
+        ts(16, ["m"], ["t1"], tn(1), m, 4095.0, 256.0 * 4096, Al.min, Al.mult)
+        tt(16, ["t1", "JB"], ["kb"], tn(2), tn(1), T.JB[:], Al.add)
+        for par in range(2):
+            act(400, bitsr + oO + ["cev", "cod"], ["XL%d" % par], XL[par][:], T.bits[:].indirect(offO[cur][:]), Af.Identity, scale=c("od" if par else "ev"))
+        mm(Ac + ["SL"], ["Z0"], [(T.pZ0[:, 16 * f + 8 * h:16 * f + 8 * h + 8], A[cur][:, 128 * h:128 * h + 128], T.SL[:, 8 * f:8 * f + 8], True, 64) for h in range(2) for f in range(2)])
+        act(32, [], ["AT%d" % cur], AT[cur][:], T.pZ0[:, 0:32], Af.Identity, bias=2048.0, b=["Z0"])
+        tt(16, ["m", "AT%d" % cur], ["dl"], tn(4), AT[cur][:, 16:32], m, Al.subtract)
+        tt(16, ["wj0", "wj1", "DT"], ["wd"], tn(7), T.wj[:], T.DT[:], Al.subtract)
+        pv = T.pZ1[:, 0:256]
+        mm(Ao + ["S01", "Mz", "Ib", "J3", "JT"], ["Z1"], [(pv, T.S01[:], A[old][:], True, 256), (pv, T.J3[:], T.JT[:], False, 256)] +
+           [(T.pZ1[:, 128 * h:128 * h + 128], T.Mz[:, 128 * h:128 * h + 128], T.Ib[:], False, 128) for h in range(2)])
+        mm(["XL0", "XL1", "DB"], ["Z1"], [(pv, T.DB[:], XL[par][:], False, 256) for par in range(2)])
+        cp(256, [], ["XR"], T.XR[:], pv, b=["Z1"])
+        act(256, [], ["V%d" % cur], V[cur][:], pv, Af.Identity, bias=2048.0, b=["Z1"])
+        if cur == 0:
+            send(3 * (n // 2 - 1) + 1, 128, ["V0"], ["lv%d" % (n // 2 - 1)], T["lv%d" % (n // 2 - 1)][:], V[0][:])
+        for k in range(8):
+            kp = (k * ZO) % 8; z = k % 2
+            two = [(2 * kp + x, pZ[z][:, 256 * x:256 * x + 256]) for x in range(2)]
+            mm(["XL0", "XL1", "XR"], ["Z%d" % z], [(o, XL[kz % 2][32 * (kz % 8 // 2):32 * (kz % 8 // 2) + 32, 128 * (kz // 8):128 * (kz // 8) + 128], T.XR[32 * (kz % 8 // 2):32 * (kz % 8 // 2) + 32, :], True, 256) for kz, o in two])
+            for kz, o in two:
+                if kz < 16 - NZD:
+                    act(280, ["kb"], ["cn%d" % kz, "jk%d" % kz], T.junk[:, 256 * kz:256 * kz + 256], o, Af.Relu, bias=T.tn[:, 32 + kz:33 + kz], scale=-1.0, b=["Z%d" % z], acc=T.cnt[:, kz:kz + 1])
+                else:
+                    v(256, [], ["mn%d" % kz], lambda q, o=o, kz=kz: q.tensor_reduce(T.tn[:, 128 + kz:129 + kz], o, AxisListType.X, Al.min), ["Z%d" % z])
+        if NZD:
+            tt(16, ["kb"] + ["mn%d" % k for k in range(16 - NZD, 16)], ["cn%d" % k for k in range(16 - NZD, 16)], T.cnt[:, 16 - NZD:16], T.tn[:, 48 - NZD:48], T.tn[:, 144 - NZD:144], Al.subtract)
+        tt(16, ["dl"] + ["cn%d" % k for k in range(16)], ["z"], tn(9), tn(4), T.cnt[:], Al.subtract)
+        ts(16, ["z"], ["wn"], tn(6), tn(9), 0.0, None, Al.is_gt)
+        tt(16, ["wn", "wd"], ["t11"], tn(11), tn(6), tn(7), Al.mult)
+        tt(400, ["t11", "offG", "MK"], ["Wn"], T.Wn[:], tn(11).indirect(T.offG[:]), T.MK[:], Al.mult)
+        if n < 6:
+            ts(16, ["z"], ["t10"], tn(10), tn(9), 0.0, 2.0, Al.max, Al.add)
+            tt(16, ["t10", "m"], ["m"], m, tn(10), m, Al.add)
+        mm(["Wn", "OH", "If", "DUM"], ["Z0"], [(T.pZ0[:, 0:16], T.If[:], T.DUM[:], True, 256)] + [(T.pZ0[:, 8 * h:8 * h + 8], T.Wn[:, 128 * h:128 * h + 128], T.OH[:], False, 256) for h in range(2)])
+        cp(16, [], ["oS%d" % cur], offS[cur][:], T.pZ0[:, 0:16], b=["Z0"])
+        if cur == 1:
+            ho = n // 2
+            cp(1000, ["oS1", "V1"], tabk(tb), tab[tb][:].indirect(offS[1][:]), V[1][:])
+            for q in range(3):
+                dma("s", 128, tabk(tb), ["cmp%d" % q], T.cmp[:, 256 * q:256 * q + 256], tab[tb][q:128:16, 0:4096])
+            send(3 * ho, 384, ["cmp0", "cmp1", "cmp2"], ["land%d" % ho], T["land%d" % ho][:], T.cmp[:])
+            unpack(T["land%d" % ho], ["land%d" % ho], 1 - tb)
+        else:
+            ho = n // 2 - 1
+            send(3 * ho + 2, 4, ["oS0"], ["lo%d" % ho], T["lo%d" % ho][:], offS[0][:])
+            cp(1000, ["lo%d" % ho, "lv%d" % ho], tabk(1 - tb), tab[1 - tb][:].indirect(T["lo%d" % ho][:]), T["lv%d" % ho][:])
+        addP(None)
+        addP(2)
+        for q in range(2):
+            for h in range(2):
+                keys = q == 1 and n < 6
+                if h == 0:
+                    kp = at[0]; k = (kp + 1) % 3 if kp < 3 or n == 1 else 0; at[0] = k
+                    new, nk = X[k], allp("X%d" % k)
+                    const(h, 0 if keys else 128, 256)
+                    tr(h, X[kp], allp("X%d" % kp), 128, 256, RR[:, 16:24])
+                else:
+                    kp, k = None, q
+                    new, nk = G[k], allp("G%d" % k)
+                    const(h, 128, 256)
+                gather(h, win, wr, offU[q], ["oU%d.%d" % (q, h)], k, kp)
+                if keys and h == 0:
+                    tr(h, new, nk, 0, 256, RR[:, 0:16])
+                else:
+                    tr(h, new, nk, 128, 256, RR[:, 8:16])
+                    escopy(h, keys)
+                if h == 1:
+                    addP(k)
+                if q == 0:
+                    nterms(h, [("D01", cur)], True)
+                    nstage(h, 4096, T.offU1, "oU1.%d" % h, n > 1)
+                    continue
+                for s in range(4 if h else 2):
+                    if h == 0:
+                        sl = slice(1024 * s, 1024 * s + 1024)
+                        ts(512, nk[s * NP // 2:(s + 1) * NP // 2], ["y0.%d" % s], T.y0[:, sl], new[:, sl], -49279.5, None, Al.add)
+                        continue
+                    sl = slice(512 * s, 512 * s + 512)
+                    if s < YV:
+                        ts(512, [], ["y1.%d" % s], T.y1[:, sl], Pb(s), -127.5, None, Al.add, b=["P%d" % s])
+                    else:
+                        act(512, [], ["y1.%d" % s], T.y1[:, sl], Pb(s), Af.Identity, bias=-127.5, b=["P%d" % s])
+                    tt(512, ["y1.%d" % s], ["G2.%d" % (s * NP // 4)], T.G2[:, sl], Pb(s), T.y1[:, sl], Al.subtract, b=["P%d" % s])
+                if keys and h == 0:
+                    tr(h, T.y0, ["y0.0", "y0.1"], 0, 128, RR[:, 24:32])
+                    escopy(h, True)
+                elif keys:
+                    const(h, 0, 128)
+                    tr(h, G[2], allp("G2"), 0, 128, RR[:, 0:8])
+                if n == 3 and h == 0:
+                    at[0] = 3
+                    reduce256(new, "X%d." % k + "%d", X[3], lambda bk: ["X3.%d" % (bk * NP // 4)], RA)
+                if n == 6:
+                    nterms(h, [("Dm1", cur)], True)
+                    nstage(h, 2048, T.yi, "yi%d" % h, False)
+                    if h == 0:
+                        reduce256(new, "X%d." % k + "%d", T.fo, lambda bk: ["fo%d" % bk], RF)
+    dma("s", 128, tabk(1), [], T.yent[:, 0:4096], T.tab1[0:128:16, 0:4096])
+    dma("s", 128, tabk(1), [], T.yent[:, 4096:8192], T.tab1[1:128:16, 0:4096])
+    dma("s", 128, tabk(1), [], T.yelen[:], T.tab1[2:128:16, 0:4096])
+    dma("s", 128, ["yi0", "yi1"], [], T.yimg[:], T.yi[:])
+    for k in range(8):
+        dma("s", 128, ["fo%d" % k if k < 4 else "G2.%d" % (k - 4)], [], T.yf[:, 512 * k:512 * k + 512], (T.fo if k < 4 else T.G2)[:, 512 * (k % 4):512 * (k % 4) + 512])
+    return ops, nout
+
+
+def schedule(ops):
+    lw, rd, lb = {}, {}, {}
+    for n, o in enumerate(ops):
+        dep = {}
+        for k in o["r"]:
+            if k in lw:
+                dep[lw[k]] = True
+        for k in o["w"]:
+            for x in ([lw[k]] if k in lw else []) + rd.get(k, []):
+                dep[x] = True
+        for k in o["b"]:
+            if k in lb:
+                dep.setdefault(lb[k], False)
+            lb[k] = n
+        dep.pop(n, None)
+        for k in o["r"]:
+            rd.setdefault(k, []).append(n)
+        for k in o["w"]:
+            lw[k] = n; rd[k] = []
+        o["dep"] = dep
+    succ = [[] for o in ops]
+    for n, o in enumerate(ops):
+        for d in o["dep"]:
+            succ[d].append(n)
+    pr = [0.0] * len(ops)
+    for n in range(len(ops) - 1, -1, -1):
+        pr[n] = ops[n]["t"] + ops[n]["lat"] + SY + max([pr[s] for s in succ[n]] + [0.0])
+    for n, o in enumerate(ops):
+        if "T1" in o["b"] or any(k[0] == "G" or k in ("wi1", "wj1", "Wz1", "A0.1", "A1.1", "uj1") or k[:2] == "y1" for k in o["w"]):
+            pr[n] += BIAS
+        if "Z0" in o["b"] or "Z1" in o["b"] or any(k[:2] in ("XL", "cn", "wn", "t1", "Wn", "z", "oS") for k in o["w"]):
+            pr[n] += WB
+        pr[n] += CB.get(o["e"] + (o["w"] + o["b"] + [""])[0][:3], 0.0)
+    left = [len(o["dep"]) for o in ops]; rdy = [0.0] * len(ops); free = {}
+    ready = [n for n in range(len(ops)) if left[n] == 0]; order = []; end = 0.0
+    while ready:
+        best = min(ready, key=lambda n: (max(rdy[n], free.get(ops[n]["e"], 0.0)), -pr[n], n))
+        e0 = ops[best]["e"]; t0 = max(rdy[best], free.get(e0, 0.0)); d0 = ops[best]["t"]; p0 = pr[best] + d0
+        for n in ready:
+            if ops[n]["e"] == e0 and rdy[n] < t0 + LOOK * d0 and pr[n] > p0:
+                best = n; p0 = pr[n]
+        ready.remove(best); o = ops[best]
+        st = max(rdy[best], free.get(e0, 0.0)); o["st"] = st
+        if e0 != "x":
+            free[e0] = st + o["t"]
+        fin = st + o["t"] + o["lat"]; end = max(end, fin); order.append(best)
+        for s in succ[best]:
+            rdy[s] = max(rdy[s], fin + (0.0 if e0 == ops[s]["e"] and (e0 == "p" or not ops[s]["dep"][best]) else SY))
+            left[s] -= 1
+            if left[s] == 0:
+                ready.append(s)
+    return order, end
+
+
+def rank_program(g, core, T, topo):
+    rank = T.rank_of(core)
+    if rank is None:
+        return
+    ops, nout = build(T, topo, core, rank)
+    order, end = schedule(ops)
+    Q = {"g": g, "v": g.vector, "a": g.scalar, "p": g.tensor, "s": g.sync}
+    cnt = {"v": 0, "a": 0, "p": 0, "g": 0}; seen = {e: {} for e in Q}; nd = [0]; total = {}
+    for n in order:
+        o = ops[n]; e = o["e"]
+        if o["k"] == "x":
+            total[o["sem"][0]] = o["sem"][1]
+            continue
+        need = {}
+        for d, data in o["dep"].items():
+            p = ops[d]
+            if p["k"] == "c" and p["e"] == e and o["k"] == "c" and (e == "p" or not data):
+                continue
+            s, val = p["sem"]
+            need[s] = max(need.get(s, 0), val)
+        for s, val in need.items():
+            if seen[e].get(s, 0) < val:
+                Q[e].wait_ge(T.sem[s], val); seen[e][s] = val
+        if o["k"] == "c":
+            cnt[e] += 1; o["sem"] = ("c" + e, cnt[e])
+            o["fn"](Q[e]).then_inc(T.sem["c" + e], 1)
+        else:
+            s = "d%d" % nd[0]; nd[0] += 1
+            if o["k"] == "d":
+                o["sem"] = (s, 16); o["fn"](Q[e]).then_inc(T.sem[s], 16)
+            else:
+                o["sem"] = (s, nout); o["fn"](Q[e], T.sem[s])
+        total[o["sem"][0]] = o["sem"][1]
+    for s, val in total.items():
+        g.wait_ge(T.sem[s], val)

@@ -1,16 +1,56 @@
 from concourse.mybir import AluOpType as Al, AxisListType, ActivationFunctionType as Af
 
 F, B, H16, I, U = "float32", "bfloat16", "float16", "int32", "uint16"
-NP = 4
+NPQ = (2, 4)
 NZD = 4
 ZO = 7
-X0A = 4
-ESA = 1
-HA, BV, YV, RA, RF = 1, 8, 0, 4, 4
-CV, CA, CP, CQ, SY, GC = 0.06, 0.08, 0.0005, 0.05, 0.1, 1.55
-LOOK, BIAS, WB = 0.0, 1.0, 0.0
-CB = {'acn6': -0.5, 'vcj3': 2, 'acn9': 2, 'ay1.': -1.0, 'pT0': 0.5, 'vWn': 1, 'vWm0': 2, 'vWz1': -1, 'vcf': -1, 'vm': -0.5, 'vcmp': -1, 'voU0': 0.5, 've15': 1, 'gsnd': 2, 'vWm1': 2, 'gA8': 2, 'vcpv': -1, 'vbit': -1.5, 'scI0': 0.5, 'vwi0': 0.5, 'acn8': -1.0, 'aRb1': 1, 'pP3': -1, 'vdE0': -1, 'vMz': 1, 'gtf0': -2, 'vES1': -1, 'vt1': -1, 'pP1': 1, 'vnn1': -1.5, 'vRm0': -2, 'vH3': 0.5, 'acn5': -0.5, 'voS1': -1, 'vdE1': 0.5, 'acn3': 0.5, 'pZ0': -1.5, 'pP2': -2, 'vH1': 1, 'acn0': -0.5, 'aX3.': 1, 'vtab': -2, 'vnn0': 2, 'vA8b': 1, 'vkb': 0.5}
+YV, NY0 = 1, 2
+RA, RF = 4, 4
+BA = 7
+NH, HA = 8, 2
+ESA = 3
+RH = 3
+UN, V6A, CMQ = 6, 1, "cn11"
+LL, E2A, FU, STRICT = 0, 3, (2, 3, 5), 2
+M1 = 2
+OPEN = True
+CV, CA, CY, CP, CQ, SY, GC = 0.05, 0.065, 0.00083, 0.00047, 0.04, 0.07, 1.55
+LOOK = 0.3
+BANKS = "Z0Z1Z0Z1Z0Z1T1T0"
+FIRST = ("tci imgi tw0 tw1 pi0 i16 G8 pi1 cf cp M16 SA0 SA P2 P3 P0 P4 ccw cg16 OH WD0 WD1 CK ones CKa CKb CKc tch offI DL Z0 ui0 uj0 offK "
+         "bits0 bits1 bits2 bits3 bits4 bits5 bits6 bits7 bits8 bits9 cncw RR0 RR1 RR2 RR3 RR4 Ib CKd tf0 tf1 tf2 tf3 If bits10 bits11 bitt11 bits12 bitt12").split()
+LATE = "mx cj4 cs01 cb2 S01 cb J3 cb1 cs1 cb0 cs0 DB JB mr WD2 kb0 kb1 DUM OHb Dm1 nI nIf Mz cp0 cp1 Mj0 Mj1".split()
+STEP = ("run3 chain window xl open00 run2 g010 xr open01 run1 g011 g000 d00 d10 g001 run0 at d11 off1 t0 d01 t4 t6 off0 t1 t2 t7 t5 g111 open10 end1 t3 sub g110 g100 g103 g112 add03 win "
+        "add10 es1 g102 g101 tr0 add12 add11 y0 add01 open11 add00 g113 add13 y10 y11 y13 key0 add02 es0 trg tr1 y12 key1 put len end0")
+EVEN = ("chain open01 xl g010 run2 g011 xr g000 open00 g001 d00 at d01 d10 run3 t4 t1 d11 t0 off1 sub off0 end1 t6 t7 window t5 t2 t3 run0 run1 add03 g100 open11 win g111 open10 add00 "
+        "g112 g110 add02 g113 g102 g101 trg g103 y0 add10 end0 add01 add13 y13 key0 tr1 add11 tr0 y10 add12 y11 len es0 put y12 key1 es1")
+LAST = ("chain len xl xr open00 g000 g001 g010 open01 g011 d10 d11 run3 run1 window d00 at d01 off1 off0 g101 run0 t5 t0 t6 t3 t7 t4 g112 t1 run2 key1 t2 g111 g102 win g110 open10 add03 "
+        "add00 sub g103 put add01 g100 add11 y11 tr0 trg g113 key0 add12 add13 y13 es0 add02 open11 add10 y12 tr1 es1 y10 end1 y0 end0")
+STEP = "out0 chain point go1 go0 open00 pv out2 window g010 xl g011 out3 out1 run1 open01 run2 xr g000 at d00 d10 g001 d11 run0 t1 t4 run3 d01 t0 off0 sub off1 t6 t5 g103 t7 add01 g111 t2 open10 t3 add03 g110 g100 g112 win add12 g102 add11 g101 open11 add10 tr0 add00 y00 list trr g113 add13 fus3 y13 y01 trg y11 y10 tr1 put fus0 key0 fus2 fus1 ring es0 add02 y12 len key1"
+EVEN = "chain mod3 mod0 point mod2 mod1 pv go1 out2 g010 go0 xl run2 xr g000 open00 d00 at open01 out3 g001 d10 d01 g011 window run3 d11 off1 t0 sub t4 t6 off0 t1 open11 out1 out0 t7 t3 t2 t5 trr g111 run0 add03 open10 g100 add02 g110 win list run1 g113 g112 g101 trg g102 g103 add13 add10 y00 y01 add12 y12 add01 tr1 put add00 y10 add11 y13 fus1 y11 fus3 len key0 tr0 es0 ring fus2 fus0 key1"
+LAST = "chain point go1 g010 pv run1 xl go0 open01 g000 run2 xr run0 open00 g001 at t1 d00 t0 run3 g011 d01 off0 d10 t7 t4 t3 d11 t5 t2 off1 t6 win g100 list g110 g101 add00 open10 y00 add02 sub ring g112 g111 add11 mod0 g103 open11 add01 g102 g113 add03 add10 add12 y12 y10 mod1 y11 tr0 add13 y01 y13 put tr1 es0 img0 es1 f1 f2 f0 mod2 f3 img1 mod3"
+STEP = "chain out3 run3 pv point out0 go1 window out2 out1 g010 run0 xl go0 run1 open00 xr g000 g001 g011 d00 open01 at d10 d01 off0 t4 run2 t0 d11 t5 t1 sub t2 t7 off1 t6 g103 g110 t3 add10 g111 g100 win open10 g112 open11 g102 add02 list add11 trg fus0 add12 add01 trr add03 g113 g101 add00 add13 fus3 put fus1 y01 y11 fus2 y00 tr1 tr0 y13 key0 es0 y10 ring y12 key1 len"
+EVEN = "mod3 window out2 chain mod0 point mod1 pv go1 go0 xl out0 mod2 run0 xr out3 open00 open01 g010 g011 run3 run2 t0 g000 d00 t3 g001 d10 d01 t4 d11 at off1 t6 out1 fus1 sub off0 open11 t2 t7 t1 t5 g103 win trr fus3 list g110 run1 g100 g112 add03 open10 add12 g101 g113 g111 add10 add13 add11 add01 fus0 fus2 trg g102 add00 y11 y00 y01 put tr1 ring tr0 key0 add02 y13 y12 y10 key1 es0 len"
+LAST = "pv chain point go1 run1 run0 xl at go0 g000 g010 xr g011 open01 open00 g001 d00 t3 t2 d01 off0 t0 t5 add01 run3 d10 d11 off1 run2 g100 t7 t1 open10 g101 t4 t6 sub g110 ring win g112 g111 list y00 g103 g113 add02 add13 add12 open11 add00 add11 tr1 add10 y12 g102 y10 y11 tr0 mod1 add03 y01 mod0 f0 y13 f2 f1 es1 f3 img1 es0 mod2 mod3 img0 put"
+STEP = "out2 chain out3 pv point out1 window go1 g010 g011 go0 xl out0 xr t5 g000 open00 d00 g001 at t0 run0 open01 t2 d01 off0 d10 run3 run1 d11 off1 g103 t7 t1 t3 g110 run2 t4 t6 fus2 g100 sub win fus1 g101 add03 open10 add10 open11 trr g111 list g102 add02 tr0 g112 g113 add12 add13 tr1 add11 add00 y13 put y01 add01 y00 y12 y11 key0 y10 es0 trg len key1 fus0 fus3 ring"
+EVEN = "fus3 chain fus1 mod0 out0 out2 point go1 mod3 mod1 out3 pv xl g010 xr run3 mod2 at open01 go0 g000 open00 g011 t4 g001 d00 d01 t0 t1 d10 off0 out1 d11 off1 window t6 t7 open11 run0 t2 trg t3 g103 g101 t5 run2 g113 win sub g112 g110 fus0 list open10 g111 add13 fus2 ring add10 add03 g100 add00 g102 run1 add11 y13 add01 y11 add02 trr y00 y01 len y10 tr0 key0 put add12 y12 tr1 es0 key1"
+LAST = "chain pv point xl run0 at xr go0 g000 go1 g001 g010 open01 d10 run1 open00 t4 d00 d01 off0 g011 t3 t0 t5 run2 add01 d11 t7 t1 off1 t2 run3 g110 ring g112 g100 t6 sub g111 add11 add02 win list open10 add00 g101 add12 g113 y00 add10 g102 add13 g103 y12 open11 y10 tr0 y11 tr1 mod1 mod0 add03 y13 f3 y01 es1 f0 es0 img1 img0 f2 mod2 f1 put mod3"
+STRICT, FU, AU, BA = 9, (), 0, 8
+NZ, YS, BK, PS = (4, 4, 4), (1, 1, 1), (BANKS, BANKS, BANKS), 2
+LB, CI, PV = "Z0", [], 0
+STEP = "chain pv out3 point window go1 xl out0 run3 go0 xr g000 at open01 open00 out2 g010 g011 run0 d00 g001 t5 out1 d10 d11 run1 t0 t2 d01 off0 run2 t4 sub g102 off1 t6 t7 t3 g103 g110 add03 t1 g111 win list fus2 add02 fus0 g113 put ring g112 add12 g101 g100 open11 add13 y01 add11 open10 add10 trr add00 add01 tr1 y11 tr0 y00 fus3 len y12 y13 trg key0 y10 es0 key1 fus1"
+EVEN = "window mod3 chain point out3 mod0 mod1 pv go1 xl open01 mod2 xr at go0 fus1 open00 g000 g001 d00 out2 g010 g011 sub d10 run2 t4 run3 d01 t0 off0 out0 d11 off1 t1 t6 fus2 t7 t5 t2 t3 open11 fus3 g113 run0 g112 fus0 out1 g111 g101 add03 open10 g102 win add12 list add00 run1 trr g103 add11 add02 g110 add01 g100 add10 len y12 trg add13 y00 tr1 y01 put y10 y11 y13 key0 ring tr0 es0 key1"
+LAST = "chain point go0 pv run1 xl go1 xr open01 g010 run0 g000 open00 at t5 d10 t4 t3 add01 g001 run2 t1 g011 d00 d01 off0 d11 off1 add02 t2 t6 t0 t7 run3 ring g100 g101 open11 win g112 y00 sub list g103 add12 add00 g110 y12 g113 g111 g102 add11 add10 open10 mod1 tr1 add13 y10 mod0 y01 f0 add03 y13 put es1 tr0 y11 f1 es0 img0 img1 mod2 f3 mod3 f2"
+STEP = "out0 pv chain point go1 xl window xr open01 go0 run0 at g010 open00 sub g000 d00 g011 d10 out1 g001 d01 d11 off0 run1 off1 t1 t2 g110 out2 t3 fus1 out3 t0 fus0 fus3 t4 add00 t5 g111 t6 g113 t7 run3 add01 g100 win fus2 g103 add03 run2 g102 open11 g101 add02 y00 add13 g112 y13 add10 list y01 add11 trr open10 tr0 trg y11 add12 tr1 key0 y10 put y12 key1 ring es0 len"
+EVEN = "ring mod1 chain mod2 point go0 mod3 mod0 go1 pv xl xr g000 out0 run1 g001 g010 open00 window g011 out3 run3 fus1 open01 at d10 d00 fus3 t5 run0 d11 fus0 d01 t4 t2 off0 t7 add03 t0 g100 t3 off1 g102 g110 add00 trg out1 t6 open11 open10 fus2 add02 trr t1 win g113 g101 add01 g111 g112 add10 sub g103 add13 run2 add12 list tr0 add11 y00 y12 tr1 y01 out2 key0 y13 y10 len put es0 y11 key1"
+LAST = "run0 chain point go1 go0 pv xl xr g001 open00 open01 d01 g000 d00 g010 off0 g011 t0 run1 t7 run2 t4 g103 at d10 t3 t1 d11 run3 t2 off1 g111 t6 add11 t5 g110 g101 win g100 add02 y00 ring sub add10 add03 g113 add00 list g112 add01 add12 y12 open11 add13 mod0 y11 f1 g102 y13 f2 open10 put y01 mod3 tr1 es1 mod2 tr0 es0 img0 img1 y10 mod1 f0 f3"
+STEP = "chain point pv xl go1 open01 window out0 xr go0 open00 at g000 sub g010 d00 out1 d10 g001 g011 d11 t5 out3 out2 d01 t1 run0 t3 off1 fus0 off0 t2 run2 fus1 t0 g111 run1 run3 t4 t6 fus3 g110 t7 g100 g112 add00 g113 win fus2 add03 open11 add13 g101 g102 y00 g103 add02 y01 add10 y13 trr add01 trg add11 add12 tr1 list open10 tr0 y10 y11 put len key0 y12 es0 ring key1"
+EVEN = "chain mod0 run3 run1 point go0 mod1 mod3 mod2 g000 go1 pv xl xr ring open00 out3 g010 window at g011 out0 d00 g001 fus3 open01 d10 t4 t5 run0 d11 d01 off0 t3 off1 t7 fus1 t2 add03 out1 t1 t0 g112 g111 t6 fus0 g102 g100 g110 fus2 add01 open11 g113 trr open10 win add13 add02 add00 g103 g101 add12 sub add10 list tr0 add11 trg y00 y01 y12 put run2 y11 key0 tr1 y13 y10 es0 out2 key1 len"
+LAST = "chain pv point go0 xl xr open00 g001 t4 go1 g000 open01 g010 run0 d01 d10 at t5 d00 run1 t0 t3 run3 t1 off0 g011 d11 t7 t2 run2 add03 off1 g103 g111 add11 g100 g110 t6 g101 add00 g113 add10 ring y00 add02 win sub list add13 g112 add12 add01 open11 y11 y12 f1 open10 g102 mod0 y13 tr1 es1 y01 mod3 tr0 y10 mod2 f2 f3 img1 put es0 img0 mod1 f0"
+FU, RH, YS = (2, 3, 4), 4, (0, 0, 1)
+STEP = STEP.replace(" window", "").replace(" xl", " window xl")
 MG = 12582912.0
+YO = 49152.0
 
 
 def _sb(n, d):
@@ -18,51 +58,45 @@ def _sb(n, d):
 
 
 SCRATCH = {
-    "tw": _sb(4096, B), "Hw": _sb(16384, B), "bits": _sb(4096, B), "tab0": _sb(4352, F), "tab1": _sb(4352, F), "Xi": _sb(2048, B),
+    "tw": _sb(4096, B), "Hw": _sb(16384, B), "bits": _sb(4096, B), "tab0": _sb(4480, F), "tab1": _sb(4480, F), "Xi": _sb(2048, B),
     "X0": _sb(2048, H16), "X1": _sb(2048, H16), "X2": _sb(2048, H16), "G0": _sb(2048, B), "G1": _sb(2048, B), "G2": _sb(2048, B),
-    "y0": _sb(2048, B), "y1": _sb(2048, B), "fo": _sb(2048, B), "Rb0": _sb(512, B), "Rb1": _sb(512, B),
-    "imgi": _sb(256, I), "imgf": _sb(256, F), "offI": _sb(256, U), "tci": _sb(512, I), "ta": _sb(512, F), "ki": _sb(512, I), "kj": _sb(512, I), "kb16": _sb(512, B),
-    "cmpI": _sb(768, I), "cmp": _sb(768, F), "land0": _sb(768, F), "land1": _sb(768, F), "land2": _sb(768, F),
-    "lv0": _sb(256, F), "lv1": _sb(256, F), "lv2": _sb(256, F), "lo0": _sb(16, U), "lo1": _sb(16, U), "lo2": _sb(16, U),
-    "owni": _sb(256, I), "A0": _sb(256, H16), "A1": _sb(256, H16), "V0": _sb(256, F), "V1": _sb(256, F), "XR": _sb(256, H16), "XL0": _sb(256, B), "XL1": _sb(256, B),
-    "IM": _sb(128, F), "IG": _sb(128, F), "A8": ("sbuf", [128, 8, 16], F), "xi": _sb(272, F), "xj": _sb(272, I), "xk": _sb(272, I), "Plo": _sb(256, B), "Phi": _sb(16, F),
-    "pi": _sb(8, I), "col": _sb(48, F), "POW": _sb(96, F), "i8": _sb(16, F), "isl": _sb(16, F), "SL": _sb(16, B), "z16": _sb(16, F),
-    "Ib": _sb(128, B), "If": _sb(128, F), "nI": _sb(128, B), "ones": _sb(128, B),
-    "Dp0": _sb(128, B), "Dm1": _sb(128, B), "D01": _sb(128, B), "S01": _sb(128, B), "DB": _sb(128, B), "J3": _sb(128, B),
-    "BD": _sb(128, B), "bd1": _sb(128, B), "bd2": _sb(128, B), "bd3": _sb(128, B), "bd4": _sb(128, B), "BC": _sb(1024, B), "CTW": _sb(144, B),
-    "RR": _sb(32, B), "CK": _sb(256, B), "CKP": _sb(512, B), "seg": _sb(128, F), "JT": _sb(256, B), "JB": _sb(16, F), "DUM": _sb(16, F),
-    "ES0": _sb(128, F), "ES1": _sb(128, F), "Rm0": _sb(128, F), "Rm1": _sb(128, F), "nn0": _sb(128, B), "nn1": _sb(128, B),
-    "dE0": _sb(128, F), "dE1": _sb(128, F), "e15": _sb(16, F), "Wm0": _sb(128, F), "Wm1": _sb(128, F),
-    "wi": _sb(16, I), "wj": _sb(16, I), "Wz": _sb(256, F), "Wn": _sb(256, F), "MK": _sb(256, F), "ogi": _sb(16, I), "offG": _sb(16, U), "OH": _sb(8, F), "DT": _sb(16, F), "Mz": _sb(256, H16),
-    "offO0": _sb(16, U), "offO1": _sb(16, U), "offU0": _sb(256, U), "offU1": _sb(256, U), "offS0": _sb(16, U), "offS1": _sb(16, U),
-    "ui": _sb(256, I), "uj": _sb(256, I), "yi": _sb(256, F), "AT0": _sb(32, F), "AT1": _sb(32, F), "tn": _sb(192, F), "cnt": _sb(16, F), "junk": _sb(4096, B),
-    "pP": ("psum", [128, 2048], F), "pT0": ("psum", [128, 512], F), "pT1": ("psum", [128, 512], F), "pZ0": ("psum", [128, 512], F), "pZ1": ("psum", [128, 512], F),
+    "y0": _sb(2048, B), "y1": _sb(2048, B), "fo": _sb(2048, B), "XA": _sb(2048, H16), "G3": _sb(2048, B), "G4": _sb(2048, B), "CKP": _sb(512, B),
+    "imgi": _sb(256, I), "imgf": _sb(256, F), "offI": _sb(256, U), "tci": _sb(1024, I), "tch": _sb(1024, H16), "offK": _sb(256, U),
+    "cmpI": _sb(768, I), "cmp": _sb(768, F), "cmq": _sb(768, F), "land0": _sb(768, F), "land1": _sb(768, F), "land2": _sb(768, F),
+    "lv1": _sb(256, H16), "lv2": _sb(256, H16), "lv3": _sb(256, H16), "lv4": _sb(256, H16), "lv5": _sb(256, F), "lv6": _sb(256, F), "V5": _sb(256, F),
+    "lo1": _sb(16, U), "lo2": _sb(16, U), "lo3": _sb(16, U), "lo4": _sb(16, U), "lo5": _sb(16, U), "lo6": _sb(16, U),
+    "owni": _sb(256, I), "A0": _sb(256, H16), "A1": _sb(256, H16), "V6": _sb(256, F), "XR0": _sb(256, H16), "XR1": _sb(256, H16), "XL0": _sb(256, B), "XL1": _sb(256, B),
+    "G8": _sb(8, F), "pi": _sb(8, I), "col": _sb(48, F), "POW": _sb(64, F), "i16": _sb(16, F), "M16": _sb(16, F), "SL": _sb(8, B), "NE": _sb(8, B), "WW": _sb(8, B), "DL": _sb(16, B),
+    "Ib": _sb(128, B), "If": _sb(128, F), "nI": _sb(128, B), "nIf": _sb(128, F), "E2": _sb(512, F), "ones": _sb(128, B),
+    "Dp0": _sb(128, B), "Dp1": _sb(128, B), "Dm1": _sb(128, B), "D01": _sb(128, B), "S01": _sb(128, B), "DB": _sb(128, B), "J3": _sb(128, B),
+    "WD": _sb(288, B), "SA": _sb(576, B), "RR": _sb(40, B), "CK": _sb(768, B), "seg": _sb(256, F), "JT": _sb(256, B), "JB": _sb(2, F), "DUM": _sb(16, F),
+    "ES": _sb(512, F), "Rm": _sb(256, I), "oi": _sb(16, I), "oj": _sb(16, I), "offW": _sb(16, U),
+    "wi": _sb(16, I), "wj": _sb(16, I), "Wz": _sb(256, F), "Wn": _sb(256, B), "MK": _sb(256, F), "ogi": _sb(16, I), "offG": _sb(16, U), "OH": _sb(8, F), "Mz": _sb(256, H16),
+    "offO": _sb(16, U), "offU0": _sb(256, U), "offU1": _sb(256, U), "offS0": _sb(16, U), "offS1": _sb(16, U),
+    "ui": _sb(256, I), "uj": _sb(256, I), "yi": _sb(256, F), "AT": _sb(16, F), "OHb": _sb(8, B), "tn": _sb(160, F), "cnt": _sb(16, F), "junk": _sb(4096, B),
+    "pP": ("psum", [128, 2048], F), "pT": ("psum", [128, 1024], F), "pZ0": ("psum", [128, 512], F), "pZ1": ("psum", [128, 512], F),
 }
-SEMAPHORES = ["cv", "ca", "cp", "cg"] + ["d%d" % k for k in range(90)] + ["r%d" % k for k in range(9)]
+SEMAPHORES = ["cv", "ca", "cp", "cg"] + ["d%d" % k for k in range(90)] + ["r%d" % k for k in range(18)]
 
 
 def build(T, topo, core, rank):
-    ops = []; tail = {}
+    ops = []; tail = {}; tag = [""]
     n4 = len(T.cores)
     nxt, prv = T.cores[(rank + 1) % n4], T.cores[(rank - 1) % n4]
     rid, pid = topo.addr(nxt)[0], topo.addr(nxt)[1]
     nout, nin = len(topo.engines(core, nxt)), len(topo.engines(prv, core))
 
     def op(e, t, r, w, fn, b=(), kind="c", lat=0.0, sem=None):
-        ops.append({"e": e, "t": t, "r": list(r), "w": list(w), "b": list(b), "fn": fn, "k": kind, "lat": lat, "sem": sem})
+        ops.append({"e": e, "t": t, "r": list(r), "w": list(w), "b": list(b), "fn": fn, "k": kind, "lat": lat, "sem": sem, "tag": tag[0]})
 
     def v(n, r, w, fn, b=()):
-        op("v", CV + max(n, 40) * 0.001, r, w, fn, b)
+        op("v", CV + max(n, 64) * CY, r, w, fn, b)
 
     def gp(n, r, w, fn):
-        op("g", 0.15 + n * 0.002, r, w, fn)
+        op("g", 0.15 + 2 * n * CY, r, w, fn)
 
     def mm(r, b, lst):
         lst = [list(x) + [True] for x in lst]
-        for x in lst:
-            if not x[3]:
-                tail[b[0]][5] = False
-            tail[b[0]] = x
 
         def fn(q):
             last = None
@@ -70,6 +104,10 @@ def build(T, topo, core, rank):
                 last = q.matmul(o, l, x, s0, s1)
             return last
         op("p", CQ + sum(m[4] for m in lst) * CP, r, [], fn, b)
+        ops[-1]["mm"] = lst
+
+    def arrange(start, order):
+        ops[start:] = sorted(ops[start:], key=lambda o: order.index(o["tag"]))
 
     def dma(e, kb, r, w, out, src):
         op(e, 0.1, r, w, lambda q: q.dma_start(out, src), kind="d", lat=2.0 + kb / 200.0)
@@ -94,7 +132,16 @@ def build(T, topo, core, rank):
         v(n, r, w, lambda q: q.memset(out, c))
 
     def act(n, r, w, out, x, f, bias=0.0, scale=1.0, b=(), acc=None):
-        op("a", CA + max(n, 40) * 0.001, r, w, lambda q: q.activation(out, x, f, bias=bias, scale=scale, accum_out=acc), b)
+        op("a", CA + max(n, 64) * CY, r, w, lambda q: q.activation(out, x, f, bias=bias, scale=scale, accum_out=acc), b)
+
+    def shift(scalar, n, r, w, out, x, add, b=()):
+        plain = isinstance(add, float) and add == 0.0
+        if scalar:
+            act(n, r, w, out, x, Af.Copy if plain else Af.Identity, bias=add, b=b)
+        elif not plain:
+            ts(n, r, w, out, x, add, None, Al.add, b=b)
+        else:
+            cp(n, r, w, out, x, b=b)
 
     def iota(n, w, out, pat, base, cm, flt=True, r=()):
         if flt:
@@ -102,44 +149,45 @@ def build(T, topo, core, rank):
         else:
             gp(n, r, w, lambda q: q.iota(out, pat, base, cm))
 
-    tab = [T.tab0, T.tab1]; X = [T.X0, T.X1, T.X2, T.Xi]; G = [T.G0, T.G1, T.G2]; A = [T.A0, T.A1]; V = [T.V0, T.V1]
-    pT = [T.pT0, T.pT1]; pZ = [T.pZ0, T.pZ1]; ES = [T.ES0, T.ES1]; offO = [T.offO0, T.offO1]; offU = [T.offU0, T.offU1]; offS = [T.offS0, T.offS1]
-    AT = [T.AT0, T.AT1]; XL = [T.XL0, T.XL1]
-    PW = 2048 // NP; PL = 128 // NP
-    allp = lambda s: ["%s.%d" % (s, k) for k in range(NP)]
+    def sel(n, r, w, out, x, pat, cmp, fill, base, cm):
+        gp(n, r, w, lambda q: q.affine_select(out, x, pat, cmp, fill, base, cm))
+
+    tab = [T.tab0, T.tab1]; X = [T.X0, T.X1, T.X2, T.Xi]; G = [T.G0, T.G1, T.G2, T.G3, T.G4]; A = [T.A0, T.A1]; XR = [T.XR0, T.XR1]; XL = [T.XL0, T.XL1]
+    pT = T.pT; pZ = [T.pZ0, T.pZ1]; ES = T.ES; offU = [T.offU0, T.offU1]; offS = [T.offS0, T.offS1]; RR = T.RR
+    U0, E0, K0, L0 = (0, 768), (128, 640), (384, 512), 896
+    EC = (256, 128)
+    allp = lambda s: ["%s.%d" % (s, k) for k in range(4)]
+    half = lambda h: slice(128 * h, 128 * h + 128)
 
     dma("s", 512, [], ["tw0"], T.tw[:, 0:2048], T.twist[:, 0:2048])
     dma("a", 512, [], ["tw1"], T.tw[:, 2048:4096], T.twist[:, 2048:4096])
     dma("s", 128, [], ["imgi"], T.imgi[:], T.img[:])
-    dma("a", 128, [], ["tc0"], T.tci[0:64, :], T.turn[:])
-    dma("s", 128, [], ["tc1"], T.tci[64:128, :], T.turn[:])
-    iota(256, ["owni"], T.owni[:], [[0, 256]], 0, 0, False)
+    dma("a", 128, [], ["tci"], T.tci[0:32, :], T.turn[:])
+    ms(256, ["owni"], T.owni[:], 0)
     for q in range(2):
-        dma("s", 128, [], ["cI%d" % q], T.cmpI[:, 256 * q:256 * q + 256], T.ent[:, 4096 * q:4096 * q + 4096])
+        dma("s", 128, CI, ["cI%d" % q], T.cmpI[:, 256 * q:256 * q + 256], T.ent[:, 4096 * q:4096 * q + 4096])
         dma("s", 8, ["owni"], ["ow%d" % q], T.owni[q:128:16, :], T.own[:, 256 * q:256 * q + 256])
-    dma("s", 128, [], ["cI2"], T.cmpI[:, 512:768], T.elen[:])
+    dma("s", 128, CI, ["cI2"], T.cmpI[:, 512:768], T.elen[:])
     dma("s", 8, ["owni"], ["ow2"], T.owni[2:128:16, :], T.olen[:])
 
     iota(8, ["pi0"], T.pi[:, 0:1], [[0, 1]], 0, 1, False)
-    iota(16, ["i8"], T.i8[:], [[1, 16]], 0, 0)
-    iota(128, ["IM"], T.IM[:], [[1, 128]], 0, 0)
-    iota(128, ["IG"], T.IG[:], [[16, 8], [0, 16]], 0, 0)
-    iota(128, ["A8"], T.A8[:], [[8, 8], [0, 16]], 0, 0)
-    iota(16, ["isl"], T.isl[:], [[1, 2], [16, 8]], 1, 0)
-    ms(128, ["CK"], T.CK[:], 0.0); iota(512, ["CKP0"], T.CKP[:], [[0, 512]], 0, 0); iota(512, ["CKP"], T.CKP[0:1, :], [[0, 512]], -49152, 0, r=["CKP0"])
-    ms(1, ["dE0"], T.dE0[:, 0:1], 0.0); ms(1, ["dE1"], T.dE1[:, 0:1], 0.0)
-    iota(128, ["CKa"], T.CK[0:1, 0:128], [[0, 8], [-1, 16]], 15, 0, r=["CK"])
-    ms(64, ["CKb"], T.CK[0:1, 128:256], 4096.0, r=["CK"]); ms(64, ["CKc"], T.CK[32:33, 128:256], -255.0 / 512, r=["CK"])
-    CKr = ["CKa", "CKb", "CKc"]
-    iota(256, ["xi0"], T.xi[:, 0:256], [[1, 256]], 0, 0)
-    iota(16, ["xi1"], T.xi[:, 256:272], [[256, 16]], 0, 0)
-    iota(256, ["JT"], T.JT[:], [[1, 256]], 0, 0)
-    iota(16, ["JB0"], T.JB[:], [[128, 2], [0, 8]], -6815744, 1)
-    ts(16, ["JB0"], ["JB"], T.JB[:], T.JB[:], 4096.0, None, Al.mult)
-    iota(16, ["DUM0"], T.DUM[:], [[16, 16]], 4096, 0)
-    for tb in range(2):
-        for k in range(8):
-            iota(544, ["tab%d" % tb if k == 7 else "tf%d.%d" % (tb, k)], tab[tb][:, 544 * k:544 * k + 544], [[0, 544]], 0, 0, r=["tf%d.%d" % (tb, x) for x in range(7)] if k == 7 else [])
+    iota(16, ["i16"], T.i16[:], [[1, 16]], 0, 0)
+    iota(8, ["G8"], T.G8[:], [[16, 8]], 0, 0)
+    iota(128, ["ones"], T.ones[:], [[0, 128]], 1, 0)
+    sel(128, ["ones"], ["Ib"], T.Ib[:], T.ones[:], [[-1, 128]], Al.is_equal, 0.0, 0, 1)
+    ms(384, ["CK"], T.CK[:], 0.0)
+    for nm, row, lo, x in (("CKa", 0, 0, -255.0 / 512), ("CKe", 0, 128, -255.0 / 512), ("CKb", 0, 384, -255.0 / 512), ("CKc", 32, 256, 4096 * YO)):
+        act(128, ["CK", "ones"], [nm], T.CK[row:row + 1, lo:lo + 128], T.ones[row:row + 1, :], Af.Identity, scale=x)
+    iota(256, ["CKd"], T.CK[0:1, 512:768], [[-128, 2], [1, 128]], 128, 0, r=["CK"])
+    CKr = ["CKa", "CKb", "CKc", "CKe", "ones"]
+    ms(288, ["SA0"], T.SA[0:32, :], 0.0)
+    sel(36, ["SA0"], ["SA"], T.SA[0:32, 15:576:16], T.SA[0:32, 15:576:16], [[1, 4], [4, 9]], Al.not_equal, -1.0, 0, -1)
+    iota(2, ["JB0"], T.JB[:], [[128, 2]], 2047 * 256 - 12 * 2 ** 19, 1)
+    act(2, ["JB0"], ["JB"], T.JB[:], T.JB[:], Af.Identity, scale=4096.0)
+    iota(16, ["DUM"], T.DUM[:], [[16, 16]], 4096, 1)
+    for k in range(4):
+        iota(1120, ["tf%d" % k], T.tab0[:, 1120 * k:1120 * k + 1120], [[0, 1120]], 0, 0)
+    fill = [["tf%d" % k for k in range(4)], ["tg%d" % k for k in range(8)]]
     names = {}
 
     def c(nm):
@@ -152,308 +200,426 @@ def build(T, topo, core, rank):
         ts(1, r, ["c" + nm], c(nm), c(src), c(s1) if isinstance(s1, str) else s1, c(s2) if isinstance(s2, str) else s2, o0, o1)
 
     def cl(nm, src, sc, bi):
-        act(1, ["c" + x for x in (src, bi) if isinstance(x, str)], ["c" + nm], c(nm), c(src), Af.Identity, bias=c(bi) if isinstance(bi, str) else bi, scale=sc)
+        act(1, ["c" + x for x in (src, sc, bi) if isinstance(x, str)], ["c" + nm], c(nm), c(src), Af.Identity,
+            bias=c(bi) if isinstance(bi, str) else bi, scale=c(sc) if isinstance(sc, str) else sc)
     cp(1, ["pi0"], ["cp"], c("p"), T.pi[:, 0:1])
-    for k, (nm, sh, mk) in enumerate((("f", 0, 15), ("p64", 0, 63), ("od", 4, 1))):
+    for k, (nm, sh, mk) in enumerate((("f", 0, 15), ("od", 4, 1))):
         ts(1, ["pi0"], ["pi%d" % (k + 1)], T.pi[:, k + 1:k + 2], T.pi[:, 0:1], sh, mk, Al.arith_shift_right, Al.bitwise_and)
         cp(1, ["pi%d" % (k + 1)], ["c" + nm], c(nm), T.pi[:, k + 1:k + 2])
-    ms(16, ["P2"], T.POW[:, 32:48], 2.0); ms(16, ["P3"], T.POW[:, 48:64], 0.5); ms(16, ["z16"], T.z16[:], 0.0)
-    ts(16, ["i8", "cf"], ["M16"], T.i8[:], T.i8[:], c("f"), None, Al.is_equal)
-    v(16, ["P2", "z16"], ["P0"], lambda q: q.tensor_tensor_scan(T.POW[:, 0:16], T.POW[:, 32:48], T.z16[:], 0.5, Al.mult, Al.add))
-    v(16, ["P3", "z16"], ["P1"], lambda q: q.tensor_tensor_scan(T.POW[:, 16:32], T.POW[:, 48:64], T.z16[:], 2.0, Al.mult, Al.add))
-    for k, nm in ((0, "pw"), (1, "pv")):
-        tt(16, ["P%d" % k, "M16"], ["P%d" % (k + 4)], T.POW[:, 64 + 16 * k:80 + 16 * k], T.POW[:, 16 * k:16 * k + 16], T.i8[:], Al.mult)
-        v(16, ["P%d" % (k + 4)], ["c" + nm], lambda q, k=k, nm=nm: q.tensor_reduce(c(nm), T.POW[:, 64 + 16 * k:80 + 16 * k], AxisListType.X, Al.add))
-    cs("l12", "f", 12, 2.0 ** -8, Al.is_lt, Al.mult)
-    cs("cw", "pw", "l12", None, Al.mult)
-    cs("cw6", "cw", 1.0 / 64, None, Al.mult); cl("ncw", "cw", -1.0, 0.0)
-    cs("g16", "p", "f", None, Al.subtract)
-    G8 = T.IG[:, 0:128:16]
-    ms(72, ["CTW"], T.CTW[:], 0.0)
-    ts(8, ["IG", "cg16", "ccw", "CTW"], ["CTa"], T.CTW[:, 7:71:8], G8, c("g16"), c("cw"), Al.is_equal, Al.mult)
-    ts(8, ["IG", "cg16", "ccw6", "CTW"], ["CTb"], T.CTW[:, 71:135:8], G8, c("g16"), c("cw6"), Al.is_equal, Al.mult)
+    ms(16, ["P2"], T.POW[:, 16:32], 2.0); ms(16, ["P3"], T.POW[:, 32:48], 0.0)
+    ts(16, ["i16", "cf"], ["M16"], T.M16[:], T.i16[:], c("f"), None, Al.is_equal)
+    v(16, ["P2", "P3"], ["P0"], lambda q: q.tensor_tensor_scan(T.POW[:, 0:16], T.POW[:, 16:32], T.POW[:, 32:48], 2.0 ** -13, Al.mult, Al.add))
+    tt(16, ["P0", "M16"], ["P4"], T.POW[:, 48:64], T.POW[:, 0:16], T.M16[:], Al.mult)
+    v(12, ["P4"], ["ccw"], lambda q: q.tensor_reduce(c("cw"), T.POW[:, 52:64], AxisListType.X, Al.add))
+    cl("ncw", "cw", -1.0, 0.0); cl("g16", "f", -1.0, "p")
+    ms(144, ["WD0"], T.WD[:], 0.0)
+    ts(8, ["G8", "cg16"], ["OH"], T.OH[:], T.G8[:], c("g16"), None, Al.is_equal)
+
+    def weights(k, nm):
+        act(8, ["OH", "c" + nm, "WD0"], ["WD%d" % (k + 1)], T.WD[:, 144 * k + 15:144 * k + 143:16], T.OH[:], Af.Identity, scale=c(nm))
+    weights(0, "cw")
     cp(256, ["imgi"], ["offI"], T.offI[:], T.imgi[:]); cp(256, ["imgi"], ["imgf"], T.imgf[:], T.imgi[:])
-    for k, w in enumerate((16.0, "cw", "ncw", -16.0)):
-        ts(8, ["IG", "cg16", "ccw", "cncw"], ["RR%d" % k], T.RR[:, 8 * k:8 * k + 8], G8, c("g16"), c(w) if isinstance(w, str) else w, Al.is_equal, Al.mult)
-    RR = T.RR; RRr = ["RR0", "RR1", "RR2", "RR3"]
-    for nm, d in (("m1", 1), ("m7", 7), ("m12", 12)):
-        cl(nm, "p", 1.0, -float(d))
-    cs("s01", "f", 2, None, Al.is_lt); cs("dv", "f", 4, -2.0 / 4096, Al.is_ge, Al.mult); cs("j3", "f", 3, None, Al.is_equal)
-    cl("ev", "od", -1.0, 1.0)
-    cs("a0", "f", 12, 512.0, Al.is_ge, Al.mult); cl("a", "a0", 1.0, -256.0)
-    cs("c", "f", 12, 512.0, Al.is_equal, Al.mult)
-    cs("b0", "f", 6, 512.0, Al.not_equal, Al.mult); cs("b1", "f", 13, "b0", Al.is_lt, Al.mult); cs("b", "f", 0, "b1", Al.is_gt, Al.mult)
-    cs("v0", "f", 6, 63.0, Al.is_ge, Al.mult); cs("pv6", "v0", 1.0, "pv", Al.add, Al.mult)
-    cl("pvb", "pv", 16.0, 0.0)
-    cl("ahi", "a0", 8192.0, 0.0); cl("chi", "a0", -4096.0, 0.0); cl("nhi", "a0", -8192.0, 0.0)
-    cl("al0", "dv", -512.0 * 4096 * 4096, "nhi")
-    cs("c2", "f", 2, 256.0, Al.is_equal, Al.mult); cs("c3", "c2", "j3", 4096.0, Al.add, Al.mult); cl("clo", "al0", -0.5, "c3")
-    k0 = len(names); names["se"] = k0; names["so"] = k0 + 1
-    ms(1, ["se0"], T.col[0:64, k0:k0 + 1], -1.0); ms(1, ["se1"], T.col[64:128, k0:k0 + 1], -1.0 / 64)
-    ms(1, ["so0"], T.col[0:64, k0 + 1:k0 + 2], 4096 - 0.5 + 2.0 ** -9); ms(1, ["so1"], T.col[64:128, k0 + 1:k0 + 2], 64 - 0.5 + 2.0 ** -15)
+    for k, w in enumerate(("cw", "ncw", -256.0, "cw", 256.0)):
+        act(8, ["OH", "ccw", "cncw"], ["RR%d" % k], RR[:, 8 * k:8 * k + 8], T.OH[:], Af.Identity, scale=c(w) if isinstance(w, str) else w)
+    RRr = ["RR%d" % k for k in range(5)]
+    cs("dv", "f", 4, -2.0 / 4096, Al.is_ge, Al.mult)
+    for nm, k, sc, bi in (("s01", 0, 1.0, T.M16[:, 1:2]), ("j4", 3, 4096.0, 0.0), ("b2", 2, 2.0 ** 20, c("j4"))):
+        act(1, ["M16", "cj4"], ["c" + nm], c(nm), T.M16[:, k:k + 1], Af.Identity, bias=bi, scale=sc)
+    cs("b", "dv", 2.0 ** 32, "b2", Al.mult, Al.add)
+    cs("b1", "od", "b", None, Al.mult); cs("b0", "b1", -1.0, "b", Al.mult, Al.add); cs("s1", "od", -2.0 ** 14, None, Al.mult); cs("s0", "od", 2.0 ** 14, -2.0 ** 14, Al.mult, Al.add)
+    act(8, ["OH"], ["OHb"], T.OHb[:], T.OH[:], Af.Identity, scale=-8192.0)
 
-    def eq(nm, src, colnm, s):
-        ts(128, [src, "c" + colnm] + (["c" + s] if isinstance(s, str) else []), [nm], T[nm][:], T[src][:], c(colnm), c(s) if isinstance(s, str) else s, Al.is_equal, Al.mult)
-
-    def scaled(nm, s):
-        act(128, ["Ib"] + (["c" + s] if isinstance(s, str) else []), [nm], T[nm][:], T.Ib[:], Af.Identity, scale=c(s) if isinstance(s, str) else s)
-    ms(48, ["A8a"], T.A8[0:64, :, 6:16], 1000.0, r=["A8"]); ms(48, ["A8b"], T.A8[64:128, :, 0:6], 1000.0, r=["A8"]); ms(48, ["A8c"], T.A8[64:128, :, 12:16], 1000.0, r=["A8"])
-    for i in range(8):
-        ts(128, ["A8a", "A8b", "A8c", "cp64"], ["BC%d" % i], T.BC[:, 128 * i:128 * i + 128], T.A8[:], float(i), c("p64"), Al.add, Al.is_equal)
-    eq("Ib", "IM", "p", 1.0)
-    scaled("bd1", "a"); eq("bd2", "IM", "m1", "b"); eq("bd3", "IG", "m12", -256.0); eq("bd4", "IM", "m7", "c")
-    tt(128, ["bd1", "bd2"], ["bd1"], T.bd1[:], T.bd1[:], T.bd2[:], Al.add); tt(128, ["bd3", "bd4"], ["bd3"], T.bd3[:], T.bd3[:], T.bd4[:], Al.add)
-    tt(128, ["bd1", "bd3"], ["BD"], T.BD[:], T.bd1[:], T.bd3[:], Al.add)
-    eq("Dp0", "IG", "p", 1.0); eq("Dm1", "IG", "m1", -1.0)
-    tt(128, ["Dp0", "Dm1"], ["D0a"], T.D01[:], T.Dm1[:], T.Dp0[:], Al.add)
-    act(128, ["D0a"], ["D01"], T.D01[:], T.D01[:], Af.Identity, scale=-1.0)
-    for nm, sc in (("If", 1.0), ("nI", -1.0), ("S01", "s01"), ("DB", "dv"), ("J3", "j3")):
+    def scaled(nm, sc):
+        act(128, ["Ib"] + (["c" + sc] if isinstance(sc, str) else []), [nm], T[nm][:], T.Ib[:], Af.Identity, scale=c(sc) if isinstance(sc, str) else sc)
+    for nm, sc in (("If", 1.0), ("nI", -1.0), ("S01", "s01"), ("DB", "dv")) + ((("nIf", -1.0),) if LL & 1 else ()):
         scaled(nm, sc)
-    ts(16, ["isl", "cp"], ["SL"], T.SL[:], T.isl[:], c("p"), None, Al.is_equal)
-    iota(128, ["ones"], T.ones[:], [[0, 128]], 1, 0)
-    iota(128, ["seg0"], T.seg[:], [[0, 128]], 1, 0); ms(8, ["seg"], T.seg[:, 0:128:16], 0.0, r=["seg0"])
-    iota(256, ["MK0"], T.MK[:], [[0, 16], [1, 16]], 0, 0); ts(256, ["MK0", "cf"], ["MK"], T.MK[:], T.MK[:], c("f"), None, Al.is_equal)
-    iota(16, ["ogi"], T.ogi[:], [[1, 16]], 0, 0, False); cp(16, ["ogi"], ["offG"], T.offG[:], T.ogi[:])
-    ts(8, ["IG", "cg16"], ["OH"], T.OH[:], G8, c("g16"), None, Al.is_equal); iota(16, ["DT"], T.DT[:], [[128, 2], [0, 8]], 4096, 1)
-    ms(128, ["Mz"], T.Mz[:], 0.0)
-    ts(16, ["DUM0", "cf"], ["DUM"], T.DUM[:], T.DUM[:], c("f"), None, Al.add)
-    ts(272, ["xi0", "xi1", "cpvb"], ["xj"], T.xj[:], T.xi[:], c("pvb"), -0.5 + 2.0 ** -12, Al.mult, Al.add)
-    ts(272, ["xj"], ["xk"], T.xk[:], T.xj[:], 1, None, Al.bitwise_and)
-    ts(256, ["xk", "cal0", "cclo"], ["Plo"], T.Plo[:], T.xk[:, 0:256], c("al0"), c("clo"), Al.mult, Al.add)
-    ts(16, ["xk", "cahi", "cchi"], ["Phi"], T.Phi[:], T.xk[:, 256:272], c("ahi"), c("chi"), Al.mult, Al.add)
-    for k in range(16):
-        if k < BV:
-            ts(128, ["Plo", "Phi"], ["bits%d" % k], T.bits[:, 256 * k:256 * k + 256], T.Plo[:], T.Phi[:, k:k + 1], None, Al.add)
-        else:
-            act(256, ["Plo", "Phi"], ["bits%d" % k], T.bits[:, 256 * k:256 * k + 256], T.Plo[:], Af.Identity, bias=T.Phi[:, k:k + 1])
-    bitsr = ["bits%d" % k for k in range(16)]
+    rows = [[-16, 8], [0, 16]]
+    sel(128, ["ones"], ["Dp0"], T.Dp0[:], T.ones[:], rows, Al.is_equal, 0.0, 0, 1)
+    sel(128, ["ones"], ["Dp1"], T.Dp1[:], T.ones[:], rows, Al.is_equal, 0.0, -1, 1)
+    sel(128, ["Dp1"], ["D01"], T.D01[:], T.Dp1[:], rows, Al.not_equal, -1.0, 0, 1)
+    act(128, ["Dp1"], ["Dm1"], T.Dm1[:], T.Dp1[:], Af.Identity, scale=-1.0)
+    sel(8, ["ones"], ["SL"], T.SL[:], T.ones[:, 0:8], [[-16, 8]], Al.is_equal, 0.0, -2, 1)
+    ms(256, ["seg0"], T.seg[:], 0.0); ms(16, ["seg"], T.seg[:, 0:256:16], 2.0 ** 23, r=["seg0"])
+    act(16, ["M16"], ["MK4"], T.MK[:, 0:16], T.M16[:], Af.Copy)
+    for s in range(4, 8):
+        act(1 << s, ["MK%d" % s], ["MK%d" % (s + 1) if s < 7 else "MK"], T.MK[:, 1 << s:2 << s], T.MK[:, 0:1 << s], Af.Copy)
+    cp(16, ["i16"], ["offG"], T.offG[:], T.i16[:])
+    ms(128, ["Mz0"], T.Mz[:], 0.0)
+    for h in range(2):
+        ts(8, ["Mz0", "WD0", "cp"], ["Mj%d" % h], T.Mz[:, 128 * h + 3:128 * h + 128:16], T.WD[:, 0:8], c("p"), 128.0 * h, Al.add, Al.add)
+    act(16, ["M16"], ["DL"], T.DL[:], T.M16[:], Af.Identity, scale=-256.0)
+    act(1, ["M16"], ["bits0"], T.bits[:, 0:1], T.M16[:, 0:1], Af.Identity, scale=0.0)
+    for s in range(12):
+        n = 1 << s
+        for j in range(2 if n > 512 else 1):
+            m = n // 2 if n > 512 else n
+            a = s < BA
+            shift(a, m if a else m // 2, ["bits%d" % s, "bitt%d" % s, "DL"], ["bit%s%d" % ("st"[j], s + 1)], T.bits[:, n + j * m:n + j * m + m], T.bits[:, j * m:j * m + m], T.DL[:, 4 + s:5 + s])
+    bitsr = ["bits12", "bitt12"]
 
     Pb = lambda k: T.pP[:, 512 * k:512 * k + 512]
+    ts(1024, ["tci"], ["tch"], T.tch[0:32, :], T.tci[0:32, :], 2048, None, Al.subtract)
+    mm(["CK", "SA"], ["Z0"], [(T.pZ0[:, 0:256], T.CK[0:32, 256:384], T.SA[0:32, 0:256], True, 256)])
+    for a in range(4):
+        mm(["tch", "SA"], ["Z0"], [(T.pZ0[:, 64 * a:64 * a + 64], T.SA[0:32, 144 * a + 15 - r:144 * a + 143 - r], T.tch[0:32, r:1024:16], False, 64) for r in range(16)])
     for hh in range(2):
-        mm(["tw%d" % hh, "CTa", "CTb"], ["Z0"], [(T.pZ0[:], T.CTW[:, 7 - i:135 - i], T.tw[:, 512 * i:512 * i + 512], i == 0, 512) for i in range(4 * hh, 4 * hh + 4)])
-    ts(512, ["tc0", "tc1", "se0", "se1", "so0", "so1"], ["ta"], T.ta[:], T.tci[:], c("se"), c("so"), Al.mult, Al.add)
-    tt(512, ["ta"], ["ki"], T.ki[:], T.pZ0[:], T.ta[:], Al.add, b=["Z0"])
-    ts(512, ["ki"], ["kj"], T.kj[:], T.ki[:], 63, None, Al.bitwise_and)
-    cp(512, ["kj"], ["kb16"], T.kb16[:], T.kj[:])
-    Rb = [T.Rb0, T.Rb1]
-    for i in range(8):
-        e = i % 2; sl = slice(512 * i, 512 * i + 512)
-        mm(["kb16", "BC%d" % i], ["P%d" % e], [(Pb(e), T.BC[:, 128 * i:128 * i + 128], T.kb16[:], True, 512)])
-        act(512, ["cpv6"], ["Rb%d" % e], Rb[e][:], Pb(e), Af.Identity, bias=191.515625, scale=c("pv6"), b=["P%d" % e])
-        if i % 4 < HA:
-            mm(["Rb%d" % e, "BD", "Ib", "tw%d" % (i // 4)], ["P%d" % (2 + e)], [(Pb(2 + e), T.Ib[:], T.tw[:, sl], True, 512), (Pb(2 + e), T.BD[:], Rb[e][:], False, 512)])
-            act(512, [], ["H%d" % i], T.Hw[:, sl], Pb(2 + e), Af.Copy, b=["P%d" % (2 + e)])
-        else:
-            mm(["Rb%d" % e, "BD"], ["P%d" % (2 + e)], [(Pb(2 + e), T.BD[:], Rb[e][:], True, 512)])
-            tt(512, ["tw%d" % (i // 4)], ["H%d" % i], T.Hw[:, sl], Pb(2 + e), T.tw[:, sl], Al.add, b=["P%d" % (2 + e)])
-    Hr = ["H%d" % i for i in range(8)]
-    for k in range(1, 4):
-        dma("s", 1024, Hr, ["Hx%d" % k], T.Hw[:, 4096 * k:4096 * k + 4096], T.Hw[:, 0:4096])
-    Hxr = Hr + ["Hx1", "Hx2", "Hx3"]
+        mm(["tw%d" % hh, "WD1"], ["Z0"], [(T.pZ0[:, half(hh)], T.WD[:, 15 - r:143 - r], T.tw[:, 2048 * hh + r:2048 * hh + 2048:16], False, 128) for r in range(16)])
+    ts(256, [], ["ui0", "ui1"], T.ui[:], T.pZ0[:, 0:256], 2048 - 255.0 / 512, None, Al.add, b=["Z0"])
+    ts(256, ["ui0", "ui1"], ["uj0", "uj1"], T.uj[:], T.ui[:], 4095, None, Al.bitwise_and)
+    cp(256, ["uj0", "uj1"], ["offK"], T.offK[:], T.uj[:])
+    iota(512, ["CKP0"], T.CKP[0:32, :], [[0, 512]], 0, 0, r=["offK"]); iota(512, ["CKP"], T.CKP[0:1, :], [[0, 512]], -int(YO), 0, r=["CKP0"])
+    for k in range(8):
+        iota(560, ["tg%d" % k], T.tab1[:, 560 * k:560 * k + 560], [[0, 560]], 0, 0, r=["offK"])
+    Hr = ["H%d" % i for i in range(NH)]
 
-    cp(768, ["cI0", "cI1", "cI2"], ["cmp0", "cmp1", "cmp2"], T.cmp[:], T.cmpI[:])
+    def window():
+        for s in range(NH):
+            n = 4096 // NH; sl = slice(n * s, n * s + n); bit = T.bits[:].indirect(T.offK[:, n * s // 16:(n * s + n) // 16])
+            if s < NH - HA:
+                tt(n * GC, bitsr + ["offK", "tw0", "tw1"], ["H%d" % s], T.Hw[:, sl], bit, T.tw[:, sl], Al.add)
+            else:
+                z = s % 2; tmp = T.y1[:, n * z:n * z + n]
+                act(n * GC, bitsr + ["offK"], ["y1.%d" % z], tmp, bit, Af.Copy)
+                mm(["y1.%d" % z, "Ib", "tw0", "tw1"], ["Z%d" % z], [(pZ[z][:], T.Ib[:], T.tw[:, sl], True, 512), (pZ[z][:], T.Ib[:], tmp, False, 512)])
+                act(n, [], ["H%d" % s], T.Hw[:, sl], pZ[z][:], Af.Copy, b=["Z%d" % z])
+        for hh in range(4):
+            for k in range(1, 4):
+                dma("s", 256, Hr[hh * NH // 4:(hh + 1) * NH // 4], ["Hx%d.%d" % (k, hh)], T.Hw[:, 4096 * k + 1024 * hh:4096 * k + 1024 * hh + 1024], T.Hw[:, 1024 * hh:1024 * hh + 1024])
+    Hxr = Hr + ["Hx%d.%d" % (k, hh) for k in range(1, 4) for hh in range(4)]
+
+    ts(768, ["cI0", "cI1", "cI2"], ["cmp0", "cmp1", "cmp2"], T.cmp[:], T.cmpI[:], 2048, None, Al.subtract)
 
     def unpack(src, keys, tb):
         for q in range(3):
-            dma("s", 128, keys + ["tab%d" % tb], ["tab%d.%d" % (tb, q)], tab[tb][q:128:16, 0:4096], src[:, 256 * q:256 * q + 256])
-    tabk = lambda tb: ["tab%d" % tb] + ["tab%d.%d" % (tb, q) for q in range(3)]
-    unpack(T.cmp, ["cmp0", "cmp1", "cmp2"], 0)
-    ts(256, ["ow0", "ow1", "ow2"], ["A0.0", "A0.1"], T.A0[:], T.owni[:], 2048, None, Al.subtract)
+            dma("s", 128, [keys % q] + fill[tb], ["tab%d.%d" % (tb, q)], tab[tb][q:128:16, 0:4096], src[:, 256 * q:256 * q + 256])
+    tabk = lambda tb: fill[tb] + ["tab%d.%d" % (tb, q) for q in range(3)]
+    unpack(T.cmp, "cmp%d", 0)
+    ts(256, ["ow0", "ow1", "ow2"], ["A0"], T.A0[:], T.owni[:], 2048, None, Al.subtract)
     tn = lambda k: T.tn[:, 16 * k:16 * k + 16]
-    m = tn(0)
-    mm(["A0.0", "A0.1", "SL"], ["Z1"], [(T.pZ1[:, 8 * h:8 * h + 8], T.A0[:, 128 * h:128 * h + 128], T.SL[:, 8:16], True, 64) for h in range(2)])
-    ts(16, [], ["m"], m, T.pZ1[:, 0:16], 2048.0, None, Al.add, b=["Z1"])
+    Mz = T.Mz[:, 2:256:16]
+    lb = T["p" + LB][:, 0:16]
+    mm(["A0", "SL"], [LB], [(T["p" + LB][:, 8 * h:8 * h + 8], T.A0[:, half(h)], T.SL[:], True, 64) for h in range(2)])
 
-    def gather(h, win, wr, off, offr, new, prev):
-        for s in range(NP):
-            o = off[:, 128 * h + PL * s:128 * h + PL * s + PL]; sl = slice(PW * s, PW * s + PW)
+    def lengths(grow, src, r, b):
+        ts(16, ["Mz0"] + r, ["Mz"], Mz, src, grow, 2047.0, Al.add, Al.min, b=b)
+        act(16, r, ["mr"], tn(8), src, Af.Relu, bias=2047.0 - grow, scale=-1.0, b=b)
+        for h in range(2):
+            act(8, ["mr", "JB"], ["kb%d" % h], T.tn[:, 32 + 8 * h:40 + 8 * h], T.tn[:, 128 + 8 * h:136 + 8 * h], Af.Identity, bias=T.JB[:, h:h + 1], scale=-2.0 ** 20)
+    lengths(0.0, lb, [], [LB])
+
+    def gather(h, npc, win, wr, off, offr, new, prev, name=""):
+        for s in range(npc):
+            tag[0] = name and "%s%d%d" % (name, h, s)
+            n = 2048 // npc; o = off[:, 128 * h + n * s // 16:128 * h + (n * s + n) // 16]; sl = slice(n * s, n * s + n)
+            ks = range(4 * s // npc, 4 * (s + 1) // npc)
             if h == 1:
-                act(PW * GC, wr + offr, ["G%d.%d" % (new, s)], G[new][:, sl], win.indirect(o), Af.Copy)
+                act(n * GC, wr + offr, ["G%d.%d" % (new, k) for k in ks], G[new][:, sl], win.indirect(o), Af.Copy)
             elif prev is not None:
-                tt(PW * GC, wr + offr + ["X%d.%d" % (prev, s)], ["X%d.%d" % (new, s)], X[new][:, sl], win.indirect(o), X[prev][:, sl], Al.add)
-            elif s < X0A:
-                act(PW * GC, wr + offr, ["X%d.%d" % (new, s)], X[new][:, sl], win.indirect(o), Af.Copy)
+                tt(n * GC, wr + offr + ["X%d.%d" % (prev, k) for k in ks], ["X%d.%d" % (new, k) for k in ks], X[new][:, sl], win.indirect(o), X[prev][:, sl], Al.add)
             else:
-                cp(PW * GC, wr + offr, ["X%d.%d" % (new, s)], X[new][:, sl], win.indirect(o))
+                act(n * GC, wr + offr, ["X%d.%d" % (new, k) for k in ks], X[new][:, sl], win.indirect(o), Af.Copy)
 
-    def addP(k):
+    def addP(src, key, q, start=False):
         for bk in range(4):
-            if k is None:
-                mm(["CKP", "Ib", "ones"], ["P%d" % bk], [(Pb(bk), T.ones[:], T.CKP[:], True, 512)])
-            else:
-                mm(["G%d.%d" % (k, bk * NP // 4), "Ib", "ones"], ["P%d" % bk], [(Pb(bk), T.Ib[:], G[k][:, 512 * bk:512 * bk + 512], False, 512)])
+            tag[0] = "add%d%d" % (q, bk)
+            mm([key % bk, "Ib"], ["P%d" % bk], [(Pb(bk), T.Ib[:], src[:, 512 * bk:512 * bk + 512], start, 512)])
 
-    def tr(h, src, keys, lo, hi, rhs):
-        mm(keys + RRr, ["T%d" % h], [(pT[h][:, lo + i:hi:16], src[:, i:2048:16], rhs, False, 64) for i in range(16)])
+    def tr(h, src, keys, lo, n, r0, last=False):
+        lst = [(pT[:, lo + i:lo + 128 * n:16], src[:, i:2048:16], RR[:, r0:r0 + 8 * n], False, 64) for i in range(16)]
+        if last:
+            lst += [(pT[:, K0[h]:K0[h] + 128], T.ones[0:32, :], T.CK[0:32, 512 + 128 * h:640 + 128 * h], False, 128)]
+        mm(keys + RRr + ["CKd", "ones"], ["T%d" % h], lst)
 
-    def const(h, lo, hi):
-        mm(CKr + ["ones"], ["T%d" % h], [(pT[h][:, lo:hi], T.ones[:], T.CK[:, lo:hi], True, hi - lo)])
+    def direct(h, src, key, neg, name=""):
+        for s in range(2):
+            tag[0] = "d%d%d" % (h, s) if name else tag[0]
+            mm([key % (2 * s), key % (2 * s + 1), "WD%d" % (1 + neg)], ["T%d" % h],
+               [(pT[:, U0[h] + 64 * s:U0[h] + 64 * s + 64], T.WD[:, 144 * neg + 15 - i:144 * neg + 143 - i], src[:, 1024 * s + i:1024 * s + 1024:16], False, 64) for i in range(16)])
 
-    def escopy(h, diff):
-        if ESA >> h & 1:
-            act(128, [], ["ES%d" % h], ES[h][:], pT[h][:, 128:256], Af.Copy, b=["T%d" % h])
-        else:
-            cp(128, [], ["ES%d" % h], ES[h][:], pT[h][:, 128:256], b=["T%d" % h])
-        if diff:
-            tt(128, ["ES%d" % h], ["dE%d" % h], T["dE%d" % h][:, 1:128], ES[h][:, 0:127], pT[h][:, 129:256], Al.subtract, b=["T%d" % h])
+    def const(h, lo, n, c0, full):
+        k = 64 if full else 32
+        mm(CKr, ["T%d" % h], [(pT[:, lo:lo + n], T.ones[0:k, :], T.CK[0:k, c0:c0 + n], True, n)])
 
-    def nterms(h, terms, turn):
-        o = pT[h][:, 256:384]
-        mm((["ES%d" % h, "If"] if turn else []) + [x for t in terms for x in (t[0], "A%d.%d" % (t[1], h))], ["T%d" % h],
-           ([(o, ES[h][:], T.If[:], True, 512)] if turn else []) + [(o, T[t[0]][:], A[t[1]][:, 128 * h:128 * h + 128], False, 128) for t in terms])
+    def escopy(h):
+        n = 256 - 128 * h
+        shift(ESA >> h & 1, n, [], ["ES%d" % h], ES[:, EC[h]:EC[h] + n], pT[:, E0[h]:E0[h] + n], 0.0, b=["T%d" % h])
+
+    def turned(h):
+        mm(["ES%d" % h, "If"], ["T%d" % h], [(pT[:, U0[h]:U0[h] + 128], ES[:, EC[h]:EC[h] + 128], T.If[:], True, 512)])
+
+    def letters(h, mat, cur):
+        mm([mat, "A%d" % cur], ["T%d" % h], [(pT[:, U0[h]:U0[h] + 128], T[mat][:], A[cur][:, half(h)], False, 128)])
 
     def nstage(h, add, out, key, plain):
-        o = pT[h][:, 256:384]; sl = slice(128 * h, 128 * h + 128)
+        o = pT[:, U0[h]:U0[h] + 128]; sl = half(h)
         if plain:
             ts(128, [], [key], out[:, sl], o, MG, MG - add, Al.add, Al.subtract, b=["T%d" % h])
         else:
-            ts(128, [], ["ui%d" % h], T.ui[:, sl], o, MG, MG - add, Al.add, Al.subtract, b=["T%d" % h])
+            ts(128, [], ["ui%d" % h], T.ui[:, sl], o, float(add), None, Al.add, b=["T%d" % h])
+            if AU and key[0] == "o":
+                ts(128, ["ui%d" % h], [key], out[:, sl], T.ui[:, sl], 4095, None, Al.bitwise_and)
+                return
             ts(128, ["ui%d" % h], ["uj%d" % h], T.uj[:, sl], T.ui[:, sl], 4095, None, Al.bitwise_and)
             cp(128, ["uj%d" % h], [key], out[:, sl], T.uj[:, sl])
 
-    def reduce256(src, sk, out, ok, ra):
+    def reduce256(src, sk, out, ok, ra, h=0):
         for bk in range(4):
-            z = bk % 2; sl = slice(512 * bk, 512 * bk + 512)
-            mm([sk % (bk * NP // 4), "y0.%d" % (bk // 2), "Ib", "nI"], ["Z%d" % z], [(pZ[z][:], T.Ib[:], src[:, sl], True, 512), (pZ[z][:], T.nI[:], T.y0[:, sl], False, 512)])
-            if bk < ra:
-                act(512, [], ok(bk), out[:, sl], pZ[z][:], Af.Identity, bias=-49152.0, b=["Z%d" % z])
-            else:
-                ts(512, [], ok(bk), out[:, sl], pZ[z][:], -49152.0, None, Al.add, b=["Z%d" % z])
+            z = bk % 2; sl = slice(512 * bk, 512 * bk + 512); tag[0] = "mod%d" % bk
+            mm([sk % bk, "y%d.%d" % (h, bk), "Ib", "nI"], ["Z%d" % z], [(pZ[z][:], T.Ib[:], src[:, sl], True, 512), (pZ[z][:], T.nI[:], T["y%d" % h][:, sl], False, 512)])
+            shift(bk < ra, 512, [], [ok % bk], out[:, sl], pZ[z][:], -YO, b=["Z%d" % z])
 
     for h in range(2):
-        gather(h, T.tw[:], ["tw0", "tw1"], T.offI, ["offI"], 2 if h else 3, None)
-        const(h, 0, 256)
-        mm(["imgf", "If"], ["T%d" % h], [(pT[h][:, 128:256], T.imgf[:, 128 * h:128 * h + 128], T.If[:], False, 512)])
-        tr(h, G[2] if h else X[3], allp("G2" if h else "X3"), 0, 128, RR[:, 0:8])
-        escopy(h, True)
+        gather(h, 2, T.tw[:], ["tw0", "tw1"], T.offI, ["offI"], 2 if h else 3, None)
+        const(h, 128 + 384 * h, 384 - 128 * h, 256 * h, False)
+        mm(["imgf", "If"], ["T%d" % h], [(pT[:, E0[h]:E0[h] + 128], T.imgf[:, half(h)], T.If[:], False, 512)])
+        if h:
+            tr(1, G[2], allp("G2"), K0[1], 1, 16, True)
+        else:
+            tr(0, X[3], allp("X3"), 256, 2, 8, True)
+    escopy(0)
     at = [3]
     for n in range(1, 7):
         cur, old = n % 2, 1 - n % 2
         tb = ((n - 1) // 2) % 2
-        win, wr = (T.Hw[:, 0:4096], Hr) if n == 1 else (T.Hw[:], Hxr)
-        for h in range(2):
-            bk = ["T%d" % h]; Rm = T["Rm%d" % h]; nn = T["nn%d" % h]; Wm = T["Wm%d" % h]; s8 = slice(8 * h, 8 * h + 8)
-            v(128, ["seg"], ["Rm%d" % h], lambda q, Rm=Rm, h=h: q.tensor_tensor_scan(Rm[:], T.seg[:], pT[h][:, 0:128], 0.0, Al.mult, Al.max), bk)
-            tt(128, ["Rm%d" % h], ["nn%d" % h], nn[:], pT[h][:, 0:128], Rm[:], Al.is_lt, b=bk)
-            v(128, ["nn%d" % h, "dE%d" % h], ["Wm%d" % h], lambda q, Wm=Wm, nn=nn, h=h: q.tensor_tensor_scan(Wm[:], T["dE%d" % h][:], nn[:], 0.0, Al.add, Al.mult))
-            e15 = ES[h][:, 15:128:16]
-            if n > 1:
-                tt(8, ["ES%d" % h, "AT%d" % old], ["e15%d" % h], T.e15[:, s8], e15, AT[old][:, s8], Al.subtract)
-            tt(8, ["Wm%d" % h, "ES%d" % h, "e15%d" % h], ["wi%d" % h], T.wi[:, s8], Wm[:, 15:128:16], T.e15[:, s8] if n > 1 else e15, Al.add)
-            ts(8, ["wi%d" % h], ["wj%d" % h], T.wj[:, s8], T.wi[:, s8], 4095, None, Al.bitwise_and)
-            tt(200, ["wj%d" % h, "offG", "MK"], ["Wz%d" % h], T.Wz[:, 128 * h:128 * h + 128], T.wj[:, s8].indirect(T.offG[:, 0:8]), T.MK[:, 0:128], Al.mult)
-            mm(["Wz%d" % h, "OH"], bk, [(pT[h][:, 384:392], T.Wz[:, 128 * h:128 * h + 128], T.OH[:], True, 256)])
-            cp(8, [], ["oO%d.%d" % (cur, h)], offO[cur][:, s8], pT[h][:, 384:392], b=bk)
-            nterms(h, [("Dm1", old)] if n > 1 else [], True)
-            ts(200, tabk(tb) + ["oO%d.%d" % (cur, h)], ["A%d.%d" % (cur, h)], A[cur][:, 128 * h:128 * h + 128], tab[tb][:].indirect(offO[cur][:, s8]), 2048.0, None, Al.subtract)
-            nterms(h, [("Dp0", cur)], False)
-            nstage(h, 2048 if n == 1 else 4096, T.offU0, "oU0.%d" % h, n > 1)
-        oO = ["oO%d.0" % cur, "oO%d.1" % cur]; Ac = ["A%d.0" % cur, "A%d.1" % cur]; Ao = ["A%d.0" % old, "A%d.1" % old]
-        ts(16, ["m"], ["Mz"], T.Mz[:, 2:256:16], m, 4095.0, 2048.0, Al.min, Al.subtract)
-        ts(16, ["m"], ["t1"], tn(1), m, 4095.0, 256.0 * 4096, Al.min, Al.mult)
-        tt(16, ["t1", "JB"], ["kb"], tn(2), tn(1), T.JB[:], Al.add)
+        kind = 2 if n == 6 else 1 - cur
+        NZD, YV, BANKS = NZ[kind], YS[kind], BK[kind]
+        first = len(ops); tag[0] = "window"
+        if n == 1:
+            window()
+        if n == 4:
+            reduce256(X[at[0]], "X%d." % at[0] + "%d", X[3], "X3.%d", RA)
+            at[0] = 3
+        tag[0] = "chain"
+        v(256, ["seg"], ["Rm"], lambda q: q.tensor_tensor_scan(T.Rm[:], T.seg[:], pT[:, 384:640], 0.0, Al.add, Al.min), ["T0", "T1"])
+        escopy(1)
+        if AU:
+            ts(16, ["Rm"], ["offW"], T.offW[:], T.Rm[:, 15:256:16], 255, None, Al.bitwise_and)
+        else:
+            ts(16, ["Rm"], ["oj"], T.oj[:], T.Rm[:, 15:256:16], 255, None, Al.bitwise_and)
+            cp(16, ["oj"], ["offW"], T.offW[:], T.oj[:])
+        tt(256 * GC, ["ES0", "ES1", "offW", "MK"], ["Wz"], T.Wz[:], ES[:, 128:384].indirect(T.offW[:]), T.MK[:], Al.mult)
+        turned(0)
+        mm(["Wz", "OH"], ["T1"], [(pT[:, L0 + 8 * h:L0 + 8 * h + 8], T.Wz[:, half(h)], T.OH[:], True, 256) for h in range(2)])
+        pv = T.pZ1[:, 0:256]; tag[0] = "pv"
+        mm(["A%d" % old, "S01", "Mz", "Mj0", "Mj1", "Ib"], ["Z1"], [(pv, T.S01[:], A[old][:], True, 256)] +
+           [(T.pZ1[:, half(h)], T.Mz[:, half(h)], T.Ib[:], False, 128) for h in range(2)])
+        if n == 1:
+            ops[-1]["tag"] = "xl"
+        tag[0] = "point"
+        ts(16, [], ["wi"], T.wi[:], pT[:, L0:L0 + 16], 2048.0 if n > 1 else 0.0, None, Al.add, b=["T1"])
+        turned(1)
+        if AU:
+            ts(16, ["wi"], ["oO"], T.offO[:], T.wi[:], 4095, None, Al.bitwise_and)
+            tag[0] = "win"
+        ts(16, ["wi"], ["wj"], T.wj[:], T.wi[:], 4095, None, Al.bitwise_and)
+        tag[0] = "point"
+        if not AU:
+            cp(16, ["wj"], ["oO"], T.offO[:], T.wj[:])
+        shift(False, 256 * GC, tabk(tb) + ["oO"], ["A%d" % cur], A[cur][:], tab[tb][:].indirect(T.offO[:]), -2048.0 if n > UN else 0.0)
+        for h in (1, 0):
+            tag[0] = "go%d" % h
+            letters(h, "Dp0", cur)
+            nstage(h, 2048 if n == 1 else 8192, T.offU0, "oU0.%d" % h, n > 1 or M1 < 1)
+        tag[0] = "xl"
         for par in range(2):
-            act(400, bitsr + oO + ["cev", "cod"], ["XL%d" % par], XL[par][:], T.bits[:].indirect(offO[cur][:]), Af.Identity, scale=c("od" if par else "ev"))
-        mm(Ac + ["SL"], ["Z0"], [(T.pZ0[:, 16 * f + 8 * h:16 * f + 8 * h + 8], A[cur][:, 128 * h:128 * h + 128], T.SL[:, 8 * f:8 * f + 8], True, 64) for h in range(2) for f in range(2)])
-        act(32, [], ["AT%d" % cur], AT[cur][:], T.pZ0[:, 0:32], Af.Identity, bias=2048.0, b=["Z0"])
-        tt(16, ["m", "AT%d" % cur], ["dl"], tn(4), AT[cur][:, 16:32], m, Al.subtract)
-        tt(16, ["wj0", "wj1", "DT"], ["wd"], tn(7), T.wj[:], T.DT[:], Al.subtract)
-        pv = T.pZ1[:, 0:256]
-        mm(Ao + ["S01", "Mz", "Ib", "J3", "JT"], ["Z1"], [(pv, T.S01[:], A[old][:], True, 256), (pv, T.J3[:], T.JT[:], False, 256)] +
-           [(T.pZ1[:, 128 * h:128 * h + 128], T.Mz[:, 128 * h:128 * h + 128], T.Ib[:], False, 128) for h in range(2)])
+            act(256 * GC, bitsr + ["oO", "cs%d" % par, "cb%d" % par], ["XL%d" % par], XL[par][:], T.bits[:].indirect(T.offO[:]), Af.Identity, bias=c("b%d" % par), scale=c("s%d" % par))
         mm(["XL0", "XL1", "DB"], ["Z1"], [(pv, T.DB[:], XL[par][:], False, 256) for par in range(2)])
-        cp(256, [], ["XR"], T.XR[:], pv, b=["Z1"])
-        act(256, [], ["V%d" % cur], V[cur][:], pv, Af.Identity, bias=2048.0, b=["Z1"])
-        if cur == 0:
-            send(3 * (n // 2 - 1) + 1, 128, ["V0"], ["lv%d" % (n // 2 - 1)], T["lv%d" % (n // 2 - 1)][:], V[0][:])
+        tag[0] = "xr"
+        cp(256, [], ["XR%d" % cur], XR[cur][:], pv, b=["Z1"])
+        tag[0] = "at"
+        mm(["A%d" % cur, "SL", "nI", "Mz"], ["Z0"], [(T.pZ0[:, 0:16], T.nI[:], Mz, True, 64)] + [(T.pZ0[:, 8 * h:8 * h + 8], A[cur][:, half(h)], T.SL[:], False, 64) for h in range(2)])
+        act(16, [], ["AT"], T.AT[:], T.pZ0[:, 0:16], Af.Copy, b=["Z0"])
+        ho = (n - 1) // 2
+        tag[0] = "xr"
+        if n == 6:
+            tag[0] = "at"
+            shift(V6A, 256, [], ["V%d" % n], T["V%d" % n][:], pv, 2048.0, b=["Z1"])
+            send(n - 1, 128, ["V%d" % n], ["lv%d" % n], T["lv%d" % n][:], T["V%d" % n][:])
+        elif cur == 0:
+            tag[0] = "at"
+            send(n - 1, 64, ["XR%d" % cur], ["lv%d" % n], T["lv%d" % n][:], XR[cur][:])
         for k in range(8):
-            kp = (k * ZO) % 8; z = k % 2
-            two = [(2 * kp + x, pZ[z][:, 256 * x:256 * x + 256]) for x in range(2)]
-            mm(["XL0", "XL1", "XR"], ["Z%d" % z], [(o, XL[kz % 2][32 * (kz % 8 // 2):32 * (kz % 8 // 2) + 32, 128 * (kz // 8):128 * (kz // 8) + 128], T.XR[32 * (kz % 8 // 2):32 * (kz % 8 // 2) + 32, :], True, 256) for kz, o in two])
+            tag[0] = "t%d" % k; bk = BANKS[2 * k:2 * k + 2]
+            lo = 0 if bk[0] == "Z" else 512 * int(bk[1])
+            two = [(2 * k + x, T["p" + (bk if bk[0] == "Z" else bk[0])][:, lo + 256 * x:lo + 256 * x + 256]) for x in range(2)]
+            mm(["XL0", "XL1", "XR%d" % cur], [bk], [(o, XL[kz % 2][32 * (kz % 8 // 2):32 * (kz % 8 // 2) + 32, half(kz // 8)], XR[cur][32 * (kz % 8 // 2):32 * (kz % 8 // 2) + 32, :], True, 256) for kz, o in two])
             for kz, o in two:
                 if kz < 16 - NZD:
-                    act(280, ["kb"], ["cn%d" % kz, "jk%d" % kz], T.junk[:, 256 * kz:256 * kz + 256], o, Af.Relu, bias=T.tn[:, 32 + kz:33 + kz], scale=-1.0, b=["Z%d" % z], acc=T.cnt[:, kz:kz + 1])
+                    act(280, ["kb%d" % (kz // 8)], ["cn%d" % kz, "jk%d" % kz], T.junk[:, 256 * kz:256 * kz + 256], o, Af.Relu, bias=T.tn[:, 32 + kz:33 + kz], scale=-1.0, b=[bk], acc=T.cnt[:, kz:kz + 1])
                 else:
-                    v(256, [], ["mn%d" % kz], lambda q, o=o, kz=kz: q.tensor_reduce(T.tn[:, 128 + kz:129 + kz], o, AxisListType.X, Al.min), ["Z%d" % z])
+                    v(256, [], ["mn%d" % kz], lambda q, o=o, kz=kz: q.tensor_reduce(T.tn[:, 64 + kz:65 + kz], o, AxisListType.X, Al.min), [bk])
+        tag[0] = "win"
         if NZD:
-            tt(16, ["kb"] + ["mn%d" % k for k in range(16 - NZD, 16)], ["cn%d" % k for k in range(16 - NZD, 16)], T.cnt[:, 16 - NZD:16], T.tn[:, 48 - NZD:48], T.tn[:, 144 - NZD:144], Al.subtract)
-        tt(16, ["dl"] + ["cn%d" % k for k in range(16)], ["z"], tn(9), tn(4), T.cnt[:], Al.subtract)
-        ts(16, ["z"], ["wn"], tn(6), tn(9), 0.0, None, Al.is_gt)
-        tt(16, ["wn", "wd"], ["t11"], tn(11), tn(6), tn(7), Al.mult)
-        tt(400, ["t11", "offG", "MK"], ["Wn"], T.Wn[:], tn(11).indirect(T.offG[:]), T.MK[:], Al.mult)
+            tt(16, ["kb0", "kb1"] + ["mn%d" % k for k in range(16 - NZD, 16)], ["cn%d" % k for k in range(16 - NZD, 16)], T.cnt[:, 16 - NZD:16], T.tn[:, 48 - NZD:48], T.tn[:, 80 - NZD:80], Al.subtract)
+        tt(16, ["AT"] + ["cn%d" % k for k in range(16)], ["wn"], tn(1), T.AT[:], T.cnt[:], Al.is_gt)
+        tt(256 * GC, ["wn", "offG", "MK"], ["Wn"], T.Wn[:], tn(1).indirect(T.offG[:]), T.MK[:], Al.mult)
         if n < 6:
-            ts(16, ["z"], ["t10"], tn(10), tn(9), 0.0, 2.0, Al.max, Al.add)
-            tt(16, ["t10", "m"], ["m"], m, tn(10), m, Al.add)
-        mm(["Wn", "OH", "If", "DUM"], ["Z0"], [(T.pZ0[:, 0:16], T.If[:], T.DUM[:], True, 256)] + [(T.pZ0[:, 8 * h:8 * h + 8], T.Wn[:, 128 * h:128 * h + 128], T.OH[:], False, 256) for h in range(2)])
-        cp(16, [], ["oS%d" % cur], offS[cur][:], T.pZ0[:, 0:16], b=["Z0"])
+            tag[0] = "len"
+            tt(16, ["wn", "AT"], ["z"], tn(0), tn(1), T.AT[:], Al.mult)
+            if PV & 1:
+                mm(["z", "Mz", "If", "Ib"], [LB], [(lb, T.If[:], tn(0), True, 256), (lb, T.Ib[:], Mz, False, 64)])
+                lengths(2.0, lb, [], [LB])
+            else:
+                tt(16, ["z", "Mz"], ["mx"], tn(6), tn(0), Mz, Al.add)
+                lengths(2.0, tn(6), ["mx"], [])
+            if n == 1:
+                weights(1, "ncw")
+        tag[0] = "list"
+        mm(["Wn", "OHb", "If", "DUM"], ["Z0"], [(T.pZ0[:, 0:16], T.If[:], T.DUM[:], True, 256)] + [(T.pZ0[:, 8 * h:8 * h + 8], T.Wn[:, half(h)], T.OHb[:], False, 64) for h in range(2)])
+        tt(16, ["wj"], ["t9"], tn(9), T.pZ0[:, 0:16], T.wj[:], Al.max, b=["Z0"])
+        cp(16, ["t9"], ["oS%d" % cur], offS[cur][:], tn(9))
+        land = T["land%d" % ho]
         if cur == 1:
-            ho = n // 2
-            cp(1000, ["oS1", "V1"], tabk(tb), tab[tb][:].indirect(offS[1][:]), V[1][:])
+            tag[0] = "put"
+            cp(1000, ["oS1", "XR1"], tabk(tb), tab[tb][:].indirect(offS[1][:]), XR[1][:])
             for q in range(3):
                 dma("s", 128, tabk(tb), ["cmp%d" % q], T.cmp[:, 256 * q:256 * q + 256], tab[tb][q:128:16, 0:4096])
-            send(3 * ho, 384, ["cmp0", "cmp1", "cmp2"], ["land%d" % ho], T["land%d" % ho][:], T.cmp[:])
-            unpack(T["land%d" % ho], ["land%d" % ho], 1 - tb)
+            tag[0] = "ring"
+            for q in range(3):
+                sl = slice(256 * q, 256 * q + 256); key = "land%d.%d" % (ho, q)
+                send(6 + 3 * ho + q, 128, ["cmp%d" % q], [key], land[:, sl], T.cmp[:, sl])
+            if n < 5:
+                unpack(land, "land%d." % ho + "%d", 1 - tb)
         else:
-            ho = n // 2 - 1
-            send(3 * ho + 2, 4, ["oS0"], ["lo%d" % ho], T["lo%d" % ho][:], offS[0][:])
-            cp(1000, ["lo%d" % ho, "lv%d" % ho], tabk(1 - tb), tab[1 - tb][:].indirect(T["lo%d" % ho][:]), T["lv%d" % ho][:])
-        addP(None)
-        addP(2)
+            send(n - 2, 4, ["oS0"], ["lo%d" % n], T["lo%d" % n][:], offS[0][:])
+            tag[0] = "ring"
+            if n == 6:
+                act(768, ["land2.0", "land2.1", "land2.2"], ["cmq0", "cmq1", "cmq2"], T.cmq[:], T.land2[:], Af.Identity, bias=2048.0)
+                unpack(T.cmq, "cmq%d", 1 - tb)
+            tag[0] = "put"
+            cp(1000, ["lo%d" % n, "lv%d" % n], tabk(1 - tb), tab[1 - tb][:].indirect(T["lo%d" % n][:]), T["lv%d" % n][:])
+        keys = n < 6
+        run, rk = (G[2], "G2.%d") if n == 1 else (T.XA, "XA.%d")
+        fused = n in FU
+
+        def again():
+            for s in range(4):
+                tag[0] = ("fus%d" if fused else "out%d") % s; sl = slice(512 * s, 512 * s + 512)
+                if fused:
+                    tt(512, ["G0.%d" % s], [rk % s], run[:, sl], Pb(s), G[0][:, sl], Al.add, b=["P%d" % s])
+                elif n == RH + 1:
+                    tt(512, ["y1.%d" % s], [rk % s], run[:, sl], Pb(s), T.y1[:, sl], Al.subtract, b=["P%d" % s])
+                elif 1 < n < 6:
+                    cp(512, [], [rk % s], run[:, sl], Pb(s), b=["P%d" % s])
+                tag[0] = ("add0%d" if fused else "run%d") % s
+                mm([rk % s, "Ib"], ["P%d" % s], [(Pb(s), T.Ib[:], run[:, sl], True, 512)])
+                if n == 6:
+                    mm(["G0.%d" % s, "G1.%d" % s], ["P%d" % s], [(Pb(s), T.Ib[:], G[x][:, sl], False, 512) for x in range(5 in FU, 2)])
+                if n in (RH, 6):
+                    tag[0] = "sub"
+                    mm(["ones", "CKP"], ["P%d" % s], [(Pb(s), T.ones[0:32, :], T.CKP[0:32, :], False, 512)])
+        if not fused:
+            again()
         for q in range(2):
+            win, wr = (T.Hw[:, 0:4096], Hr) if n == 1 and q < M1 else (T.Hw[:], Hxr)
             for h in range(2):
-                keys = q == 1 and n < 6
                 if h == 0:
                     kp = at[0]; k = (kp + 1) % 3 if kp < 3 or n == 1 else 0; at[0] = k
-                    new, nk = X[k], allp("X%d" % k)
-                    const(h, 0 if keys else 128, 256)
-                    tr(h, X[kp], allp("X%d" % kp), 128, 256, RR[:, 16:24])
+                    new, nk = X[k], "X%d." % k + "%d"
                 else:
-                    kp, k = None, q
-                    new, nk = G[k], allp("G%d" % k)
-                    const(h, 128, 256)
-                gather(h, win, wr, offU[q], ["oU%d.%d" % (q, h)], k, kp)
-                if keys and h == 0:
-                    tr(h, new, nk, 0, 256, RR[:, 0:16])
-                else:
-                    tr(h, new, nk, 128, 256, RR[:, 8:16])
-                    escopy(h, keys)
-                if h == 1:
-                    addP(k)
+                    kp, k = None, q + (3 if n == 6 else 0)
+                    new, nk = G[k], "G%d." % k + "%d"
+                tag[0] = "open%d%d" % (q, h)
+                lanes = LL >> h & 1; both = h == 1 and keys and not fused
                 if q == 0:
-                    nterms(h, [("D01", cur)], True)
-                    nstage(h, 4096, T.offU1, "oU1.%d" % h, n > 1)
-                    continue
-                for s in range(4 if h else 2):
-                    if h == 0:
-                        sl = slice(1024 * s, 1024 * s + 1024)
-                        ts(512, nk[s * NP // 2:(s + 1) * NP // 2], ["y0.%d" % s], T.y0[:, sl], new[:, sl], -49279.5, None, Al.add)
-                        continue
-                    sl = slice(512 * s, 512 * s + 512)
-                    if s < YV:
-                        ts(512, [], ["y1.%d" % s], T.y1[:, sl], Pb(s), -127.5, None, Al.add, b=["P%d" % s])
+                    o = pT[:, U0[h]:U0[h] + 128]
+                    if h == 0 and n != 4:
+                        lst = [(o, ES[:, 384:512], T.If[:], not lanes, 512)]
                     else:
-                        act(512, [], ["y1.%d" % s], T.y1[:, sl], Pb(s), Af.Identity, bias=-127.5, b=["P%d" % s])
-                    tt(512, ["y1.%d" % s], ["G2.%d" % (s * NP // 4)], T.G2[:, sl], Pb(s), T.y1[:, sl], Al.subtract, b=["P%d" % s])
-                if keys and h == 0:
-                    tr(h, T.y0, ["y0.0", "y0.1"], 0, 128, RR[:, 24:32])
-                    escopy(h, True)
-                elif keys:
-                    const(h, 0, 128)
-                    tr(h, G[2], allp("G2"), 0, 128, RR[:, 0:8])
-                if n == 3 and h == 0:
-                    at[0] = 3
-                    reduce256(new, "X%d." % k + "%d", X[3], lambda bk: ["X3.%d" % (bk * NP // 4)], RA)
+                        lst = [(o, T.ones[0:32, :], T.CK[0:32, 0:128], not lanes, 128)] if h == 0 or not lanes else []
+                    lst += [(o, T.D01[:], A[cur][:, half(h)], False, 128)]
+                    if not lanes:
+                        mm(CKr + ["ES0", "If", "D01", "A%d" % cur], ["T%d" % h], lst)
+                        if h == 0 and n == 4:
+                            direct(0, X[3], "X3.%d", 1)
+                    elif h == 0:
+                        mm(CKr, ["T0"], [(pT[:, 128:256], T.CK[0:32, 256:384], T.CK[0:32, 0:128], True, 128)])
+                    else:
+                        const(1, 512, 256, 256, False)
+                    gather(h, NPQ[0], win, wr, offU[0], ["oU0.%d" % h], k, kp, "g0")
+                    if lanes:
+                        tag[0] = "d%d0" % h
+                        tr(h, new, allp(nk[:2]), 512 if both else E0[h], 2 if both else 1, 16 if both else 0)
+                        m = 256 if both else 128; lo = 512 if both else E0[h]; e = T.E2[:, 256 * h + m - 128:256 * h + m]
+                        shift(E2A >> h & 1, m, [], ["E2%d" % h], T.E2[:, 256 * h:256 * h + m], pT[:, lo:lo + m], 0.0, b=["T%d" % h])
+                        tag[0] = "d%d1" % h
+                        mm(CKr + ["ES0", "If", "D01", "A%d" % cur, "E2%d" % h], ["T%d" % h], [(o, e, T.If[:], True, 512)] + lst)
+                        if h == 0 and n == 4:
+                            direct(0, X[3], "X3.%d", 1)
+                    else:
+                        direct(h, new, nk, 0, "g0")
+                    tag[0] = "off%d" % h
+                    nstage(h, 8192, T.offU1, "oU1.%d" % h, n > 1 or M1 < 2)
+                    if h and fused:
+                        again()
+                    elif h:
+                        addP(new, nk, 0)
+                    continue
+                lst = [(pT[:, 128 + 384 * h:512 + 256 * h], T.ones[0:64, :], T.CK[0:64, 256 * h:384 + 128 * h], True, 384 - 128 * h),
+                       (pT[:, E0[h]:E0[h] + 128], A[cur][:, half(h)], T.Dm1[:], False, 128)]
+                if h == 0 and lanes:
+                    lst += [(pT[:, 128:256], T.nIf[:], T.E2[:, 0:128], False, 512)]
+                elif both and lanes:
+                    lst += [(pT[:, 512:640], T.If[:], T.E2[:, 256:384], False, 512)]
+                mm(CKr + ["A%d" % cur, "Dm1", "If", "nIf", "E2%d" % h], ["T%d" % h], lst)
+                if h == 0 and not lanes:
+                    tr(0, X[kp], allp("X%d" % kp), 128, 1, 8)
+                elif h and keys:
+                    tag[0] = "trr"
+                    tr(1, run, allp(rk[:2]), 512, 1, 16)
+                    tag[0] = "trg"
+                    if both and not lanes:
+                        tr(1, G[0], allp("G0"), 512, 1, 16)
+                gather(h, NPQ[1], win, wr, offU[1], ["oU1.%d" % h], k, kp, "g1")
+                if h == 0:
+                    tag[0] = "tr0"
+                    tr(0, new, allp(nk[:2]), 128, 3 if keys else 1, 0)
+                    tag[0] = "y0"
+                    for s in range(NY0):
+                        tag[0] = "y0%d" % s
+                        m = 2048 // NY0; ks = range(4 * s // NY0, 4 * (s + 1) // NY0)
+                        ts(m // 2, [nk % x for x in ks], ["y0.%d" % x for x in ks], T.y0[:, m * s:m * s + m], new[:, m * s:m * s + m], -YO - 127.5, None, Al.add)
+                else:
+                    addP(new, nk, 1)
+                    tag[0] = "tr1"
+                    if keys:
+                        tr(1, new, allp("G1"), 512, 2, 16)
+                    else:
+                        tr(1, new, allp(nk[:2]), 640, 1, 0)
+                    for s in range(4):
+                        tag[0] = "y1%d" % s
+                        shift(s >= YV, 512, [], ["y1.%d" % s], T.y1[:, 512 * s:512 * s + 512], Pb(s), -127.5 - (0 if n in (RH, 6) else YO), b=["P%d" % s])
+                tag[0] = "key%d" % h
+                if keys:
+                    tr(h, T["y%d" % h], allp("y%d" % h), K0[h], 1, 32, True)
+                tag[0] = "es%d" % h
+                if h == 0 or n == 6:
+                    escopy(h)
+                tag[0] = "end%d" % h
                 if n == 6:
-                    nterms(h, [("Dm1", cur)], True)
-                    nstage(h, 2048, T.yi, "yi%d" % h, False)
                     if h == 0:
-                        reduce256(new, "X%d." % k + "%d", T.fo, lambda bk: ["fo%d" % bk], RF)
+                        reduce256(new, nk, T.fo, "fo%d", RF)
+                    tag[0] = "img%d" % h
+                    turned(h)
+                    nstage(h, 2048, T.yi, "yi%d" % h, False)
+                    if h == 1:
+                        for s in range(4):
+                            tag[0] = "f%d" % s
+                            tt(512, ["y1.%d" % s], ["G2.%d" % s], T.G2[:, 512 * s:512 * s + 512], Pb(s), T.y1[:, 512 * s:512 * s + 512], Al.subtract, b=["P%d" % s])
+        arrange(first, (LAST if n == 6 else STEP if cur else EVEN).split())
+        for o in ops[first:]:
+            o["step"] = n
     dma("s", 128, tabk(1), [], T.yent[:, 0:4096], T.tab1[0:128:16, 0:4096])
     dma("s", 128, tabk(1), [], T.yent[:, 4096:8192], T.tab1[1:128:16, 0:4096])
     dma("s", 128, tabk(1), [], T.yelen[:], T.tab1[2:128:16, 0:4096])
     dma("s", 128, ["yi0", "yi1"], [], T.yimg[:], T.yi[:])
     for k in range(8):
         dma("s", 128, ["fo%d" % k if k < 4 else "G2.%d" % (k - 4)], [], T.yf[:, 512 * k:512 * k + 512], (T.fo if k < 4 else T.G2)[:, 512 * (k % 4):512 * (k % 4) + 512])
+    for o in ops:
+        for j, x in enumerate(o.get("mm", [])):
+            if not x[3] and (OPEN or j):
+                tail[o["b"][0]][5] = False
+            tail[o["b"][0]] = x
     return ops, nout
 
 
@@ -485,16 +651,24 @@ def schedule(ops):
     for n in range(len(ops) - 1, -1, -1):
         pr[n] = ops[n]["t"] + ops[n]["lat"] + SY + max([pr[s] for s in succ[n]] + [0.0])
     for n, o in enumerate(ops):
-        if "T1" in o["b"] or any(k[0] == "G" or k in ("wi1", "wj1", "Wz1", "A0.1", "A1.1", "uj1") or k[:2] == "y1" for k in o["w"]):
-            pr[n] += BIAS
-        if "Z0" in o["b"] or "Z1" in o["b"] or any(k[:2] in ("XL", "cn", "wn", "t1", "Wn", "z", "oS") for k in o["w"]):
-            pr[n] += WB
-        pr[n] += CB.get(o["e"] + (o["w"] + o["b"] + [""])[0][:3], 0.0)
-    left = [len(o["dep"]) for o in ops]; rdy = [0.0] * len(ops); free = {}
+        k = (o["w"] + o["b"] + [""])[0]
+        if o["tag"]:
+            pr[n] = -n
+        elif k in FIRST:
+            pr[n] = 1000 - FIRST.index(k)
+        elif k in LATE:
+            pr[n] = pr[n] / 1000 - [x["tag"] for x in ops].index("window")
+    left = [len(o["dep"]) for o in ops]; last = {}
+    for n, o in enumerate(ops):
+        if o.get("step", 0) >= STRICT and o["e"] != "x":
+            if o["e"] in last and last[o["e"]] not in o["dep"]:
+                succ[last[o["e"]]].append(n); left[n] += 1
+            last[o["e"]] = n
+    rdy = [0.0] * len(ops); free = {}
     ready = [n for n in range(len(ops)) if left[n] == 0]; order = []; end = 0.0
     while ready:
         best = min(ready, key=lambda n: (max(rdy[n], free.get(ops[n]["e"], 0.0)), -pr[n], n))
-        e0 = ops[best]["e"]; t0 = max(rdy[best], free.get(e0, 0.0)); d0 = ops[best]["t"]; p0 = pr[best] + d0
+        e0 = ops[best]["e"]; t0 = max(rdy[best], free.get(e0, 0.0)); d0 = ops[best]["t"]; p0 = pr[best]
         for n in ready:
             if ops[n]["e"] == e0 and rdy[n] < t0 + LOOK * d0 and pr[n] > p0:
                 best = n; p0 = pr[n]
@@ -504,7 +678,7 @@ def schedule(ops):
             free[e0] = st + o["t"]
         fin = st + o["t"] + o["lat"]; end = max(end, fin); order.append(best)
         for s in succ[best]:
-            rdy[s] = max(rdy[s], fin + (0.0 if e0 == ops[s]["e"] and (e0 == "p" or not ops[s]["dep"][best]) else SY))
+            rdy[s] = max(rdy[s], fin + (0.0 if e0 == ops[s]["e"] and (e0 == "p" or not ops[s]["dep"].get(best)) else SY))
             left[s] -= 1
             if left[s] == 0:
                 ready.append(s)

@@ -1,56 +1,48 @@
+import math
+import numpy
 from concourse.mybir import AluOpType as Al, AxisListType, ActivationFunctionType as Af
 
 F, B, H16, I, U = "float32", "bfloat16", "float16", "int32", "uint16"
-NPQ = (2, 4)
-NZD = 4
-ZO = 7
-YV, NY0 = 1, 2
-RA, RF = 4, 4
-BA = 7
-NH, HA = 8, 2
-ESA = 3
-RH = 3
-UN, V6A, CMQ = 6, 1, "cn11"
-LL, E2A, FU, STRICT = 0, 3, (2, 3, 5), 2
-M1 = 2
-OPEN = True
-CV, CA, CY, CP, CQ, SY, GC = 0.05, 0.065, 0.00083, 0.00047, 0.04, 0.07, 1.55
-LOOK = 0.3
-BANKS = "Z0Z1Z0Z1Z0Z1T1T0"
-FIRST = ("tci imgi tw0 tw1 pi0 i16 G8 pi1 cf cp M16 SA0 SA P2 P3 P0 P4 ccw cg16 OH WD0 WD1 CK ones CKa CKb CKc tch offI DL Z0 ui0 uj0 offK "
-         "bits0 bits1 bits2 bits3 bits4 bits5 bits6 bits7 bits8 bits9 cncw RR0 RR1 RR2 RR3 RR4 Ib CKd tf0 tf1 tf2 tf3 If bits10 bits11 bitt11 bits12 bitt12").split()
-LATE = "mx cj4 cs01 cb2 S01 cb J3 cb1 cs1 cb0 cs0 DB JB mr WD2 kb0 kb1 DUM OHb Dm1 nI nIf Mz cp0 cp1 Mj0 Mj1".split()
-STEP = ("run3 chain window xl open00 run2 g010 xr open01 run1 g011 g000 d00 d10 g001 run0 at d11 off1 t0 d01 t4 t6 off0 t1 t2 t7 t5 g111 open10 end1 t3 sub g110 g100 g103 g112 add03 win "
-        "add10 es1 g102 g101 tr0 add12 add11 y0 add01 open11 add00 g113 add13 y10 y11 y13 key0 add02 es0 trg tr1 y12 key1 put len end0")
-EVEN = ("chain open01 xl g010 run2 g011 xr g000 open00 g001 d00 at d01 d10 run3 t4 t1 d11 t0 off1 sub off0 end1 t6 t7 window t5 t2 t3 run0 run1 add03 g100 open11 win g111 open10 add00 "
-        "g112 g110 add02 g113 g102 g101 trg g103 y0 add10 end0 add01 add13 y13 key0 tr1 add11 tr0 y10 add12 y11 len es0 put y12 key1 es1")
-LAST = ("chain len xl xr open00 g000 g001 g010 open01 g011 d10 d11 run3 run1 window d00 at d01 off1 off0 g101 run0 t5 t0 t6 t3 t7 t4 g112 t1 run2 key1 t2 g111 g102 win g110 open10 add03 "
-        "add00 sub g103 put add01 g100 add11 y11 tr0 trg g113 key0 add12 add13 y13 es0 add02 open11 add10 y12 tr1 es1 y10 end1 y0 end0")
-STEP = "out0 chain point go1 go0 open00 pv out2 window g010 xl g011 out3 out1 run1 open01 run2 xr g000 at d00 d10 g001 d11 run0 t1 t4 run3 d01 t0 off0 sub off1 t6 t5 g103 t7 add01 g111 t2 open10 t3 add03 g110 g100 g112 win add12 g102 add11 g101 open11 add10 tr0 add00 y00 list trr g113 add13 fus3 y13 y01 trg y11 y10 tr1 put fus0 key0 fus2 fus1 ring es0 add02 y12 len key1"
-EVEN = "chain mod3 mod0 point mod2 mod1 pv go1 out2 g010 go0 xl run2 xr g000 open00 d00 at open01 out3 g001 d10 d01 g011 window run3 d11 off1 t0 sub t4 t6 off0 t1 open11 out1 out0 t7 t3 t2 t5 trr g111 run0 add03 open10 g100 add02 g110 win list run1 g113 g112 g101 trg g102 g103 add13 add10 y00 y01 add12 y12 add01 tr1 put add00 y10 add11 y13 fus1 y11 fus3 len key0 tr0 es0 ring fus2 fus0 key1"
-LAST = "chain point go1 g010 pv run1 xl go0 open01 g000 run2 xr run0 open00 g001 at t1 d00 t0 run3 g011 d01 off0 d10 t7 t4 t3 d11 t5 t2 off1 t6 win g100 list g110 g101 add00 open10 y00 add02 sub ring g112 g111 add11 mod0 g103 open11 add01 g102 g113 add03 add10 add12 y12 y10 mod1 y11 tr0 add13 y01 y13 put tr1 es0 img0 es1 f1 f2 f0 mod2 f3 img1 mod3"
-STEP = "chain out3 run3 pv point out0 go1 window out2 out1 g010 run0 xl go0 run1 open00 xr g000 g001 g011 d00 open01 at d10 d01 off0 t4 run2 t0 d11 t5 t1 sub t2 t7 off1 t6 g103 g110 t3 add10 g111 g100 win open10 g112 open11 g102 add02 list add11 trg fus0 add12 add01 trr add03 g113 g101 add00 add13 fus3 put fus1 y01 y11 fus2 y00 tr1 tr0 y13 key0 es0 y10 ring y12 key1 len"
-EVEN = "mod3 window out2 chain mod0 point mod1 pv go1 go0 xl out0 mod2 run0 xr out3 open00 open01 g010 g011 run3 run2 t0 g000 d00 t3 g001 d10 d01 t4 d11 at off1 t6 out1 fus1 sub off0 open11 t2 t7 t1 t5 g103 win trr fus3 list g110 run1 g100 g112 add03 open10 add12 g101 g113 g111 add10 add13 add11 add01 fus0 fus2 trg g102 add00 y11 y00 y01 put tr1 ring tr0 key0 add02 y13 y12 y10 key1 es0 len"
-LAST = "pv chain point go1 run1 run0 xl at go0 g000 g010 xr g011 open01 open00 g001 d00 t3 t2 d01 off0 t0 t5 add01 run3 d10 d11 off1 run2 g100 t7 t1 open10 g101 t4 t6 sub g110 ring win g112 g111 list y00 g103 g113 add02 add13 add12 open11 add00 add11 tr1 add10 y12 g102 y10 y11 tr0 mod1 add03 y01 mod0 f0 y13 f2 f1 es1 f3 img1 es0 mod2 mod3 img0 put"
-STEP = "out2 chain out3 pv point out1 window go1 g010 g011 go0 xl out0 xr t5 g000 open00 d00 g001 at t0 run0 open01 t2 d01 off0 d10 run3 run1 d11 off1 g103 t7 t1 t3 g110 run2 t4 t6 fus2 g100 sub win fus1 g101 add03 open10 add10 open11 trr g111 list g102 add02 tr0 g112 g113 add12 add13 tr1 add11 add00 y13 put y01 add01 y00 y12 y11 key0 y10 es0 trg len key1 fus0 fus3 ring"
-EVEN = "fus3 chain fus1 mod0 out0 out2 point go1 mod3 mod1 out3 pv xl g010 xr run3 mod2 at open01 go0 g000 open00 g011 t4 g001 d00 d01 t0 t1 d10 off0 out1 d11 off1 window t6 t7 open11 run0 t2 trg t3 g103 g101 t5 run2 g113 win sub g112 g110 fus0 list open10 g111 add13 fus2 ring add10 add03 g100 add00 g102 run1 add11 y13 add01 y11 add02 trr y00 y01 len y10 tr0 key0 put add12 y12 tr1 es0 key1"
-LAST = "chain pv point xl run0 at xr go0 g000 go1 g001 g010 open01 d10 run1 open00 t4 d00 d01 off0 g011 t3 t0 t5 run2 add01 d11 t7 t1 off1 t2 run3 g110 ring g112 g100 t6 sub g111 add11 add02 win list open10 add00 g101 add12 g113 y00 add10 g102 add13 g103 y12 open11 y10 tr0 y11 tr1 mod1 mod0 add03 y13 f3 y01 es1 f0 es0 img1 img0 f2 mod2 f1 put mod3"
-STRICT, FU, AU, BA = 9, (), 0, 8
-NZ, YS, BK, PS = (4, 4, 4), (1, 1, 1), (BANKS, BANKS, BANKS), 2
-LB, CI, PV = "Z0", [], 0
-STEP = "chain pv out3 point window go1 xl out0 run3 go0 xr g000 at open01 open00 out2 g010 g011 run0 d00 g001 t5 out1 d10 d11 run1 t0 t2 d01 off0 run2 t4 sub g102 off1 t6 t7 t3 g103 g110 add03 t1 g111 win list fus2 add02 fus0 g113 put ring g112 add12 g101 g100 open11 add13 y01 add11 open10 add10 trr add00 add01 tr1 y11 tr0 y00 fus3 len y12 y13 trg key0 y10 es0 key1 fus1"
-EVEN = "window mod3 chain point out3 mod0 mod1 pv go1 xl open01 mod2 xr at go0 fus1 open00 g000 g001 d00 out2 g010 g011 sub d10 run2 t4 run3 d01 t0 off0 out0 d11 off1 t1 t6 fus2 t7 t5 t2 t3 open11 fus3 g113 run0 g112 fus0 out1 g111 g101 add03 open10 g102 win add12 list add00 run1 trr g103 add11 add02 g110 add01 g100 add10 len y12 trg add13 y00 tr1 y01 put y10 y11 y13 key0 ring tr0 es0 key1"
-LAST = "chain point go0 pv run1 xl go1 xr open01 g010 run0 g000 open00 at t5 d10 t4 t3 add01 g001 run2 t1 g011 d00 d01 off0 d11 off1 add02 t2 t6 t0 t7 run3 ring g100 g101 open11 win g112 y00 sub list g103 add12 add00 g110 y12 g113 g111 g102 add11 add10 open10 mod1 tr1 add13 y10 mod0 y01 f0 add03 y13 put es1 tr0 y11 f1 es0 img0 img1 mod2 f3 mod3 f2"
-STEP = "out0 pv chain point go1 xl window xr open01 go0 run0 at g010 open00 sub g000 d00 g011 d10 out1 g001 d01 d11 off0 run1 off1 t1 t2 g110 out2 t3 fus1 out3 t0 fus0 fus3 t4 add00 t5 g111 t6 g113 t7 run3 add01 g100 win fus2 g103 add03 run2 g102 open11 g101 add02 y00 add13 g112 y13 add10 list y01 add11 trr open10 tr0 trg y11 add12 tr1 key0 y10 put y12 key1 ring es0 len"
-EVEN = "ring mod1 chain mod2 point go0 mod3 mod0 go1 pv xl xr g000 out0 run1 g001 g010 open00 window g011 out3 run3 fus1 open01 at d10 d00 fus3 t5 run0 d11 fus0 d01 t4 t2 off0 t7 add03 t0 g100 t3 off1 g102 g110 add00 trg out1 t6 open11 open10 fus2 add02 trr t1 win g113 g101 add01 g111 g112 add10 sub g103 add13 run2 add12 list tr0 add11 y00 y12 tr1 y01 out2 key0 y13 y10 len put es0 y11 key1"
-LAST = "run0 chain point go1 go0 pv xl xr g001 open00 open01 d01 g000 d00 g010 off0 g011 t0 run1 t7 run2 t4 g103 at d10 t3 t1 d11 run3 t2 off1 g111 t6 add11 t5 g110 g101 win g100 add02 y00 ring sub add10 add03 g113 add00 list g112 add01 add12 y12 open11 add13 mod0 y11 f1 g102 y13 f2 open10 put y01 mod3 tr1 es1 mod2 tr0 es0 img0 img1 y10 mod1 f0 f3"
-STEP = "chain point pv xl go1 open01 window out0 xr go0 open00 at g000 sub g010 d00 out1 d10 g001 g011 d11 t5 out3 out2 d01 t1 run0 t3 off1 fus0 off0 t2 run2 fus1 t0 g111 run1 run3 t4 t6 fus3 g110 t7 g100 g112 add00 g113 win fus2 add03 open11 add13 g101 g102 y00 g103 add02 y01 add10 y13 trr add01 trg add11 add12 tr1 list open10 tr0 y10 y11 put len key0 y12 es0 ring key1"
-EVEN = "chain mod0 run3 run1 point go0 mod1 mod3 mod2 g000 go1 pv xl xr ring open00 out3 g010 window at g011 out0 d00 g001 fus3 open01 d10 t4 t5 run0 d11 d01 off0 t3 off1 t7 fus1 t2 add03 out1 t1 t0 g112 g111 t6 fus0 g102 g100 g110 fus2 add01 open11 g113 trr open10 win add13 add02 add00 g103 g101 add12 sub add10 list tr0 add11 trg y00 y01 y12 put run2 y11 key0 tr1 y13 y10 es0 out2 key1 len"
-LAST = "chain pv point go0 xl xr open00 g001 t4 go1 g000 open01 g010 run0 d01 d10 at t5 d00 run1 t0 t3 run3 t1 off0 g011 d11 t7 t2 run2 add03 off1 g103 g111 add11 g100 g110 t6 g101 add00 g113 add10 ring y00 add02 win sub list add13 g112 add12 add01 open11 y11 y12 f1 open10 g102 mod0 y13 tr1 es1 y01 mod3 tr0 y10 mod2 f2 f3 img1 put es0 img0 mod1 f0"
-FU, RH, YS = (2, 3, 4), 4, (0, 0, 1)
-STEP = STEP.replace(" window", "").replace(" xl", " window xl")
+P = {
+    "g": ((2, 2), (3, 4)),
+    "y": (2, 2),
+    "zv": (0, 3, 4),
+    "zo": ("01234567", "01723645", "07162534"),
+    "zb": ("123010101", "101230123", "101230123"),
+    "pb": ("2323", "0123", "01230123"),
+    "xa": (0, 2, 0),
+    "xo": "a", "au": "gob offb",
+    "look": "v",
+    "ha": "037",
+    "ba": 8,
+    "fv": 0,
+    "rf": 4,
+    "m1": 2,
+}
+CV, CA, CY, CP, CQ, SY, SX, GC = 0.05, 0.065, 0.00083, 0.00043, 0.03, 0.05, 0.22, 1.45
+RATE = 350.0
+WIDTH, SWEEPS, MOVES, HEAT, SEED = 16.0, 2, 12000, 0.15, 1
+START = {
+    "s": "tci tw0 imgi cI0 cI1 cI2 ow0 ow1 ow2",
+    "g": "pi0 OH0 OH1 OH SA Ib CKd tf0 tf1 tf2 tf3 Dp0 Dp1 D01 SL G8 JB0 S01 Dm1 nI sez0 i16 DUM CKP0 CKP",
+    "v": "SA0 ones pi1 P2 M16 CK WD0 P0 owni seg0 CKc seg offI bits9 bits10 bits11 bitt11 bits12 bitt12 mones Mz0 ui0 uj0 offK0 ia ui1 uj1 offK1 ia2 H1 H2 1:scan 1:scan2 1:scan3 1:scan4 H4 "
+         "1:scan5 1:scan6 1:scan7 1:look H5 1:gob 1:gob2 1:gob3 H6 1:goa 1:goa2 1:goa3 1:g0a",
+    "a": "tw1 DL bits0 bits1 ccw bits2 WD bits3 cncw bits4 bits5 tch bits6 bits7 bits8 RR0 RR1 RR2 If imgf MK4 MK5 MK6 MK7 MK8 ib ib2 esb cmp0 H0 esa H3 H0.2 H7 H3.2 H7.2 1:xl 1:g0b",
+    "p": "Kt0 Kt1 Kt0.2 Kt0.3 Kt1.2 Kt1.3 Kw0 Kw1 ka kb ka2 kb2 H0 1:tub H3 1:scan 1:tua H7 1:gob 1:goa"}
+END = {}
+ROUND = {
+    "v": "e:scan e:scan2 o:list+ e:scan3 o:list2+ e:scan4 o:put+ e:scan5 e:scan6 e:scan7 e:look e:goa e:g0a e:g0a2 e:z7 e:offa e:g1a e:z5 e:z6 e:win e:g1a3 e:win2 e:g1a2 e:win3 e:x2 e:ya "
+         "e:list e:x e:list2 e:ya2 e:yb2 e:yb o:scan o:scan2 o:scan3 o:scan4 e:put o:scan5 o:scan6 o:scan7 o:look o:goa o:g0a o:g0a2 o:offa o:g1a o:g1a2 o:g1a3 o:ya o:x2 o:x o:ya2 o:yb "
+         "o:x3 o:x4 o:yb2 o:win o:win2",
+    "a": "o:len2+ o:own+ o:own2+ e:xl e:xo e:gob e:xr e:g0b e:z2 e:z0 e:z1 e:z0.2 e:z1.2 e:z2.2 e:g0b2 e:z3 e:z4 e:z4.2 e:z3.2 e:offb e:g1b4 e:g1b2 e:g1b3 e:g1b e:x2 e:x e:esa e:len e:esb "
+         "e:len2 e:own e:own2 o:xl o:xo o:gob o:xr o:g0b o:g0b2 o:z1 o:z0 o:z0.2 o:z3 o:z2 o:offb o:z2.2 o:z3.2 o:z1.2 o:g1b2 o:z4 o:g1b o:z4.2 o:g1b3 o:z5 o:z5.2 o:g1b4 o:z6 o:z6.2 o:z7 "
+         "o:z7.2 o:esa o:esb o:len",
+    "p": "o:z6+ o:p4+ o:p3+ o:z7+ o:keya+ o:trb+ o:trx2+ o:keyb+ o:list+ o:len+ e:tub e:scan e:pv e:tua e:goa e:gob e:xr e:oqa e:opa e:opb e:z0 e:z1 e:z2 e:da e:z7 e:db e:da2 e:z3 e:z6 e:z5 "
+         "e:z4 e:at e:db2 e:oqa2 e:p2 e:p4 e:p3 e:p e:list e:trx e:x2 e:oqb e:tra e:x e:trb e:keya e:trx2 e:keyb e:len o:pv o:tub o:scan o:tua o:gob o:goa o:xr o:opa o:at o:z0 o:z3 o:opb "
+         "o:z1 o:z2 o:db o:da o:da2 o:db2 o:oqa o:oqa2 o:oqb o:z4 o:p2 o:p o:trx o:tra o:z5"}
 MG = 12582912.0
 YO = 49152.0
+RC = -255.0 / 512
 
 
 def _sb(n, d):
@@ -58,36 +50,36 @@ def _sb(n, d):
 
 
 SCRATCH = {
-    "tw": _sb(4096, B), "Hw": _sb(16384, B), "bits": _sb(4096, B), "tab0": _sb(4480, F), "tab1": _sb(4480, F), "Xi": _sb(2048, B),
-    "X0": _sb(2048, H16), "X1": _sb(2048, H16), "X2": _sb(2048, H16), "G0": _sb(2048, B), "G1": _sb(2048, B), "G2": _sb(2048, B),
-    "y0": _sb(2048, B), "y1": _sb(2048, B), "fo": _sb(2048, B), "XA": _sb(2048, H16), "G3": _sb(2048, B), "G4": _sb(2048, B), "CKP": _sb(512, B),
+    "tw": _sb(4096, B), "Hw": _sb(16384, B), "bits": _sb(4096, B), "tab0": _sb(4480, F), "tab1": _sb(4480, F),
+    "X00": _sb(2048, H16), "X01": _sb(2048, H16), "X10": _sb(2048, H16), "X11": _sb(2048, H16), "M0": _sb(2048, H16), "M1": _sb(2048, B),
+    "G0": _sb(2048, B), "G1": _sb(2048, B), "y0": _sb(2048, B), "y1": _sb(2048, B), "fo": _sb(4096, B), "CKP": _sb(512, B),
     "imgi": _sb(256, I), "imgf": _sb(256, F), "offI": _sb(256, U), "tci": _sb(1024, I), "tch": _sb(1024, H16), "offK": _sb(256, U),
     "cmpI": _sb(768, I), "cmp": _sb(768, F), "cmq": _sb(768, F), "land0": _sb(768, F), "land1": _sb(768, F), "land2": _sb(768, F),
-    "lv1": _sb(256, H16), "lv2": _sb(256, H16), "lv3": _sb(256, H16), "lv4": _sb(256, H16), "lv5": _sb(256, F), "lv6": _sb(256, F), "V5": _sb(256, F),
-    "lo1": _sb(16, U), "lo2": _sb(16, U), "lo3": _sb(16, U), "lo4": _sb(16, U), "lo5": _sb(16, U), "lo6": _sb(16, U),
+    "lv2": _sb(256, H16), "lv4": _sb(256, H16), "lv6": _sb(256, F), "lo2": _sb(16, U), "lo4": _sb(16, U), "lo6": _sb(16, U),
     "owni": _sb(256, I), "A0": _sb(256, H16), "A1": _sb(256, H16), "V6": _sb(256, F), "XR0": _sb(256, H16), "XR1": _sb(256, H16), "XL0": _sb(256, B), "XL1": _sb(256, B),
-    "G8": _sb(8, F), "pi": _sb(8, I), "col": _sb(48, F), "POW": _sb(64, F), "i16": _sb(16, F), "M16": _sb(16, F), "SL": _sb(8, B), "NE": _sb(8, B), "WW": _sb(8, B), "DL": _sb(16, B),
-    "Ib": _sb(128, B), "If": _sb(128, F), "nI": _sb(128, B), "nIf": _sb(128, F), "E2": _sb(512, F), "ones": _sb(128, B),
-    "Dp0": _sb(128, B), "Dp1": _sb(128, B), "Dm1": _sb(128, B), "D01": _sb(128, B), "S01": _sb(128, B), "DB": _sb(128, B), "J3": _sb(128, B),
-    "WD": _sb(288, B), "SA": _sb(576, B), "RR": _sb(40, B), "CK": _sb(768, B), "seg": _sb(256, F), "JT": _sb(256, B), "JB": _sb(2, F), "DUM": _sb(16, F),
-    "ES": _sb(512, F), "Rm": _sb(256, I), "oi": _sb(16, I), "oj": _sb(16, I), "offW": _sb(16, U),
-    "wi": _sb(16, I), "wj": _sb(16, I), "Wz": _sb(256, F), "Wn": _sb(256, B), "MK": _sb(256, F), "ogi": _sb(16, I), "offG": _sb(16, U), "OH": _sb(8, F), "Mz": _sb(256, H16),
+    "G8": _sb(16, F), "pi": _sb(32, I), "col": _sb(48, F), "odb": _sb(2, B), "POW": _sb(64, F), "i16": _sb(16, F), "M16": _sb(16, F), "SL": _sb(8, B), "DL": _sb(16, B),
+    "Ib": _sb(128, B), "If": _sb(128, F), "nI": _sb(128, B), "ones": _sb(128, B), "mones": _sb(128, B),
+    "Dp0": _sb(128, B), "Dp1": _sb(128, B), "Dm1": _sb(128, B), "D01": _sb(128, B), "S01": _sb(128, B), "DB": _sb(128, B),
+    "WD": _sb(144, B), "SA": _sb(576, B), "RR": _sb(40, B), "CK": _sb(896, B), "seg": _sb(256, F), "sez": _sb(512, F), "JB": _sb(2, F), "DUM": _sb(16, F),
+    "ES": _sb(512, F), "Rm": _sb(256, I), "oj": _sb(16, I), "offW": _sb(16, U),
+    "wi": _sb(16, I), "wj": _sb(16, I), "Wz": _sb(256, F), "Wn": _sb(256, B), "MK": _sb(256, F), "MB": _sb(256, F), "offG": _sb(16, U), "OH": _sb(8, F), "Mz": _sb(256, H16),
     "offO": _sb(16, U), "offU0": _sb(256, U), "offU1": _sb(256, U), "offS0": _sb(16, U), "offS1": _sb(16, U),
-    "ui": _sb(256, I), "uj": _sb(256, I), "yi": _sb(256, F), "AT": _sb(16, F), "OHb": _sb(8, B), "tn": _sb(160, F), "cnt": _sb(16, F), "junk": _sb(4096, B),
-    "pP": ("psum", [128, 2048], F), "pT": ("psum", [128, 1024], F), "pZ0": ("psum", [128, 512], F), "pZ1": ("psum", [128, 512], F),
+    "ui": _sb(256, I), "uj": _sb(256, I), "yi": _sb(256, F), "OHb": _sb(8, B), "tn": _sb(64, F), "cnt": _sb(16, F), "junk": _sb(4096, B), "zs": _sb(4096, F),
+    "pT": ("psum", [128, 1536], F), "pS": ("psum", [128, 512], F), "pQ": ("psum", [128, 2048], F),
 }
 SEMAPHORES = ["cv", "ca", "cp", "cg"] + ["d%d" % k for k in range(90)] + ["r%d" % k for k in range(18)]
 
 
 def build(T, topo, core, rank):
-    ops = []; tail = {}; tag = [""]
+    ops = []; tag = ["", 0]
     n4 = len(T.cores)
     nxt, prv = T.cores[(rank + 1) % n4], T.cores[(rank - 1) % n4]
     rid, pid = topo.addr(nxt)[0], topo.addr(nxt)[1]
     nout, nin = len(topo.engines(core, nxt)), len(topo.engines(prv, core))
 
-    def op(e, t, r, w, fn, b=(), kind="c", lat=0.0, sem=None):
-        ops.append({"e": e, "t": t, "r": list(r), "w": list(w), "b": list(b), "fn": fn, "k": kind, "lat": lat, "sem": sem, "tag": tag[0]})
+    def op(e, t, r, w, fn, b=(), kind="c", lat=0.0, sem=None, kb=0.0):
+        ops.append({"e": e, "t": t, "r": list(r), "w": list(w), "b": list(b), "fn": fn, "k": kind, "lat": lat, "sem": sem, "kb": kb,
+                    "tag": tag[0] or (list(w) + list(b) + [""])[0], "step": tag[1]})
 
     def v(n, r, w, fn, b=()):
         op("v", CV + max(n, 64) * CY, r, w, fn, b)
@@ -103,18 +95,15 @@ def build(T, topo, core, rank):
             for o, l, x, s0, c, s1 in lst:
                 last = q.matmul(o, l, x, s0, s1)
             return last
-        op("p", CQ + sum(m[4] for m in lst) * CP, r, [], fn, b)
+        op("p", CQ + sum(m[4] for m in lst) * CP, r, [], fn, [b])
         ops[-1]["mm"] = lst
 
-    def arrange(start, order):
-        ops[start:] = sorted(ops[start:], key=lambda o: order.index(o["tag"]))
-
     def dma(e, kb, r, w, out, src):
-        op(e, 0.1, r, w, lambda q: q.dma_start(out, src), kind="d", lat=2.0 + kb / 200.0)
+        op(e, 0.1, r, w, lambda q: q.dma_start(out, src), kind="d", lat=1.3, kb=kb)
 
     def send(k, kb, r, w, dst, src):
         op("g", 0.3, r, ["snd%d" % k], lambda q, ls: q.remote_dma(dst, src, T.sem["r%d" % k], ls, pid, rid, topo.mask(core, nxt)), kind="s", lat=2.0 + kb / 80.0)
-        op("x", 0.0, ["snd%d" % k], w, None, kind="x", lat=0.5, sem=("r%d" % k, nin))
+        op("x", 0.0, ["snd%d" % k], w, None, kind="x", lat=0.3, sem=("r%d" % k, nin))
 
     def ts(n, r, w, out, in0, s1, s2, o0, o1=None, b=()):
         if o1 is None:
@@ -131,8 +120,11 @@ def build(T, topo, core, rank):
     def ms(n, w, out, c, r=()):
         v(n, r, w, lambda q: q.memset(out, c))
 
+    def scan(n, r, w, out, seg, x, b):
+        v(n, r, w, lambda q: q.tensor_tensor_scan(out, seg, x, 0.0, Al.add, Al.min), b)
+
     def act(n, r, w, out, x, f, bias=0.0, scale=1.0, b=(), acc=None):
-        op("a", CA + max(n, 64) * CY, r, w, lambda q: q.activation(out, x, f, bias=bias, scale=scale, accum_out=acc), b)
+        op("a", CA + max(n, 64) * CY + (0.02 if acc is not None else 0.0), r, w, lambda q: q.activation(out, x, f, bias=bias, scale=scale, accum_out=acc), b)
 
     def shift(scalar, n, r, w, out, x, add, b=()):
         plain = isinstance(add, float) and add == 0.0
@@ -152,42 +144,55 @@ def build(T, topo, core, rank):
     def sel(n, r, w, out, x, pat, cmp, fill, base, cm):
         gp(n, r, w, lambda q: q.affine_select(out, x, pat, cmp, fill, base, cm))
 
-    tab = [T.tab0, T.tab1]; X = [T.X0, T.X1, T.X2, T.Xi]; G = [T.G0, T.G1, T.G2, T.G3, T.G4]; A = [T.A0, T.A1]; XR = [T.XR0, T.XR1]; XL = [T.XL0, T.XL1]
-    pT = T.pT; pZ = [T.pZ0, T.pZ1]; ES = T.ES; offU = [T.offU0, T.offU1]; offS = [T.offS0, T.offS1]; RR = T.RR
-    U0, E0, K0, L0 = (0, 768), (128, 640), (384, 512), 896
-    EC = (256, 128)
-    allp = lambda s: ["%s.%d" % (s, k) for k in range(4)]
-    half = lambda h: slice(128 * h, 128 * h + 128)
+    def bank(k):
+        k = int(k)
+        return "Q%d" % k, T.pQ[:, 512 * k:512 * k + 512]
 
+    tab = [T.tab0, T.tab1]; A = [T.A0, T.A1]; XR = [T.XR0, T.XR1]; XL = [T.XL0, T.XL1]
+    pT = T.pT; pS = T.pS; ES = T.ES; offU = [T.offU0, T.offU1]; offS = [T.offS0, T.offS1]; RR = T.RR; CK = T.CK
+    half = lambda h: slice(128 * h, 128 * h + 128)
+    U0, E0, K0 = (640, 1024), (128, 1152), (384, 512)
+    UB, EB, KB = ("T1", "T2"), ("T0", "T2"), ("T0", "T1")
+    EC = (256, 128)
+    reg = lambda lo, n=128: pT[:, lo:lo + n]
+    blk = lambda nm, lo=0, hi=2048: ["%s.%d" % (nm, k) for k in range(lo // 256, hi // 256)]
+
+    def cuts(n, hi=2048):
+        return [(256 * (hi // 256 * i // n), 256 * (hi // 256 * (i + 1) // n)) for i in range(n)]
+
+    dma("s", 128, [], ["tci"], T.tci[0:32, :], T.turn[:])
     dma("s", 512, [], ["tw0"], T.tw[:, 0:2048], T.twist[:, 0:2048])
     dma("a", 512, [], ["tw1"], T.tw[:, 2048:4096], T.twist[:, 2048:4096])
     dma("s", 128, [], ["imgi"], T.imgi[:], T.img[:])
-    dma("a", 128, [], ["tci"], T.tci[0:32, :], T.turn[:])
     ms(256, ["owni"], T.owni[:], 0)
     for q in range(2):
-        dma("s", 128, CI, ["cI%d" % q], T.cmpI[:, 256 * q:256 * q + 256], T.ent[:, 4096 * q:4096 * q + 4096])
+        dma("s", 128, [], ["cI%d" % q], T.cmpI[:, 256 * q:256 * q + 256], T.ent[:, 4096 * q:4096 * q + 4096])
         dma("s", 8, ["owni"], ["ow%d" % q], T.owni[q:128:16, :], T.own[:, 256 * q:256 * q + 256])
-    dma("s", 128, CI, ["cI2"], T.cmpI[:, 512:768], T.elen[:])
+    dma("s", 128, [], ["cI2"], T.cmpI[:, 512:768], T.elen[:])
     dma("s", 8, ["owni"], ["ow2"], T.owni[2:128:16, :], T.olen[:])
 
-    iota(8, ["pi0"], T.pi[:, 0:1], [[0, 1]], 0, 1, False)
+    iota(16, ["pi0"], T.pi[:, 0:16], [[1, 16]], 128, -1, False)
     iota(16, ["i16"], T.i16[:], [[1, 16]], 0, 0)
-    iota(8, ["G8"], T.G8[:], [[16, 8]], 0, 0)
-    iota(128, ["ones"], T.ones[:], [[0, 128]], 1, 0)
+    iota(16, ["G8"], T.G8[:], [[128, 2], [0, 8]], 0, 1)
+    ms(64, ["ones"], T.ones[:], 1.0); ms(64, ["mones"], T.mones[:], -1.0)
     sel(128, ["ones"], ["Ib"], T.Ib[:], T.ones[:], [[-1, 128]], Al.is_equal, 0.0, 0, 1)
-    ms(384, ["CK"], T.CK[:], 0.0)
-    for nm, row, lo, x in (("CKa", 0, 0, -255.0 / 512), ("CKe", 0, 128, -255.0 / 512), ("CKb", 0, 384, -255.0 / 512), ("CKc", 32, 256, 4096 * YO)):
-        act(128, ["CK", "ones"], [nm], T.CK[row:row + 1, lo:lo + 128], T.ones[row:row + 1, :], Af.Identity, scale=x)
-    iota(256, ["CKd"], T.CK[0:1, 512:768], [[-128, 2], [1, 128]], 128, 0, r=["CK"])
-    CKr = ["CKa", "CKb", "CKc", "CKe", "ones"]
+    sel(128, ["mones"], ["nI"], T.nI[:], T.mones[:], [[-1, 128]], Al.is_equal, 0.0, 0, 1)
+    ms(448, ["CK"], CK[0:64, :], 0.0)
+    ms(64, ["CKc"], CK[32:33, 256:384], 4096 * YO, r=["CK"])
+    iota(256, ["CKd"], CK[0:1, 384:640], [[-128, 2], [1, 128]], 128, 0, r=["CK"])
+    ms(64, ["CKf"], CK[0:1, 640:768], 16 * YO, r=["CK"]); ms(64, ["CKe"], CK[32:33, 640:768], -YO / 256, r=["CKf"])
+    ms(64, ["CKg"], CK[0:1, 768:896], RC, r=["CK"])
     ms(288, ["SA0"], T.SA[0:32, :], 0.0)
     sel(36, ["SA0"], ["SA"], T.SA[0:32, 15:576:16], T.SA[0:32, 15:576:16], [[1, 4], [4, 9]], Al.not_equal, -1.0, 0, -1)
-    iota(2, ["JB0"], T.JB[:], [[128, 2]], 2047 * 256 - 12 * 2 ** 19, 1)
+    iota(2, ["JB0"], T.JB[:], [[128, 2]], -12 * 2 ** 19, 1)
     act(2, ["JB0"], ["JB"], T.JB[:], T.JB[:], Af.Identity, scale=4096.0)
     iota(16, ["DUM"], T.DUM[:], [[16, 16]], 4096, 1)
+    fv = P["fv"]; fg = (4096 - fv) // 4
     for k in range(4):
-        iota(1120, ["tf%d" % k], T.tab0[:, 1120 * k:1120 * k + 1120], [[0, 1120]], 0, 0)
-    fill = [["tf%d" % k for k in range(4)], ["tg%d" % k for k in range(8)]]
+        iota(fg, ["tf%d" % k], T.tab0[:, fg * k:fg * k + fg], [[0, fg]], 0, 0)
+    if fv:
+        ms(fv, ["tf4"], T.tab0[:, 4096 - fv:4096], 0.0)
+    fill = [["tf%d" % k for k in range(5)], ["tg%d" % k for k in range(8)]]
     names = {}
 
     def c(nm):
@@ -195,292 +200,264 @@ def build(T, topo, core, rank):
             names[nm] = len(names)
         return T.col[:, names[nm]:names[nm] + 1]
 
-    def cs(nm, src, s1, s2, o0, o1=None):
-        r = ["c" + x for x in (src, s1, s2) if isinstance(x, str)]
-        ts(1, r, ["c" + nm], c(nm), c(src), c(s1) if isinstance(s1, str) else s1, c(s2) if isinstance(s2, str) else s2, o0, o1)
-
-    def cl(nm, src, sc, bi):
-        act(1, ["c" + x for x in (src, sc, bi) if isinstance(x, str)], ["c" + nm], c(nm), c(src), Af.Identity,
-            bias=c(bi) if isinstance(bi, str) else bi, scale=c(sc) if isinstance(sc, str) else sc)
-    cp(1, ["pi0"], ["cp"], c("p"), T.pi[:, 0:1])
-    for k, (nm, sh, mk) in enumerate((("f", 0, 15), ("od", 4, 1))):
-        ts(1, ["pi0"], ["pi%d" % (k + 1)], T.pi[:, k + 1:k + 2], T.pi[:, 0:1], sh, mk, Al.arith_shift_right, Al.bitwise_and)
-        cp(1, ["pi%d" % (k + 1)], ["c" + nm], c(nm), T.pi[:, k + 1:k + 2])
-    ms(16, ["P2"], T.POW[:, 16:32], 2.0); ms(16, ["P3"], T.POW[:, 32:48], 0.0)
-    ts(16, ["i16", "cf"], ["M16"], T.M16[:], T.i16[:], c("f"), None, Al.is_equal)
-    v(16, ["P2", "P3"], ["P0"], lambda q: q.tensor_tensor_scan(T.POW[:, 0:16], T.POW[:, 16:32], T.POW[:, 32:48], 2.0 ** -13, Al.mult, Al.add))
-    tt(16, ["P0", "M16"], ["P4"], T.POW[:, 48:64], T.POW[:, 0:16], T.M16[:], Al.mult)
-    v(12, ["P4"], ["ccw"], lambda q: q.tensor_reduce(c("cw"), T.POW[:, 52:64], AxisListType.X, Al.add))
-    cl("ncw", "cw", -1.0, 0.0); cl("g16", "f", -1.0, "p")
-    ms(144, ["WD0"], T.WD[:], 0.0)
-    ts(8, ["G8", "cg16"], ["OH"], T.OH[:], T.G8[:], c("g16"), None, Al.is_equal)
-
-    def weights(k, nm):
-        act(8, ["OH", "c" + nm, "WD0"], ["WD%d" % (k + 1)], T.WD[:, 144 * k + 15:144 * k + 143:16], T.OH[:], Af.Identity, scale=c(nm))
-    weights(0, "cw")
-    cp(256, ["imgi"], ["offI"], T.offI[:], T.imgi[:]); cp(256, ["imgi"], ["imgf"], T.imgf[:], T.imgi[:])
+    ts(16, ["pi0"], ["pi1"], T.pi[:, 16:32], T.pi[:, 0:16], 15, None, Al.bitwise_and)
+    ts(16, ["pi1"], ["M16"], T.M16[:], T.pi[:, 16:32], 0, None, Al.is_equal)
+    ms(12, ["P2"], T.POW[:, 16:28], 0.5)
+    v(12, ["P2", "M16"], ["P0"], lambda q: q.tensor_tensor_scan(T.POW[:, 0:12], T.POW[:, 16:28], T.M16[:, 4:16], 0.0, Al.mult, Al.add))
+    act(1, ["P0"], ["ccw"], c("cw"), T.POW[:, 11:12], Af.Identity, scale=8.0)
+    act(1, ["P0"], ["cncw"], c("ncw"), T.POW[:, 11:12], Af.Identity, scale=-8.0)
+    ms(72, ["WD0"], T.WD[:], 0.0)
+    iota(8, ["OH0"], T.OH[:], [[0, 8]], 1, 0)
+    sel(8, ["OH0"], ["OH1"], T.OH[:], T.OH[:], [[-16, 8]], Al.is_ge, 0.0, 0, 1)
+    sel(8, ["OH1"], ["OH"], T.OH[:], T.OH[:], [[16, 8]], Al.is_ge, 0.0, 15, -1)
+    act(4, ["OH"], ["cod"], T.POW[:, 32:36], T.OH[:, 1:8:2], Af.Copy, acc=c("od"))
+    if P["xo"] == "v":
+        cp(1, ["cod"], ["odb"], T.odb[:, 0:1], c("od"))
+    act(8, ["OH", "ccw", "WD0"], ["WD"], T.WD[:, 15:143:16], T.OH[:], Af.Identity, scale=c("cw"))
+    cp(256, ["imgi"], ["offI"], T.offI[:], T.imgi[:]); act(256, ["imgi"], ["imgf"], T.imgf[:], T.imgi[:], Af.Copy)
     for k, w in enumerate(("cw", "ncw", -256.0, "cw", 256.0)):
         act(8, ["OH", "ccw", "cncw"], ["RR%d" % k], RR[:, 8 * k:8 * k + 8], T.OH[:], Af.Identity, scale=c(w) if isinstance(w, str) else w)
-    RRr = ["RR%d" % k for k in range(5)]
-    cs("dv", "f", 4, -2.0 / 4096, Al.is_ge, Al.mult)
-    for nm, k, sc, bi in (("s01", 0, 1.0, T.M16[:, 1:2]), ("j4", 3, 4096.0, 0.0), ("b2", 2, 2.0 ** 20, c("j4"))):
+    act(12, ["M16"], ["cdv"], T.POW[:, 36:48], T.M16[:, 4:16], Af.Identity, scale=-2.0 / 4096, acc=c("dv"))
+    for nm, k, sc, bi in (("j4", 3, 4096.0, 0.0), ("b2", 2, 2.0 ** 20, c("j4"))):
         act(1, ["M16", "cj4"], ["c" + nm], c(nm), T.M16[:, k:k + 1], Af.Identity, bias=bi, scale=sc)
-    cs("b", "dv", 2.0 ** 32, "b2", Al.mult, Al.add)
-    cs("b1", "od", "b", None, Al.mult); cs("b0", "b1", -1.0, "b", Al.mult, Al.add); cs("s1", "od", -2.0 ** 14, None, Al.mult); cs("s0", "od", 2.0 ** 14, -2.0 ** 14, Al.mult, Al.add)
+    act(1, ["cdv", "cb2"], ["cb"], c("b"), c("dv"), Af.Identity, bias=c("b2"), scale=2.0 ** 32)
     act(8, ["OH"], ["OHb"], T.OHb[:], T.OH[:], Af.Identity, scale=-8192.0)
-
-    def scaled(nm, sc):
-        act(128, ["Ib"] + (["c" + sc] if isinstance(sc, str) else []), [nm], T[nm][:], T.Ib[:], Af.Identity, scale=c(sc) if isinstance(sc, str) else sc)
-    for nm, sc in (("If", 1.0), ("nI", -1.0), ("S01", "s01"), ("DB", "dv")) + ((("nIf", -1.0),) if LL & 1 else ()):
-        scaled(nm, sc)
+    act(128, ["Ib"], ["If"], T.If[:], T.Ib[:], Af.Copy)
+    act(128, ["Ib", "cdv"], ["DB"], T.DB[:], T.Ib[:], Af.Identity, scale=c("dv"))
+    sel(128, ["Ib"], ["S01"], T.S01[:], T.Ib[:], [[0, 8], [-1, 16]], Al.is_ge, 0.0, 1, 0)
     rows = [[-16, 8], [0, 16]]
-    sel(128, ["ones"], ["Dp0"], T.Dp0[:], T.ones[:], rows, Al.is_equal, 0.0, 0, 1)
-    sel(128, ["ones"], ["Dp1"], T.Dp1[:], T.ones[:], rows, Al.is_equal, 0.0, -1, 1)
+    for nm, src, k in (("Dp0", "ones", 0), ("Dp1", "ones", 1), ("Dm1", "mones", 1)):
+        sel(128, [src], [nm], T[nm][:], T[src][:], rows, Al.is_equal, 0.0, -k, 1)
     sel(128, ["Dp1"], ["D01"], T.D01[:], T.Dp1[:], rows, Al.not_equal, -1.0, 0, 1)
-    act(128, ["Dp1"], ["Dm1"], T.Dm1[:], T.Dp1[:], Af.Identity, scale=-1.0)
     sel(8, ["ones"], ["SL"], T.SL[:], T.ones[:, 0:8], [[-16, 8]], Al.is_equal, 0.0, -2, 1)
     ms(256, ["seg0"], T.seg[:], 0.0); ms(16, ["seg"], T.seg[:, 0:256:16], 2.0 ** 23, r=["seg0"])
+    iota(512, ["sez0"], T.sez[:], [[0, 512]], 0, 0); ms(2, ["sez"], T.sez[:, 0:512:256], 2.0 ** 40, r=["sez0"])
     act(16, ["M16"], ["MK4"], T.MK[:, 0:16], T.M16[:], Af.Copy)
     for s in range(4, 8):
-        act(1 << s, ["MK%d" % s], ["MK%d" % (s + 1) if s < 7 else "MK"], T.MK[:, 1 << s:2 << s], T.MK[:, 0:1 << s], Af.Copy)
-    cp(16, ["i16"], ["offG"], T.offG[:], T.i16[:])
+        act(1 << s, ["MK%d" % s], ["MK%d" % (s + 1)], T.MK[:, 1 << s:2 << s], T.MK[:, 0:1 << s], Af.Copy)
+    act(256, ["MK8"], ["MB"], T.MB[:], T.MK[:], Af.Identity, bias=8192.0, scale=-8192.0)
+    act(16, ["i16"], ["offG"], T.offG[:], T.i16[:], Af.Copy)
     ms(128, ["Mz0"], T.Mz[:], 0.0)
-    for h in range(2):
-        ts(8, ["Mz0", "WD0", "cp"], ["Mj%d" % h], T.Mz[:, 128 * h + 3:128 * h + 128:16], T.WD[:, 0:8], c("p"), 128.0 * h, Al.add, Al.add)
+    act(16, ["Mz0", "G8"], ["Mj"], T.Mz[:, 3:256:16], T.G8[:], Af.Copy)
     act(16, ["M16"], ["DL"], T.DL[:], T.M16[:], Af.Identity, scale=-256.0)
     act(1, ["M16"], ["bits0"], T.bits[:, 0:1], T.M16[:, 0:1], Af.Identity, scale=0.0)
     for s in range(12):
         n = 1 << s
         for j in range(2 if n > 512 else 1):
             m = n // 2 if n > 512 else n
-            a = s < BA
+            a = s < P["ba"]
             shift(a, m if a else m // 2, ["bits%d" % s, "bitt%d" % s, "DL"], ["bit%s%d" % ("st"[j], s + 1)], T.bits[:, n + j * m:n + j * m + m], T.bits[:, j * m:j * m + m], T.DL[:, 4 + s:5 + s])
     bitsr = ["bits12", "bitt12"]
 
-    Pb = lambda k: T.pP[:, 512 * k:512 * k + 512]
-    ts(1024, ["tci"], ["tch"], T.tch[0:32, :], T.tci[0:32, :], 2048, None, Al.subtract)
-    mm(["CK", "SA"], ["Z0"], [(T.pZ0[:, 0:256], T.CK[0:32, 256:384], T.SA[0:32, 0:256], True, 256)])
-    for a in range(4):
-        mm(["tch", "SA"], ["Z0"], [(T.pZ0[:, 64 * a:64 * a + 64], T.SA[0:32, 144 * a + 15 - r:144 * a + 143 - r], T.tch[0:32, r:1024:16], False, 64) for r in range(16)])
+    act(1024, ["tci"], ["tch"], T.tch[0:32, :], T.tci[0:32, :], Af.Identity, bias=-2048.0)
     for hh in range(2):
-        mm(["tw%d" % hh, "WD1"], ["Z0"], [(T.pZ0[:, half(hh)], T.WD[:, 15 - r:143 - r], T.tw[:, 2048 * hh + r:2048 * hh + 2048:16], False, 128) for r in range(16)])
-    ts(256, [], ["ui0", "ui1"], T.ui[:], T.pZ0[:, 0:256], 2048 - 255.0 / 512, None, Al.add, b=["Z0"])
-    ts(256, ["ui0", "ui1"], ["uj0", "uj1"], T.uj[:], T.ui[:], 4095, None, Al.bitwise_and)
-    cp(256, ["uj0", "uj1"], ["offK"], T.offK[:], T.uj[:])
-    iota(512, ["CKP0"], T.CKP[0:32, :], [[0, 512]], 0, 0, r=["offK"]); iota(512, ["CKP"], T.CKP[0:1, :], [[0, 512]], -int(YO), 0, r=["CKP0"])
+        bk, pk = bank(hh); tag[0] = "Kt%d" % hh
+        mm(["CK", "SA"], bk, [(pk[:, 0:128], CK[0:32, 0:128], T.SA[0:32, 0:128], True, 128)])
+        for a in range(2 * hh, 2 * hh + 2):
+            mm(["tch", "SA"], bk, [(pk[:, 64 * (a % 2):64 * (a % 2) + 64], T.SA[0:32, 144 * a + 15 - r:144 * a + 143 - r], T.tch[0:32, r:1024:16], False, 64) for r in range(16)])
+        tag[0] = "Kw%d" % hh
+        mm(["tw%d" % hh, "WD"], bk, [(pk[:, 0:128], T.WD[:, 15 - r:143 - r], T.tw[:, 2048 * hh + r:2048 * hh + 2048:16], False, 128) for r in range(16)])
+        tag[0] = ""
+        ts(128, [], ["ui%d" % hh], T.ui[:, half(hh)], pk[:, 0:128], 2048 + RC, None, Al.add, b=[bk])
+        ts(128, ["ui%d" % hh], ["uj%d" % hh], T.uj[:, half(hh)], T.ui[:, half(hh)], 4095, None, Al.bitwise_and)
+        cp(128, ["uj%d" % hh], ["offK%d" % hh], T.offK[:, half(hh)], T.uj[:, half(hh)])
+    iota(512, ["CKP0"], T.CKP[0:32, :], [[0, 512]], 0, 0); iota(512, ["CKP"], T.CKP[0:1, :], [[0, 512]], -int(YO), 0, r=["CKP0"])
     for k in range(8):
-        iota(560, ["tg%d" % k], T.tab1[:, 560 * k:560 * k + 560], [[0, 560]], 0, 0, r=["offK"])
-    Hr = ["H%d" % i for i in range(NH)]
-
-    def window():
-        for s in range(NH):
-            n = 4096 // NH; sl = slice(n * s, n * s + n); bit = T.bits[:].indirect(T.offK[:, n * s // 16:(n * s + n) // 16])
-            if s < NH - HA:
-                tt(n * GC, bitsr + ["offK", "tw0", "tw1"], ["H%d" % s], T.Hw[:, sl], bit, T.tw[:, sl], Al.add)
-            else:
-                z = s % 2; tmp = T.y1[:, n * z:n * z + n]
-                act(n * GC, bitsr + ["offK"], ["y1.%d" % z], tmp, bit, Af.Copy)
-                mm(["y1.%d" % z, "Ib", "tw0", "tw1"], ["Z%d" % z], [(pZ[z][:], T.Ib[:], T.tw[:, sl], True, 512), (pZ[z][:], T.Ib[:], tmp, False, 512)])
-                act(n, [], ["H%d" % s], T.Hw[:, sl], pZ[z][:], Af.Copy, b=["Z%d" % z])
-        for hh in range(4):
-            for k in range(1, 4):
-                dma("s", 256, Hr[hh * NH // 4:(hh + 1) * NH // 4], ["Hx%d.%d" % (k, hh)], T.Hw[:, 4096 * k + 1024 * hh:4096 * k + 1024 * hh + 1024], T.Hw[:, 1024 * hh:1024 * hh + 1024])
+        iota(512, ["tg%d" % k], T.tab1[:, 512 * k:512 * k + 512], [[0, 512]], 0, 0)
+    Hr = ["H%d" % i for i in range(8)]
+    for s in range(8):
+        sl = slice(512 * s, 512 * s + 512); bit = T.bits[:].indirect(T.offK[:, 32 * s:32 * s + 32]); tag[0] = "H%d" % s
+        if str(s) not in P["ha"]:
+            tt(512 * GC, bitsr + ["offK%d" % (s // 4), "tw%d" % (s // 4)], ["H%d" % s], T.Hw[:, sl], bit, T.tw[:, sl], Al.add)
+        else:
+            bk, pk = bank(2 + P["ha"].index(str(s)) % 2); lo = 512 * (s % 4); tmp = T["G%d" % (s // 4)][:, lo:lo + 512]; key = blk("G%d" % (s // 4), lo, lo + 512)
+            act(512 * GC, bitsr + ["offK%d" % (s // 4)], key, tmp, bit, Af.Copy)
+            mm(key + ["Ib", "tw%d" % (s // 4)], bk, [(pk, T.Ib[:], T.tw[:, sl], True, 512), (pk, T.Ib[:], tmp, False, 512)])
+            act(512, [], ["H%d" % s], T.Hw[:, sl], pk, Af.Copy, b=[bk])
+    tag[0] = ""
+    for hh in range(4):
+        for k in range(1, 4):
+            dma("s", 256, Hr[2 * hh:2 * hh + 2], ["Hx%d.%d" % (k, hh)], T.Hw[:, 4096 * k + 1024 * hh:4096 * k + 1024 * hh + 1024], T.Hw[:, 1024 * hh:1024 * hh + 1024])
     Hxr = Hr + ["Hx%d.%d" % (k, hh) for k in range(1, 4) for hh in range(4)]
 
-    ts(768, ["cI0", "cI1", "cI2"], ["cmp0", "cmp1", "cmp2"], T.cmp[:], T.cmpI[:], 2048, None, Al.subtract)
+    act(768, ["cI0", "cI1", "cI2"], ["cmp0", "cmp1", "cmp2"], T.cmp[:], T.cmpI[:], Af.Identity, bias=-2048.0)
 
     def unpack(src, keys, tb):
         for q in range(3):
             dma("s", 128, [keys % q] + fill[tb], ["tab%d.%d" % (tb, q)], tab[tb][q:128:16, 0:4096], src[:, 256 * q:256 * q + 256])
     tabk = lambda tb: fill[tb] + ["tab%d.%d" % (tb, q) for q in range(3)]
     unpack(T.cmp, "cmp%d", 0)
-    ts(256, ["ow0", "ow1", "ow2"], ["A0"], T.A0[:], T.owni[:], 2048, None, Al.subtract)
+    act(256, ["ow0", "ow1", "ow2"], ["A0"], T.A0[:], T.owni[:], Af.Identity, bias=-2048.0)
     tn = lambda k: T.tn[:, 16 * k:16 * k + 16]
     Mz = T.Mz[:, 2:256:16]
-    lb = T["p" + LB][:, 0:16]
-    mm(["A0", "SL"], [LB], [(T["p" + LB][:, 8 * h:8 * h + 8], T.A0[:, half(h)], T.SL[:], True, 64) for h in range(2)])
+    tag[0] = "Mz"
+    mm(["A0", "SL"], "S", [(pS[:, 8 * h:8 * h + 8], T.A0[:, half(h)], T.SL[:], True, 64) for h in range(2)])
+    act(16, ["Mz0"], ["Mz"], Mz, pS[:, 0:16], Af.Copy, b=["S"])
 
-    def lengths(grow, src, r, b):
-        ts(16, ["Mz0"] + r, ["Mz"], Mz, src, grow, 2047.0, Al.add, Al.min, b=b)
-        act(16, r, ["mr"], tn(8), src, Af.Relu, bias=2047.0 - grow, scale=-1.0, b=b)
+    def ownkeys():
         for h in range(2):
-            act(8, ["mr", "JB"], ["kb%d" % h], T.tn[:, 32 + 8 * h:40 + 8 * h], T.tn[:, 128 + 8 * h:136 + 8 * h], Af.Identity, bias=T.JB[:, h:h + 1], scale=-2.0 ** 20)
-    lengths(0.0, lb, [], [LB])
+            act(8, ["Mz", "JB"], ["kb%d" % h], T.tn[:, 32 + 8 * h:40 + 8 * h], T.Mz[:, 128 * h + 2:128 * h + 128:16], Af.Identity, bias=T.JB[:, h:h + 1], scale=2.0 ** 20)
+    ownkeys()
 
-    def gather(h, npc, win, wr, off, offr, new, prev, name=""):
-        for s in range(npc):
-            tag[0] = name and "%s%d%d" % (name, h, s)
-            n = 2048 // npc; o = off[:, 128 * h + n * s // 16:128 * h + (n * s + n) // 16]; sl = slice(n * s, n * s + n)
-            ks = range(4 * s // npc, 4 * (s + 1) // npc)
-            if h == 1:
-                act(n * GC, wr + offr, ["G%d.%d" % (new, k) for k in ks], G[new][:, sl], win.indirect(o), Af.Copy)
-            elif prev is not None:
-                tt(n * GC, wr + offr + ["X%d.%d" % (prev, k) for k in ks], ["X%d.%d" % (new, k) for k in ks], X[new][:, sl], win.indirect(o), X[prev][:, sl], Al.add)
+    def gather(h, pieces, win, wr, off, offr, new, prev=None):
+        for lo, hi in cuts(pieces):
+            o = win.indirect(off[:, 128 * h + lo // 16:128 * h + hi // 16]); n = (hi - lo) * GC
+            if prev:
+                tt(n, wr + offr + blk(prev, lo, hi), blk(new, lo, hi), T[new][:, lo:hi], o, T[prev][:, lo:hi], Al.add)
             else:
-                act(n * GC, wr + offr, ["X%d.%d" % (new, k) for k in ks], X[new][:, sl], win.indirect(o), Af.Copy)
+                shift(h, n, wr + offr, blk(new, lo, hi), T[new][:, lo:hi], o, 0.0)
 
-    def addP(src, key, q, start=False):
-        for bk in range(4):
-            tag[0] = "add%d%d" % (q, bk)
-            mm([key % bk, "Ib"], ["P%d" % bk], [(Pb(bk), T.Ib[:], src[:, 512 * bk:512 * bk + 512], start, 512)])
+    def column(h, start=False):
+        return [(reg(K0[h]), T.ones[0:32, :], CK[0:32, 384 + 128 * h:512 + 128 * h], start, 128)]
 
-    def tr(h, src, keys, lo, n, r0, last=False):
-        lst = [(pT[:, lo + i:lo + 128 * n:16], src[:, i:2048:16], RR[:, r0:r0 + 8 * n], False, 64) for i in range(16)]
-        if last:
-            lst += [(pT[:, K0[h]:K0[h] + 128], T.ones[0:32, :], T.CK[0:32, 512 + 128 * h:640 + 128 * h], False, 128)]
-        mm(keys + RRr + ["CKd", "ones"], ["T%d" % h], lst)
+    def tr(b, src, lo, n, r0, more=()):
+        mm(blk(src) + ["RR%d" % k for k in range(r0, r0 + n)] + ["CKd", "ones"], b,
+           [(pT[:, lo + i:lo + 128 * n:16], T[src][:, i:2048:16], RR[:, 8 * r0:8 * (r0 + n)], False, 64) for i in range(16)] + list(more))
 
-    def direct(h, src, key, neg, name=""):
+    def direct(h, src):
         for s in range(2):
-            tag[0] = "d%d%d" % (h, s) if name else tag[0]
-            mm([key % (2 * s), key % (2 * s + 1), "WD%d" % (1 + neg)], ["T%d" % h],
-               [(pT[:, U0[h] + 64 * s:U0[h] + 64 * s + 64], T.WD[:, 144 * neg + 15 - i:144 * neg + 143 - i], src[:, 1024 * s + i:1024 * s + 1024:16], False, 64) for i in range(16)])
+            mm(blk(src, 1024 * s, 1024 * s + 1024) + ["WD"], UB[h],
+               [(reg(U0[h] + 64 * s, 64), T.WD[:, 15 - i:143 - i], T[src][:, 1024 * s + i:1024 * s + 1024:16], False, 64) for i in range(16)])
 
-    def const(h, lo, n, c0, full):
-        k = 64 if full else 32
-        mm(CKr, ["T%d" % h], [(pT[:, lo:lo + n], T.ones[0:k, :], T.CK[0:k, c0:c0 + n], True, n)])
+    def const(lo, n, c0, rows, start=True):
+        return (reg(lo, n), T.ones[0:rows, :], CK[0:rows, c0:c0 + n], start, n)
 
-    def escopy(h):
-        n = 256 - 128 * h
-        shift(ESA >> h & 1, n, [], ["ES%d" % h], ES[:, EC[h]:EC[h] + n], pT[:, E0[h]:E0[h] + n], 0.0, b=["T%d" % h])
+    def turn(h, lo):
+        return (reg(U0[h]), ES[:, lo:lo + 128], T.If[:], True, 512)
 
-    def turned(h):
-        mm(["ES%d" % h, "If"], ["T%d" % h], [(pT[:, U0[h]:U0[h] + 128], ES[:, EC[h]:EC[h] + 128], T.If[:], True, 512)])
-
-    def letters(h, mat, cur):
-        mm([mat, "A%d" % cur], ["T%d" % h], [(pT[:, U0[h]:U0[h] + 128], T[mat][:], A[cur][:, half(h)], False, 128)])
+    def points(h):
+        tag[0] = "es" + "ab"[h]; n = 256 - 128 * h
+        act(n, [], ["ES%d" % h], ES[:, EC[h]:EC[h] + n], reg(E0[h], n), Af.Identity, bias=RC, b=[EB[h]])
 
     def nstage(h, add, out, key, plain):
-        o = pT[:, U0[h]:U0[h] + 128]; sl = half(h)
-        if plain:
-            ts(128, [], [key], out[:, sl], o, MG, MG - add, Al.add, Al.subtract, b=["T%d" % h])
+        o = reg(U0[h]); sl = half(h); b = [UB[h]]
+        if plain and tag[0] in P["au"]:
+            act(128, [], [key], out[:, sl], o, Af.Identity, bias=float(add), b=b)
+        elif plain:
+            ts(128, [], [key], out[:, sl], o, MG, MG - add, Al.add, Al.subtract, b=b)
         else:
-            ts(128, [], ["ui%d" % h], T.ui[:, sl], o, float(add), None, Al.add, b=["T%d" % h])
-            if AU and key[0] == "o":
-                ts(128, ["ui%d" % h], [key], out[:, sl], T.ui[:, sl], 4095, None, Al.bitwise_and)
-                return
+            ts(128, [], ["ui%d" % h], T.ui[:, sl], o, float(add), None, Al.add, b=b)
             ts(128, ["ui%d" % h], ["uj%d" % h], T.uj[:, sl], T.ui[:, sl], 4095, None, Al.bitwise_and)
-            cp(128, ["uj%d" % h], [key], out[:, sl], T.uj[:, sl])
+            shift(tag[0] in P["au"], 128, ["uj%d" % h], [key], out[:, sl], T.uj[:, sl], 0.0)
 
-    def reduce256(src, sk, out, ok, ra, h=0):
-        for bk in range(4):
-            z = bk % 2; sl = slice(512 * bk, 512 * bk + 512); tag[0] = "mod%d" % bk
-            mm([sk % bk, "y%d.%d" % (h, bk), "Ib", "nI"], ["Z%d" % z], [(pZ[z][:], T.Ib[:], src[:, sl], True, 512), (pZ[z][:], T.nI[:], T["y%d" % h][:, sl], False, 512)])
-            shift(bk < ra, 512, [], [ok % bk], out[:, sl], pZ[z][:], -YO, b=["Z%d" % z])
+    def reduce256(src, out, ra, banks):
+        for k, (lo, hi) in enumerate(cuts(4)):
+            bk, pk = bank(banks[k])
+            mm(blk(src, lo, hi) + blk("y0", lo, hi) + ["Ib", "nI"], bk, [(pk, T.Ib[:], T[src][:, lo:hi], True, 512), (pk, T.nI[:], T.y0[:, lo:hi], False, 512)])
+            shift(k < ra, 512, [], blk(out, lo, hi), T[out][:, lo:hi], pk, -YO, b=[bk])
+
+    def carries(h, src):
+        tag[0] = "y" + "ab"[h]
+        for lo, hi in cuts(P["y"][h]):
+            ts((hi - lo) // 2, blk(src, lo, hi), blk("y%d" % h, lo, hi), T["y%d" % h][:, lo:hi], T[src][:, lo:hi], -YO - 127.5, None, Al.add)
 
     for h in range(2):
-        gather(h, 2, T.tw[:], ["tw0", "tw1"], T.offI, ["offI"], 2 if h else 3, None)
-        const(h, 128 + 384 * h, 384 - 128 * h, 256 * h, False)
-        mm(["imgf", "If"], ["T%d" % h], [(pT[:, E0[h]:E0[h] + 128], T.imgf[:, half(h)], T.If[:], False, 512)])
-        if h:
-            tr(1, G[2], allp("G2"), K0[1], 1, 16, True)
-        else:
-            tr(0, X[3], allp("X3"), 256, 2, 8, True)
-    escopy(0)
-    at = [3]
+        tag[0] = "i" + "ab"[h]
+        gather(h, 2, T.tw[:], ["tw0", "tw1"], T.offI, ["offI"], "X%d0" % h)
+    tag[0] = "ka"
+    mm(["CK", "ones", "imgf", "If"], "T0", [const(128, 384, 0, 32), (reg(E0[0]), T.imgf[:, half(0)], T.If[:], False, 512)])
+    tr("T0", "X00", 256, 2, 1, column(0))
+    points(0)
+    tag[0] = "kb"
+    mm(["imgf", "If"], "T2", [(reg(E0[1]), T.imgf[:, half(1)], T.If[:], True, 512)])
+    points(1)
+    tag[0] = "kb"
+    mm(["CKd", "ones"], "T1", column(1, True))
+    tr("T1", "X10", K0[1], 1, 2)
     for n in range(1, 7):
         cur, old = n % 2, 1 - n % 2
-        tb = ((n - 1) // 2) % 2
+        tb = ((n - 1) // 2) % 2; ho = (n - 1) // 2
         kind = 2 if n == 6 else 1 - cur
-        NZD, YV, BANKS = NZ[kind], YS[kind], BK[kind]
-        first = len(ops); tag[0] = "window"
-        if n == 1:
-            window()
+        keys = n < 6
+        tag[1] = n
+        Ak, Ao = "A%d" % cur, "A%d" % old
         if n == 4:
-            reduce256(X[at[0]], "X%d." % at[0] + "%d", X[3], "X3.%d", RA)
-            at[0] = 3
-        tag[0] = "chain"
-        v(256, ["seg"], ["Rm"], lambda q: q.tensor_tensor_scan(T.Rm[:], T.seg[:], pT[:, 384:640], 0.0, Al.add, Al.min), ["T0", "T1"])
-        escopy(1)
-        if AU:
-            ts(16, ["Rm"], ["offW"], T.offW[:], T.Rm[:, 15:256:16], 255, None, Al.bitwise_and)
-        else:
-            ts(16, ["Rm"], ["oj"], T.oj[:], T.Rm[:, 15:256:16], 255, None, Al.bitwise_and)
-            cp(16, ["oj"], ["offW"], T.offW[:], T.oj[:])
-        tt(256 * GC, ["ES0", "ES1", "offW", "MK"], ["Wz"], T.Wz[:], ES[:, 128:384].indirect(T.offW[:]), T.MK[:], Al.mult)
-        turned(0)
-        mm(["Wz", "OH"], ["T1"], [(pT[:, L0 + 8 * h:L0 + 8 * h + 8], T.Wz[:, half(h)], T.OH[:], True, 256) for h in range(2)])
-        pv = T.pZ1[:, 0:256]; tag[0] = "pv"
-        mm(["A%d" % old, "S01", "Mz", "Mj0", "Mj1", "Ib"], ["Z1"], [(pv, T.S01[:], A[old][:], True, 256)] +
-           [(T.pZ1[:, half(h)], T.Mz[:, half(h)], T.Ib[:], False, 128) for h in range(2)])
-        if n == 1:
-            ops[-1]["tag"] = "xl"
-        tag[0] = "point"
-        ts(16, [], ["wi"], T.wi[:], pT[:, L0:L0 + 16], 2048.0 if n > 1 else 0.0, None, Al.add, b=["T1"])
-        turned(1)
-        if AU:
-            ts(16, ["wi"], ["oO"], T.offO[:], T.wi[:], 4095, None, Al.bitwise_and)
-            tag[0] = "win"
+            tag[0] = "m"
+            reduce256("X0%d" % old, "X0%d" % cur, 4, "2323")
+        tag[0] = "tub"
+        mm(["ES1", "If"], UB[1], [turn(1, EC[1])])
+        tag[0] = "scan"
+        scan(256, ["seg"], ["Rm"], T.Rm[:], T.seg[:], reg(384, 256), ["T0", "T1"])
+        ts(16, ["Rm"], ["oj"], T.oj[:], T.Rm[:, 15:256:16], 255, None, Al.bitwise_and)
+        cp(16, ["oj"], ["offW"], T.offW[:], T.oj[:])
+        tt(256 * GC, ["ES0", "ES1", "offW", "MK8"], ["Wz"], T.Wz[:], ES[:, 128:384].indirect(T.offW[:]), T.MK[:], Al.mult)
+        mm(["Wz", "OH"], "S", [(pS[:, 8 * h:8 * h + 8], T.Wz[:, half(h)], T.OH[:], True, 256) for h in range(2)])
+        ts(16, [], ["wi"], T.wi[:], pS[:, 0:16], 2048.0 if n > 1 else 0.0, None, Al.add, b=["S"])
         ts(16, ["wi"], ["wj"], T.wj[:], T.wi[:], 4095, None, Al.bitwise_and)
-        tag[0] = "point"
-        if not AU:
-            cp(16, ["wj"], ["oO"], T.offO[:], T.wj[:])
-        shift(False, 256 * GC, tabk(tb) + ["oO"], ["A%d" % cur], A[cur][:], tab[tb][:].indirect(T.offO[:]), -2048.0 if n > UN else 0.0)
-        for h in (1, 0):
-            tag[0] = "go%d" % h
-            letters(h, "Dp0", cur)
-            nstage(h, 2048 if n == 1 else 8192, T.offU0, "oU0.%d" % h, n > 1 or M1 < 1)
+        cp(16, ["wj"], ["oO"], T.offO[:], T.wj[:])
+        tag[0] = "look"
+        shift(P["look"] == "a", 256 * GC, tabk(tb) + ["oO"], [Ak], A[cur][:], tab[tb][:, 0:4096].indirect(T.offO[:]), 0.0)
+        tag[0] = "tua"
+        mm(["ES0", "If"], UB[0], [turn(0, EC[0])])
+        for h in range(2):
+            tag[0] = "go" + "ab"[h]
+            mm(["Dp0", Ak], UB[h], [(reg(U0[h]), T.Dp0[:], A[cur][:, half(h)], False, 128)])
+            nstage(h, 2048 if n == 1 else 8192, T.offU0, "oU0.%d" % h, n > 1)
         tag[0] = "xl"
-        for par in range(2):
-            act(256 * GC, bitsr + ["oO", "cs%d" % par, "cb%d" % par], ["XL%d" % par], XL[par][:], T.bits[:].indirect(T.offO[:]), Af.Identity, bias=c("b%d" % par), scale=c("s%d" % par))
-        mm(["XL0", "XL1", "DB"], ["Z1"], [(pv, T.DB[:], XL[par][:], False, 256) for par in range(2)])
+        act(256 * GC, bitsr + ["oO", "cb"], ["XL0"], XL[0][:], T.bits[:].indirect(T.offO[:]), Af.Identity, bias=c("b"), scale=-2.0 ** 14)
+        tag[0] = "xo"
+        if P["xo"] == "v":
+            ts(128, ["XL0", "odb"], ["XL1"], XL[1][:], XL[0][:], T.odb[:, 0:1], None, Al.mult)
+        else:
+            act(256, ["XL0", "cod"], ["XL1"], XL[1][:], XL[0][:], Af.Identity, scale=c("od"))
+        tag[0] = "pv"; bk, pk = bank(P["zb"][kind][0]); pv = pk[:, 0:256]
+        mm([Ao, "S01", "Mz", "Mj", "Ib"], bk, [(pv, T.S01[:], A[old][:], True, 256)] + [(pk[:, half(h)], T.Mz[:, half(h)], T.Ib[:], False, 128) for h in range(2)])
         tag[0] = "xr"
-        cp(256, [], ["XR%d" % cur], XR[cur][:], pv, b=["Z1"])
-        tag[0] = "at"
-        mm(["A%d" % cur, "SL", "nI", "Mz"], ["Z0"], [(T.pZ0[:, 0:16], T.nI[:], Mz, True, 64)] + [(T.pZ0[:, 8 * h:8 * h + 8], A[cur][:, half(h)], T.SL[:], False, 64) for h in range(2)])
-        act(16, [], ["AT"], T.AT[:], T.pZ0[:, 0:16], Af.Copy, b=["Z0"])
-        ho = (n - 1) // 2
-        tag[0] = "xr"
+        mm(["XL0", "DB"], bk, [(pv, T.DB[:], XL[0][:], False, 256)])
+        act(256, [], ["XR%d" % cur], XR[cur][:], pv, Af.Copy, b=[bk])
+        tag[0] = "lv"
         if n == 6:
-            tag[0] = "at"
-            shift(V6A, 256, [], ["V%d" % n], T["V%d" % n][:], pv, 2048.0, b=["Z1"])
-            send(n - 1, 128, ["V%d" % n], ["lv%d" % n], T["lv%d" % n][:], T["V%d" % n][:])
+            shift(True, 256, [], ["V6"], T.V6[:], pv, 2048.0, b=[bk])
+            send(n - 1, 128, ["V6"], ["lv6"], T.lv6[:], T.V6[:])
         elif cur == 0:
-            tag[0] = "at"
-            send(n - 1, 64, ["XR%d" % cur], ["lv%d" % n], T["lv%d" % n][:], XR[cur][:])
-        for k in range(8):
-            tag[0] = "t%d" % k; bk = BANKS[2 * k:2 * k + 2]
-            lo = 0 if bk[0] == "Z" else 512 * int(bk[1])
-            two = [(2 * k + x, T["p" + (bk if bk[0] == "Z" else bk[0])][:, lo + 256 * x:lo + 256 * x + 256]) for x in range(2)]
-            mm(["XL0", "XL1", "XR%d" % cur], [bk], [(o, XL[kz % 2][32 * (kz % 8 // 2):32 * (kz % 8 // 2) + 32, half(kz // 8)], XR[cur][32 * (kz % 8 // 2):32 * (kz % 8 // 2) + 32, :], True, 256) for kz, o in two])
-            for kz, o in two:
-                if kz < 16 - NZD:
-                    act(280, ["kb%d" % (kz // 8)], ["cn%d" % kz, "jk%d" % kz], T.junk[:, 256 * kz:256 * kz + 256], o, Af.Relu, bias=T.tn[:, 32 + kz:33 + kz], scale=-1.0, b=[bk], acc=T.cnt[:, kz:kz + 1])
-                else:
-                    v(256, [], ["mn%d" % kz], lambda q, o=o, kz=kz: q.tensor_reduce(T.tn[:, 64 + kz:65 + kz], o, AxisListType.X, Al.min), [bk])
-        tag[0] = "win"
-        if NZD:
-            tt(16, ["kb0", "kb1"] + ["mn%d" % k for k in range(16 - NZD, 16)], ["cn%d" % k for k in range(16 - NZD, 16)], T.cnt[:, 16 - NZD:16], T.tn[:, 48 - NZD:48], T.tn[:, 80 - NZD:80], Al.subtract)
-        tt(16, ["AT"] + ["cn%d" % k for k in range(16)], ["wn"], tn(1), T.AT[:], T.cnt[:], Al.is_gt)
-        tt(256 * GC, ["wn", "offG", "MK"], ["Wn"], T.Wn[:], tn(1).indirect(T.offG[:]), T.MK[:], Al.mult)
-        if n < 6:
-            tag[0] = "len"
-            tt(16, ["wn", "AT"], ["z"], tn(0), tn(1), T.AT[:], Al.mult)
-            if PV & 1:
-                mm(["z", "Mz", "If", "Ib"], [LB], [(lb, T.If[:], tn(0), True, 256), (lb, T.Ib[:], Mz, False, 64)])
-                lengths(2.0, lb, [], [LB])
+            send(n - 1, 64, ["XR0"], ["lv%d" % n], T["lv%d" % n][:], XR[0][:])
+        tag[0] = "at"; AT, M2, LS = pS[:, 16:32], pS[:, 32:48], pS[:, 48:64]
+        mm([Ak, "SL", "nI", "Mz"], "S", [(AT, T.nI[:], Mz, True, 64)] + [(pS[:, 16 + 8 * h:24 + 8 * h], A[cur][:, half(h)], T.SL[:], False, 64) for h in range(2)])
+        zv = P["zv"][kind]; za = 16 - 2 * zv
+        for k, zb in zip([int(x) for x in P["zo"][kind]], P["zb"][kind][1:]):
+            tag[0] = "z%d" % k; bk, pk = bank(zb); lst = []
+            for x in range(2):
+                kz = 2 * k + x; r0 = 32 * (kz % 8 // 2); rs = slice(r0, r0 + 16 + 16 * x)
+                lst.append((pk[:, 256 * x:256 * x + 256], XL[x][rs, half(kz // 8)], XR[cur][rs, :], True, 256))
+            mm(["XL0", "XL1", "XR%d" % cur], bk, lst)
+            if k >= 8 - zv:
+                j = k - 8 + zv
+                scan(512, ["sez"], ["mn%d" % k], T.zs[:, 512 * j:512 * j + 512], T.sez[:], pk, [bk])
             else:
-                tt(16, ["z", "Mz"], ["mx"], tn(6), tn(0), Mz, Al.add)
-                lengths(2.0, tn(6), ["mx"], [])
-            if n == 1:
-                weights(1, "ncw")
+                for x in range(2):
+                    kz = 2 * k + x
+                    act(256, ["kb%d" % (kz // 8)], ["cn%d" % kz], T.junk[:, 256 * kz:256 * kz + 256], pk[:, 256 * x:256 * x + 256], Af.Relu,
+                        bias=T.tn[:, 32 + kz:33 + kz], scale=-1.0, b=[bk], acc=T.cnt[:, kz:kz + 1])
+        tag[0] = "win"
+        if zv:
+            tt(16, ["kb0", "kb1"] + ["mn%d" % k for k in range(8 - zv, 8)], ["cn%d" % k for k in range(za, 16)], T.cnt[:, za:16], T.tn[:, 32 + za:48], T.zs[:, 255:512 * zv:256], Al.subtract)
+        tt(16, ["cn%d" % k for k in range(16)], ["d"], tn(1), AT, T.cnt[:], Al.subtract, b=["S"])
+        tt(256 * GC, ["d", "offG", "MB"], ["Wn"], T.Wn[:], tn(1).indirect(T.offG[:]), T.MB[:], Al.is_gt)
         tag[0] = "list"
-        mm(["Wn", "OHb", "If", "DUM"], ["Z0"], [(T.pZ0[:, 0:16], T.If[:], T.DUM[:], True, 256)] + [(T.pZ0[:, 8 * h:8 * h + 8], T.Wn[:, half(h)], T.OHb[:], False, 64) for h in range(2)])
-        tt(16, ["wj"], ["t9"], tn(9), T.pZ0[:, 0:16], T.wj[:], Al.max, b=["Z0"])
-        cp(16, ["t9"], ["oS%d" % cur], offS[cur][:], tn(9))
+        mm(["Wn", "OHb", "If", "DUM"], "S", [(LS, T.If[:], T.DUM[:], True, 256)] + [(pS[:, 48 + 8 * h:56 + 8 * h], T.Wn[:, half(h)], T.OHb[:], False, 64) for h in range(2)])
+        tt(16, ["wj"], ["t9"], tn(3), LS, T.wj[:], Al.max, b=["S"])
+        cp(16, ["t9"], ["oS%d" % cur], offS[cur][:], tn(3))
+        if keys:
+            tag[0] = "len"
+            act(16, ["d"], ["z"], tn(0), tn(1), Af.Relu)
+            mm(["z", "Mz", "If", "Ib", "ones"], "S", [(M2, T.If[:], tn(0), True, 256), (M2, T.Ib[:], Mz, False, 64), (M2, T.ones[0:2, :], T.ones[0:2, 0:16], False, 64)])
+            act(16, [], ["Mz"], Mz, M2, Af.Copy, b=["S"])
+            tag[0] = "own"
+            ownkeys()
         land = T["land%d" % ho]
         if cur == 1:
             tag[0] = "put"
             cp(1000, ["oS1", "XR1"], tabk(tb), tab[tb][:].indirect(offS[1][:]), XR[1][:])
+            tag[0] = "ring"
             for q in range(3):
                 dma("s", 128, tabk(tb), ["cmp%d" % q], T.cmp[:, 256 * q:256 * q + 256], tab[tb][q:128:16, 0:4096])
-            tag[0] = "ring"
             for q in range(3):
                 sl = slice(256 * q, 256 * q + 256); key = "land%d.%d" % (ho, q)
                 send(6 + 3 * ho + q, 128, ["cmp%d" % q], [key], land[:, sl], T.cmp[:, sl])
             if n < 5:
                 unpack(land, "land%d." % ho + "%d", 1 - tb)
         else:
+            tag[0] = "lo"
             send(n - 2, 4, ["oS0"], ["lo%d" % n], T["lo%d" % n][:], offS[0][:])
             tag[0] = "ring"
             if n == 6:
@@ -488,143 +465,84 @@ def build(T, topo, core, rank):
                 unpack(T.cmq, "cmq%d", 1 - tb)
             tag[0] = "put"
             cp(1000, ["lo%d" % n, "lv%d" % n], tabk(1 - tb), tab[1 - tb][:].indirect(T["lo%d" % n][:]), T["lv%d" % n][:])
-        keys = n < 6
-        run, rk = (G[2], "G2.%d") if n == 1 else (T.XA, "XA.%d")
-        fused = n in FU
-
-        def again():
-            for s in range(4):
-                tag[0] = ("fus%d" if fused else "out%d") % s; sl = slice(512 * s, 512 * s + 512)
-                if fused:
-                    tt(512, ["G0.%d" % s], [rk % s], run[:, sl], Pb(s), G[0][:, sl], Al.add, b=["P%d" % s])
-                elif n == RH + 1:
-                    tt(512, ["y1.%d" % s], [rk % s], run[:, sl], Pb(s), T.y1[:, sl], Al.subtract, b=["P%d" % s])
-                elif 1 < n < 6:
-                    cp(512, [], [rk % s], run[:, sl], Pb(s), b=["P%d" % s])
-                tag[0] = ("add0%d" if fused else "run%d") % s
-                mm([rk % s, "Ib"], ["P%d" % s], [(Pb(s), T.Ib[:], run[:, sl], True, 512)])
-                if n == 6:
-                    mm(["G0.%d" % s, "G1.%d" % s], ["P%d" % s], [(Pb(s), T.Ib[:], G[x][:, sl], False, 512) for x in range(5 in FU, 2)])
-                if n in (RH, 6):
-                    tag[0] = "sub"
-                    mm(["ones", "CKP"], ["P%d" % s], [(Pb(s), T.ones[0:32, :], T.CKP[0:32, :], False, 512)])
-        if not fused:
-            again()
-        for q in range(2):
-            win, wr = (T.Hw[:, 0:4096], Hr) if n == 1 and q < M1 else (T.Hw[:], Hxr)
+        Xo, Xn = ["X%d%d" % (h, old) for h in range(2)], ["X%d%d" % (h, cur) for h in range(2)]
+        plain = [n > 1 or q >= P["m1"] for q in range(2)]
+        win = [(T.Hw[:], Hxr) if x else (T.Hw[:, 0:4096], Hr) for x in plain]
+        for h in range(2):
+            z = "ab"[h]; tag[0] = "op" + z
+            mm([Ak, "D01", "If", "ES0", "CKg", "ones"], UB[h], [const(U0[1], 128, 768, 32) if h else turn(0, 384), (reg(U0[h]), T.D01[:], A[cur][:, half(h)], False, 128)])
+            tag[0] = "g0" + z
+            gather(h, P["g"][0][h], win[0][0], win[0][1], offU[0], ["oU0.%d" % h], "M%d" % h, None if h else Xn[0] if n == 4 else Xo[0])
+            tag[0] = "d" + z
+            direct(h, "M%d" % h)
+            tag[0] = "off" + z
+            nstage(h, 8192, T.offU1, "oU1.%d" % h, plain[1])
+        tag[0] = "oqa"
+        mm(["CKc", "ones", Ak, "Dm1"], "T0", [const(128, 384 if keys else 128, 0, 64), (reg(128), A[cur][:, half(0)], T.Dm1[:], False, 128)])
+        tr("T0", "M0", 128, 1, 1)
+        tag[0] = "g1a"
+        gather(0, P["g"][1][0], win[1][0], win[1][1], offU[1], ["oU1.0"], Xn[0], "M0")
+        carries(0, Xn[0])
+        tag[0] = "tra"
+        if n == 3:
+            mm(["CKe", "ones"], "T0", [const(256, 128, 640, 64, False)])
+            tr("T0", "y0", 256, 2, 3)
+            tag[0] = "keya"
+            tr("T0", Xn[0], 128, 3, 0, column(0))
+        else:
+            tr("T0", Xn[0], 128, 3 if keys else 1, 0)
+            tag[0] = "keya"
+            if keys:
+                tr("T0", "y0", K0[0], 1, 4, column(0))
+        points(0)
+        tag[0] = "oqb"
+        mm([Ak, "Dm1"], "T2", [(reg(E0[1]), A[cur][:, half(1)], T.Dm1[:], True, 128)])
+        tag[0] = "g1b"
+        gather(1, P["g"][1][1], win[1][0], win[1][1], offU[1], ["oU1.1"], "G1")
+        tag[0] = "trb"
+        tr("T2", "G1", E0[1], 1, 0)
+        points(1)
+        for k, (lo, hi) in enumerate(cuts(4)):
+            tag[0] = "p"; bk, pk = bank(P["pb"][kind][k]); G = T.G1[:, lo:hi]; Y = T.y1[:, lo:hi]; yk = blk("y1", lo, hi); onv = keys and k >= P["xa"][kind]
+            mm(blk(Xo[1], lo, hi) + blk("M1", lo, hi) + ["Ib", "nI", "ones", "CKP"] + yk * (n == 4), bk,
+               [(pk, T.Ib[:], T[Xo[1]][:, lo:hi], True, 512), (pk, T.Ib[:], T.M1[:, lo:hi], False, 512)] + [(pk, T.nI[:], Y, False, 512)] * (n == 4) +
+               [(pk, T.ones[0:32, :], T.CKP[0:32, :], False, 512)] * (n == 4 and onv or not keys))
+            tag[0] = "x"
+            if onv:
+                tt(512, blk("G1", lo, hi), blk(Xn[1], lo, hi), T[Xn[1]][:, lo:hi], pk, G, Al.add, b=[bk])
+                continue
+            mm(blk("G1", lo, hi) + ["Ib"], bk, [(pk, T.Ib[:], G, False, 512)])
+            if keys:
+                shift(True, 512, [], blk(Xn[1], lo, hi), T[Xn[1]][:, lo:hi], pk, -YO if n == 4 else 0.0, b=[bk])
+            else:
+                shift(True, 512, [], yk, Y, pk, -127.5, b=[bk])
+                tt(512, yk, blk("fo", 2048 + lo, 2048 + hi), T.fo[:, 2048 + lo:2048 + hi], pk, Y, Al.subtract, b=[bk])
+        if keys:
+            carries(1, Xn[1])
+            tag[0] = "trx"
+            mm(["CKc", "ones"], "T1", [const(K0[1], 128, 256, 64)])
+            tr("T1", Xn[1], K0[1], 1, 2)
+            tag[0] = "keyb"
+            tr("T1", "y1", K0[1], 1, 4, column(1))
+        else:
+            tag[0] = "f"
+            reduce256(Xn[0], "fo", P["rf"], P["pb"][kind][4:])
             for h in range(2):
-                if h == 0:
-                    kp = at[0]; k = (kp + 1) % 3 if kp < 3 or n == 1 else 0; at[0] = k
-                    new, nk = X[k], "X%d." % k + "%d"
-                else:
-                    kp, k = None, q + (3 if n == 6 else 0)
-                    new, nk = G[k], "G%d." % k + "%d"
-                tag[0] = "open%d%d" % (q, h)
-                lanes = LL >> h & 1; both = h == 1 and keys and not fused
-                if q == 0:
-                    o = pT[:, U0[h]:U0[h] + 128]
-                    if h == 0 and n != 4:
-                        lst = [(o, ES[:, 384:512], T.If[:], not lanes, 512)]
-                    else:
-                        lst = [(o, T.ones[0:32, :], T.CK[0:32, 0:128], not lanes, 128)] if h == 0 or not lanes else []
-                    lst += [(o, T.D01[:], A[cur][:, half(h)], False, 128)]
-                    if not lanes:
-                        mm(CKr + ["ES0", "If", "D01", "A%d" % cur], ["T%d" % h], lst)
-                        if h == 0 and n == 4:
-                            direct(0, X[3], "X3.%d", 1)
-                    elif h == 0:
-                        mm(CKr, ["T0"], [(pT[:, 128:256], T.CK[0:32, 256:384], T.CK[0:32, 0:128], True, 128)])
-                    else:
-                        const(1, 512, 256, 256, False)
-                    gather(h, NPQ[0], win, wr, offU[0], ["oU0.%d" % h], k, kp, "g0")
-                    if lanes:
-                        tag[0] = "d%d0" % h
-                        tr(h, new, allp(nk[:2]), 512 if both else E0[h], 2 if both else 1, 16 if both else 0)
-                        m = 256 if both else 128; lo = 512 if both else E0[h]; e = T.E2[:, 256 * h + m - 128:256 * h + m]
-                        shift(E2A >> h & 1, m, [], ["E2%d" % h], T.E2[:, 256 * h:256 * h + m], pT[:, lo:lo + m], 0.0, b=["T%d" % h])
-                        tag[0] = "d%d1" % h
-                        mm(CKr + ["ES0", "If", "D01", "A%d" % cur, "E2%d" % h], ["T%d" % h], [(o, e, T.If[:], True, 512)] + lst)
-                        if h == 0 and n == 4:
-                            direct(0, X[3], "X3.%d", 1)
-                    else:
-                        direct(h, new, nk, 0, "g0")
-                    tag[0] = "off%d" % h
-                    nstage(h, 8192, T.offU1, "oU1.%d" % h, n > 1 or M1 < 2)
-                    if h and fused:
-                        again()
-                    elif h:
-                        addP(new, nk, 0)
-                    continue
-                lst = [(pT[:, 128 + 384 * h:512 + 256 * h], T.ones[0:64, :], T.CK[0:64, 256 * h:384 + 128 * h], True, 384 - 128 * h),
-                       (pT[:, E0[h]:E0[h] + 128], A[cur][:, half(h)], T.Dm1[:], False, 128)]
-                if h == 0 and lanes:
-                    lst += [(pT[:, 128:256], T.nIf[:], T.E2[:, 0:128], False, 512)]
-                elif both and lanes:
-                    lst += [(pT[:, 512:640], T.If[:], T.E2[:, 256:384], False, 512)]
-                mm(CKr + ["A%d" % cur, "Dm1", "If", "nIf", "E2%d" % h], ["T%d" % h], lst)
-                if h == 0 and not lanes:
-                    tr(0, X[kp], allp("X%d" % kp), 128, 1, 8)
-                elif h and keys:
-                    tag[0] = "trr"
-                    tr(1, run, allp(rk[:2]), 512, 1, 16)
-                    tag[0] = "trg"
-                    if both and not lanes:
-                        tr(1, G[0], allp("G0"), 512, 1, 16)
-                gather(h, NPQ[1], win, wr, offU[1], ["oU1.%d" % h], k, kp, "g1")
-                if h == 0:
-                    tag[0] = "tr0"
-                    tr(0, new, allp(nk[:2]), 128, 3 if keys else 1, 0)
-                    tag[0] = "y0"
-                    for s in range(NY0):
-                        tag[0] = "y0%d" % s
-                        m = 2048 // NY0; ks = range(4 * s // NY0, 4 * (s + 1) // NY0)
-                        ts(m // 2, [nk % x for x in ks], ["y0.%d" % x for x in ks], T.y0[:, m * s:m * s + m], new[:, m * s:m * s + m], -YO - 127.5, None, Al.add)
-                else:
-                    addP(new, nk, 1)
-                    tag[0] = "tr1"
-                    if keys:
-                        tr(1, new, allp("G1"), 512, 2, 16)
-                    else:
-                        tr(1, new, allp(nk[:2]), 640, 1, 0)
-                    for s in range(4):
-                        tag[0] = "y1%d" % s
-                        shift(s >= YV, 512, [], ["y1.%d" % s], T.y1[:, 512 * s:512 * s + 512], Pb(s), -127.5 - (0 if n in (RH, 6) else YO), b=["P%d" % s])
-                tag[0] = "key%d" % h
-                if keys:
-                    tr(h, T["y%d" % h], allp("y%d" % h), K0[h], 1, 32, True)
-                tag[0] = "es%d" % h
-                if h == 0 or n == 6:
-                    escopy(h)
-                tag[0] = "end%d" % h
-                if n == 6:
-                    if h == 0:
-                        reduce256(new, nk, T.fo, "fo%d", RF)
-                    tag[0] = "img%d" % h
-                    turned(h)
-                    nstage(h, 2048, T.yi, "yi%d" % h, False)
-                    if h == 1:
-                        for s in range(4):
-                            tag[0] = "f%d" % s
-                            tt(512, ["y1.%d" % s], ["G2.%d" % s], T.G2[:, 512 * s:512 * s + 512], Pb(s), T.y1[:, 512 * s:512 * s + 512], Al.subtract, b=["P%d" % s])
-        arrange(first, (LAST if n == 6 else STEP if cur else EVEN).split())
-        for o in ops[first:]:
-            o["step"] = n
+                tag[0] = "img" + "ab"[h]
+                mm(["ES%d" % h, "If"], UB[h], [turn(h, EC[h])])
+                nstage(h, 2048, T.yi, "yi%d" % h, False)
+    tag[0] = "out"
     dma("s", 128, tabk(1), [], T.yent[:, 0:4096], T.tab1[0:128:16, 0:4096])
     dma("s", 128, tabk(1), [], T.yent[:, 4096:8192], T.tab1[1:128:16, 0:4096])
     dma("s", 128, tabk(1), [], T.yelen[:], T.tab1[2:128:16, 0:4096])
     dma("s", 128, ["yi0", "yi1"], [], T.yimg[:], T.yi[:])
     for k in range(8):
-        dma("s", 128, ["fo%d" % k if k < 4 else "G2.%d" % (k - 4)], [], T.yf[:, 512 * k:512 * k + 512], (T.fo if k < 4 else T.G2)[:, 512 * (k % 4):512 * (k % 4) + 512])
-    for o in ops:
-        for j, x in enumerate(o.get("mm", [])):
-            if not x[3] and (OPEN or j):
-                tail[o["b"][0]][5] = False
-            tail[o["b"][0]] = x
+        dma("s", 128, blk("fo", 512 * k, 512 * k + 512), [], T.yf[:, 512 * k:512 * k + 512], T.fo[:, 512 * k:512 * k + 512])
     return ops, nout
 
 
-def schedule(ops):
-    lw, rd, lb = {}, {}, {}
+def link(ops):
+    lw, rd, lb, tail = {}, {}, {}, {}
     for n, o in enumerate(ops):
         dep = {}
         for k in o["r"]:
@@ -637,52 +555,159 @@ def schedule(ops):
             if k in lb:
                 dep.setdefault(lb[k], False)
             lb[k] = n
+            for x in o.get("mm", []):
+                if not x[3]:
+                    tail[k][5] = False
+                tail[k] = x
         dep.pop(n, None)
         for k in o["r"]:
             rd.setdefault(k, []).append(n)
         for k in o["w"]:
             lw[k] = n; rd[k] = []
         o["dep"] = dep
-    succ = [[] for o in ops]
+
+
+def graph(ops):
+    eng = [o["e"] for o in ops]; dur = [o["t"] for o in ops]; last = list(range(len(ops))); edges = []
     for n, o in enumerate(ops):
-        for d in o["dep"]:
-            succ[d].append(n)
-    pr = [0.0] * len(ops)
-    for n in range(len(ops) - 1, -1, -1):
-        pr[n] = ops[n]["t"] + ops[n]["lat"] + SY + max([pr[s] for s in succ[n]] + [0.0])
+        if o["kb"]:
+            last[n] = len(eng); eng.append("w"); dur.append(o["kb"] / RATE); edges.append((n, last[n], o["lat"] - 0.5))
     for n, o in enumerate(ops):
-        k = (o["w"] + o["b"] + [""])[0]
-        if o["tag"]:
-            pr[n] = -n
-        elif k in FIRST:
-            pr[n] = 1000 - FIRST.index(k)
-        elif k in LATE:
-            pr[n] = pr[n] / 1000 - [x["tag"] for x in ops].index("window")
-    left = [len(o["dep"]) for o in ops]; last = {}
+        for d, data in o["dep"].items():
+            p = ops[d]; same = p["e"] == o["e"] and p["k"] == o["k"] == "c"
+            edges.append((last[d], n, (0.5 if p["kb"] else p["lat"]) + (SX if not same else SY if data and o["e"] != "p" else 0.0)))
+    return eng, dur, edges
+
+
+def first(ops, eng, dur, edges):
+    N = len(eng); seen = {}; where = {}; before = {}; named = set()
     for n, o in enumerate(ops):
-        if o.get("step", 0) >= STRICT and o["e"] != "x":
-            if o["e"] in last and last[o["e"]] not in o["dep"]:
-                succ[last[o["e"]]].append(n); left[n] += 1
-            last[o["e"]] = n
-    rdy = [0.0] * len(ops); free = {}
-    ready = [n for n in range(len(ops)) if left[n] == 0]; order = []; end = 0.0
+        k = (o["step"], o["tag"], o["e"]); seen[k] = seen.get(k, 0) + 1
+        o["nm"] = o["tag"] + ("" if seen[k] == 1 else "." * o["tag"][-1].isdigit() + str(seen[k])); where[(o["step"], o["nm"], o["e"])] = n
+    for e in START:
+        ends = [[where.get((int(x[0]), x[2:], e) if x[1] == ":" else (s, x, e)) for x in L.get(e, "").split()] for s, L in ((0, START), (6, END))]
+        line = [where.get((2 * k + 2 + (x[0] == "o") - 2 * {"+": 1, "-": -1}.get(x[-1], 0), x[2:].rstrip("+-"), e)) for k in range(-2, 4) for x in ROUND.get(e, "").split()]
+        line = [n for n in ends[0] + [n for n in line if n not in ends[0] + ends[1] and n is not None and ops[n]["step"]] + ends[1] if n is not None]
+        before.update(zip(line[1:], line)); named.update(line)
+    succ = [[] for e in eng]; pred = [[] for e in eng]; left = [0] * N; st = [0.0] * N; free = {}; seq = []
+    for a, b, d in edges:
+        succ[a].append((b, d)); pred[b].append(a); left[b] += 1
+    ready = [n for n in range(N) if not left[n]]; done = set()
     while ready:
-        best = min(ready, key=lambda n: (max(rdy[n], free.get(ops[n]["e"], 0.0)), -pr[n], n))
-        e0 = ops[best]["e"]; t0 = max(rdy[best], free.get(e0, 0.0)); d0 = ops[best]["t"]; p0 = pr[best]
-        for n in ready:
-            if ops[n]["e"] == e0 and rdy[n] < t0 + LOOK * d0 and pr[n] > p0:
-                best = n; p0 = pr[n]
-        ready.remove(best); o = ops[best]
-        st = max(rdy[best], free.get(e0, 0.0)); o["st"] = st
-        if e0 != "x":
-            free[e0] = st + o["t"]
-        fin = st + o["t"] + o["lat"]; end = max(end, fin); order.append(best)
-        for s in succ[best]:
-            rdy[s] = max(rdy[s], fin + (0.0 if e0 == ops[s]["e"] and (e0 == "p" or not ops[s]["dep"].get(best)) else SY))
-            left[s] -= 1
-            if left[s] == 0:
-                ready.append(s)
-    return order, end
+        n = min(ready, key=lambda n: (n in before and before[n] not in done, st[n], n)); ready.remove(n); done.add(n); seq.append(n)
+        if n in named:
+            st[n] = max(st[n], free.get(eng[n], 0.0)); free[eng[n]] = st[n] + dur[n]
+        for b, d in succ[n]:
+            st[b] = max(st[b], st[n] + dur[n] + d); left[b] -= 1
+            if not left[b]:
+                ready.append(b)
+    for n in reversed(seq):
+        if n not in named and succ[n]:
+            st[n] = min(st[b] - d for b, d in succ[n]) - dur[n]
+    for n in seq:
+        st[n] = max([st[n]] + [st[a] + 1e-4 for a in pred[n]])
+    return st
+
+
+def polish(eng, dur, edges, st):
+    N = len(eng); gap = {}
+    for a, b, d in edges:
+        gap[(a, b)] = max(gap.get((a, b), 0.0), d + dur[a])
+    succ = [[] for e in eng]; pred = [[] for e in eng]
+    for (a, b), d in gap.items():
+        succ[a].append((b, d)); pred[b].append((a, d))
+    order = sorted(range(N), key=lambda n: (st[n], n)); rnd = numpy.random.RandomState(SEED)
+
+    def heads():
+        st = [0.0] * N; free = {}
+        for n in order:
+            st[n] = max([st[a] + d for a, d in pred[n]] + [free.get(eng[n], 0.0) * (eng[n] != "x")]); free[eng[n]] = st[n] + dur[n]
+        return st
+    for t0 in [WIDTH / 2 * k for s in range(SWEEPS) for k in range(int(300 / WIDTH))]:
+        st = heads(); order.sort(key=lambda n: st[n]); tail = [0.0] * N; after = {}
+        for n in reversed(order):
+            tail[n] = max([tail[b] + d for b, d in succ[n]] + [dur[n] + after.get(eng[n], 0.0) * (eng[n] != "x")]); after[eng[n]] = tail[n]
+        W = [n for n in order if t0 <= st[n] < t0 + WIDTH]
+        if not W:
+            continue
+        i0 = order.index(W[0]); M = len(W); m = {n: i for i, n in enumerate(W)}; free = {}; after = {}; line = {}
+        head = [max([st[a] + d for a, d in pred[n] if a not in m] + [0.0]) for n in W]
+        rest = [max([tail[b] + d for b, d in succ[n] if b not in m] + [dur[n]]) for n in W]
+        sc = [[(m[b], d) for b, d in succ[n] if b in m] for n in W]; wait = [sum(a in m for a, d in pred[n]) for n in W]; du = [dur[n] for n in W]
+        for n in order[:i0]:
+            free[eng[n]] = st[n] + dur[n]
+        for n in reversed(order[i0 + M:]):
+            after[eng[n]] = tail[n]
+        for i, n in enumerate(W):
+            if eng[n] != "x":
+                line.setdefault(eng[n], []).append(i)
+        nx = [-1] * M; pv = [-1] * M
+
+        def relink(l):
+            for j, i in enumerate(l):
+                pv[i] = l[j - 1] if j else -1; nx[i] = l[j + 1] if j + 1 < len(l) else -1
+
+        def run():
+            left = [x + (p >= 0) for x, p in zip(wait, pv)]; s = list(head); by = [-1] * M
+            for e, l in line.items():
+                s[l[0]] = max(s[l[0]], free.get(e, 0.0))
+            q = [i for i in range(M) if not left[i]]
+            for i in q:
+                t = s[i]
+                for b, d in sc[i]:
+                    if t + d > s[b]:
+                        s[b] = t + d; by[b] = i
+                    left[b] -= 1
+                    if not left[b]:
+                        q.append(b)
+                b = nx[i]
+                if b >= 0:
+                    if t + du[i] >= s[b]:
+                        s[b] = t + du[i]; by[b] = i
+                    left[b] -= 1
+                    if not left[b]:
+                        q.append(b)
+            if len(q) < M:
+                return 1e9, q, []
+            v, i = max([(s[i] + rest[i], i) for i in range(M)] + [(s[l[-1]] + du[l[-1]] + after.get(e, 0.0), l[-1]) for e, l in line.items()])
+            on = []
+            while by[i] >= 0:
+                if pv[i] == by[i] and (W[by[i]], W[i]) not in gap:
+                    on.append(i)
+                i = by[i]
+            return v, q, on
+        for l in line.values():
+            relink(l)
+        cur, q, on = run(); best = (cur, q)
+        for it, (u, k, up, z) in enumerate(rnd.random_sample((MOVES, 4)).tolist()):
+            if not on:
+                break
+            x = on[int(u * len(on))]; l = line[eng[W[x]]]; i = l.index(x); k = (1, 1, 1, 2, 2, 3, 4, 6, 9)[int(9 * k)]; old = list(l)
+            if up < 0.5:
+                l.insert(max(i - k, 0), l.pop(i))
+            else:
+                l.insert(min(i - 1 + k, len(l) - 1), l.pop(i - 1))
+            relink(l); v, q, o2 = run()
+            if v - cur <= -(HEAT * (1 - it / MOVES) + 0.002) * math.log(z + 1e-12):
+                cur, on = v, o2; best = min(best, (v, q))
+            else:
+                l[:] = old; relink(l)
+        order[i0:i0 + M] = [W[i] for i in best[1]]
+    return heads()
+
+
+KEPT = []
+
+
+def schedule(ops):
+    if not KEPT:
+        eng, dur, edges = graph(ops)
+        st = polish(eng, dur, edges, first(ops, eng, dur, edges))
+        KEPT.append((st, max(t + d for t, d in zip(st, dur)) + 0.5))
+    st, end = KEPT[0]
+    for n, o in enumerate(ops):
+        o["st"] = st[n]
+    return sorted(range(len(ops)), key=lambda n: (st[n], n)), end
 
 
 def rank_program(g, core, T, topo):
@@ -690,6 +715,7 @@ def rank_program(g, core, T, topo):
     if rank is None:
         return
     ops, nout = build(T, topo, core, rank)
+    link(ops)
     order, end = schedule(ops)
     Q = {"g": g, "v": g.vector, "a": g.scalar, "p": g.tensor, "s": g.sync}
     cnt = {"v": 0, "a": 0, "p": 0, "g": 0}; seen = {e: {} for e in Q}; nd = [0]; total = {}

@@ -5,12 +5,13 @@ from concourse.mybir import AluOpType as Al, AxisListType, ActivationFunctionTyp
 F, B, H16, I, U = "float32", "bfloat16", "float16", "int32", "uint16"
 P = {
     "g": ((2, 2), (3, 4)),
-    "y": (2, 2),
-    "zv": (0, 3, 4),
-    "zo": ("01234567", "01723645", "07162534"),
-    "zb": ("123010101", "101230123", "101230123"),
-    "pb": ("2323", "0123", "01230123"),
-    "xa": (0, 2, 0),
+    "y": ((0, 1024, 2048), (0, 1024, 2048)),
+    "pa": 0, "ra": "vvv", "mb": ("0101", "0123"), "ia": 0, "ts": "", "kp": ((0, 128),), "ye": (("vvvv", "vvvv"),) * 3,
+    "zv": (2, 3, 4),
+    "zo": ("76012345", "76012345", "70615243"),
+    "zb": ("123010101", "123012301", "101230123"),
+    "pb": ("2323", "0123", "01230101"),
+    "xa": (1, 2, 0),
     "xo": "a", "au": "gob offb",
     "look": "v",
     "ha": "037",
@@ -19,28 +20,32 @@ P = {
     "rf": 4,
     "m1": 2,
 }
-CV, CA, CY, CP, CQ, SY, SX, GC = 0.05, 0.065, 0.00083, 0.00043, 0.03, 0.05, 0.22, 1.45
-RATE = 350.0
-WIDTH, SWEEPS, MOVES, HEAT, SEED = 16.0, 2, 12000, 0.15, 1
+CV, CA, CY, CP, CQ, SY, SX, GC = 0.05, 0.065, 0.00083, 0.00043, 0.035, 0.07, 0.19, 1.55
+RATE = 300.0
+WIDTH, SWEEPS, MOVES, HEAT, SEED = 16.0, 3, 12000, 0.08, 1
 START = {
     "s": "tci tw0 imgi cI0 cI1 cI2 ow0 ow1 ow2",
-    "g": "pi0 OH0 OH1 OH SA Ib CKd tf0 tf1 tf2 tf3 Dp0 Dp1 D01 SL G8 JB0 S01 Dm1 nI sez0 i16 DUM CKP0 CKP",
-    "v": "SA0 ones pi1 P2 M16 CK WD0 P0 owni seg0 CKc seg offI bits9 bits10 bits11 bitt11 bits12 bitt12 mones Mz0 ui0 uj0 offK0 ia ui1 uj1 offK1 ia2 H1 H2 1:scan 1:scan2 1:scan3 1:scan4 H4 "
-         "1:scan5 1:scan6 1:scan7 1:look H5 1:gob 1:gob2 1:gob3 H6 1:goa 1:goa2 1:goa3 1:g0a",
-    "a": "tw1 DL bits0 bits1 ccw bits2 WD bits3 cncw bits4 bits5 tch bits6 bits7 bits8 RR0 RR1 RR2 If imgf MK4 MK5 MK6 MK7 MK8 ib ib2 esb cmp0 H0 esa H3 H0.2 H7 H3.2 H7.2 1:xl 1:g0b",
-    "p": "Kt0 Kt1 Kt0.2 Kt0.3 Kt1.2 Kt1.3 Kw0 Kw1 ka kb ka2 kb2 H0 1:tub H3 1:scan 1:tua H7 1:gob 1:goa"}
-END = {}
+    "g": "pi0 OH0 OH1 OH SA Ib CKd tf0 tf1 tf2 tf3 Dp0 SL G8 JB0 DB0 DB S01 Dp1 D01 Dm1 nI sez0 sez i16 DUM RR40 RR41 RR4 OHb0 OHb1 OHb CKP0 CKP tg0 tg1 tg2 tg3 tg4 tg5 tg6 tg7 cmq",
+    "v": "SA0 ones pi1 P2 M16 CK WD0 P0 owni seg0 CKc seg offI bits9 bits10 bits11 bitt11 bits12 bitt12 mones Mz0 ui0 uj0 offK0 ia ui1 uj1 offK1 nmb ia2 H1 nma H2 1:scan 1:scan2 1:scan3 1:scan4 H4 "
+         "1:scan5 1:look H5 1:gob 1:gob2 H6 1:goa 1:goa2 1:goa3 1:g0a",
+    "a": "tw1 DL bits0 bits1 ccw bits2 WD bits3 cncw bits4 bits5 tch bits6 bits7 bits8 RR0 RR1 RR2 If imgf MK4 MK5 MK6 MK7 MK8 esb ib ib2 cmp0 H0 esa H3 H0.2 H7 H3.2 H7.2 1:xl 1:gob 1:g0b",
+    "p": "Kt0 Kt1 Kt0.2 Kt0.3 Kt1.2 Kt1.3 kb Kw0 Kw1 ka kb2 ka2 kb3 H0 1:tub H3 1:scan 1:tua H7 1:gob 1:goa"}
+END = {
+    "v": "look goa g0a z7 z6 g0a2 z5 z4 offa win g1a win2 win3 ring list ring2 list2 ring3 g1a2 g1a3 ya x ya2 x2 put nma x3 nmb f x4 img",
+    "a": "xl xo gob xr lv g0b z0 z0.2 z1 z1.2 z2 z2.2 z3 z3.2 g0b2 offb g1b g1b2 x g1b3 x2 g1b4 esa x3 esb f x4 nma f2 nmb f3 f4",
+    "p": "goa gob xr at opa opb z7 z0 z6 z1 da z2 z5 z3 z4 db da2 db2 oqa list oqa2 p p2 x oqb p3 x2 p4 tra trb x3 f x4 f2 f3 img img2 f4"}
 ROUND = {
-    "v": "e:scan e:scan2 o:list+ e:scan3 o:list2+ e:scan4 o:put+ e:scan5 e:scan6 e:scan7 e:look e:goa e:g0a e:g0a2 e:z7 e:offa e:g1a e:z5 e:z6 e:win e:g1a3 e:win2 e:g1a2 e:win3 e:x2 e:ya "
-         "e:list e:x e:list2 e:ya2 e:yb2 e:yb o:scan o:scan2 o:scan3 o:scan4 e:put o:scan5 o:scan6 o:scan7 o:look o:goa o:g0a o:g0a2 o:offa o:g1a o:g1a2 o:g1a3 o:ya o:x2 o:x o:ya2 o:yb "
-         "o:x3 o:x4 o:yb2 o:win o:win2",
-    "a": "o:len2+ o:own+ o:own2+ e:xl e:xo e:gob e:xr e:g0b e:z2 e:z0 e:z1 e:z0.2 e:z1.2 e:z2.2 e:g0b2 e:z3 e:z4 e:z4.2 e:z3.2 e:offb e:g1b4 e:g1b2 e:g1b3 e:g1b e:x2 e:x e:esa e:len e:esb "
-         "e:len2 e:own e:own2 o:xl o:xo o:gob o:xr o:g0b o:g0b2 o:z1 o:z0 o:z0.2 o:z3 o:z2 o:offb o:z2.2 o:z3.2 o:z1.2 o:g1b2 o:z4 o:g1b o:z4.2 o:g1b3 o:z5 o:z5.2 o:g1b4 o:z6 o:z6.2 o:z7 "
-         "o:z7.2 o:esa o:esb o:len",
-    "p": "o:z6+ o:p4+ o:p3+ o:z7+ o:keya+ o:trb+ o:trx2+ o:keyb+ o:list+ o:len+ e:tub e:scan e:pv e:tua e:goa e:gob e:xr e:oqa e:opa e:opb e:z0 e:z1 e:z2 e:da e:z7 e:db e:da2 e:z3 e:z6 e:z5 "
-         "e:z4 e:at e:db2 e:oqa2 e:p2 e:p4 e:p3 e:p e:list e:trx e:x2 e:oqb e:tra e:x e:trb e:keya e:trx2 e:keyb e:len o:pv o:tub o:scan o:tua o:gob o:goa o:xr o:opa o:at o:z0 o:z3 o:opb "
-         "o:z1 o:z2 o:db o:da o:da2 o:db2 o:oqa o:oqa2 o:oqb o:z4 o:p2 o:p o:trx o:tra o:z5"}
+    "v": "o:win3+ o:nmb+ o:nma+ e:scan e:scan2 o:list+ e:scan3 o:list2+ e:scan4 o:put+ e:scan5 e:look e:goa e:g0a e:z6 e:g0a2 e:z7 e:z5 e:offa e:win e:g1a3 e:g1a2 e:win2 e:g1a e:win3 e:x "
+         "e:ya2 e:list e:ya e:list2 e:x2 e:yb2 e:yb e:nmb e:nma o:scan o:scan2 o:scan3 o:scan4 e:put o:scan5 o:look o:goa o:g0a o:g0a2 o:z7 o:z6 o:offa o:win o:g1a o:g1a2 o:g1a3 o:ya o:x "
+         "o:ya2 o:yb o:x2 o:x3 o:yb2 o:win2",
+    "a": "o:esa2+ e:m o:len+ e:m2 o:nma+ o:nmb+ e:m3 o:len2+ e:m4 o:own+ o:own2+ e:xl e:scan e:xo e:gob e:xr e:g0b2 e:z0 e:z1 e:z0.2 e:z1.2 e:g0b e:z4 e:z2 e:z3 e:z2.2 e:z3.2 e:offb e:z4.2 "
+         "e:g1b3 e:g1b2 e:g1b e:g1b4 e:x e:x2 e:esb e:len e:esa e:esa2 e:nma e:nmb e:len2 o:m e:own2 e:own o:m2 o:m3 o:m4 o:xl o:scan o:xo o:gob o:xr o:g0b o:z1 o:z1.2 o:g0b2 o:z0 o:z0.2 o:z3 o:z3.2 o:offb "
+         "o:z2 o:g1b o:g1b2 o:x o:z2.2 o:g1b3 o:g1b4 o:z5 o:z4 o:z4.2 o:z5.2 o:esb o:esa",
+    "p": "e:m e:m2 e:m3 o:len+ e:m4 e:scan e:pv e:tub e:tua e:goa e:gob e:xr e:oqa e:opa e:z6 e:at e:z1 e:z0 e:da e:z7 e:opb e:z3 e:z4 e:z5 e:da2 e:z2 e:db e:db2 e:p2 e:p4 e:p3 e:trx e:oqb "
+         "e:p e:oqa2 e:list e:tra e:x e:x2 e:trb e:keya e:trx2 e:keyb e:len o:m o:m2 o:tub o:tua o:scan o:m3 o:m4 o:pv o:gob o:goa o:xr o:at o:opb o:opa o:z7 o:z0 o:z1 o:oqa o:da o:z6 o:db o:z3 o:da2 o:db2 "
+         "o:z2 o:p o:p2 o:trx o:oqb o:x o:z5 o:oqa2 o:tra o:p3 o:z4 o:p4 o:tra2 o:keya o:trb o:trx2 o:keyb o:list"}
 MG = 12582912.0
+TO = 2112.0
 YO = 49152.0
 RC = -255.0 / 512
 
@@ -53,7 +58,7 @@ SCRATCH = {
     "tw": _sb(4096, B), "Hw": _sb(16384, B), "bits": _sb(4096, B), "tab0": _sb(4480, F), "tab1": _sb(4480, F),
     "X00": _sb(2048, H16), "X01": _sb(2048, H16), "X10": _sb(2048, H16), "X11": _sb(2048, H16), "M0": _sb(2048, H16), "M1": _sb(2048, B),
     "G0": _sb(2048, B), "G1": _sb(2048, B), "y0": _sb(2048, B), "y1": _sb(2048, B), "fo": _sb(4096, B), "CKP": _sb(512, B),
-    "imgi": _sb(256, I), "imgf": _sb(256, F), "offI": _sb(256, U), "tci": _sb(1024, I), "tch": _sb(1024, H16), "offK": _sb(256, U),
+    "imgi": _sb(256, I), "imgf": _sb(256, H16), "offI": _sb(256, U), "tci": _sb(1024, I), "tch": _sb(1024, H16), "offK": _sb(256, U),
     "cmpI": _sb(768, I), "cmp": _sb(768, F), "cmq": _sb(768, F), "land0": _sb(768, F), "land1": _sb(768, F), "land2": _sb(768, F),
     "lv2": _sb(256, H16), "lv4": _sb(256, H16), "lv6": _sb(256, F), "lo2": _sb(16, U), "lo4": _sb(16, U), "lo6": _sb(16, U),
     "owni": _sb(256, I), "A0": _sb(256, H16), "A1": _sb(256, H16), "V6": _sb(256, F), "XR0": _sb(256, H16), "XR1": _sb(256, H16), "XL0": _sb(256, B), "XL1": _sb(256, B),
@@ -61,8 +66,8 @@ SCRATCH = {
     "Ib": _sb(128, B), "If": _sb(128, F), "nI": _sb(128, B), "ones": _sb(128, B), "mones": _sb(128, B),
     "Dp0": _sb(128, B), "Dp1": _sb(128, B), "Dm1": _sb(128, B), "D01": _sb(128, B), "S01": _sb(128, B), "DB": _sb(128, B),
     "WD": _sb(144, B), "SA": _sb(576, B), "RR": _sb(40, B), "CK": _sb(896, B), "seg": _sb(256, F), "sez": _sb(512, F), "JB": _sb(2, F), "DUM": _sb(16, F),
-    "ES": _sb(512, F), "Rm": _sb(256, I), "oj": _sb(16, I), "offW": _sb(16, U),
-    "wi": _sb(16, I), "wj": _sb(16, I), "Wz": _sb(256, F), "Wn": _sb(256, B), "MK": _sb(256, F), "MB": _sb(256, F), "offG": _sb(16, U), "OH": _sb(8, F), "Mz": _sb(256, H16),
+    "run": _sb(128, F), "pn": _sb(256, I), "pm": _sb(256, I), "PF": _sb(256, H16), "Rm": _sb(256, I), "oj": _sb(16, I), "offW": _sb(16, U),
+    "wj": _sb(16, F), "Wz": _sb(256, F), "Wn": _sb(256, B), "MK": _sb(256, F), "MB": _sb(256, F), "offG": _sb(16, U), "OH": _sb(8, F), "Mz": _sb(256, H16),
     "offO": _sb(16, U), "offU0": _sb(256, U), "offU1": _sb(256, U), "offS0": _sb(16, U), "offS1": _sb(16, U),
     "ui": _sb(256, I), "uj": _sb(256, I), "yi": _sb(256, F), "OHb": _sb(8, B), "tn": _sb(64, F), "cnt": _sb(16, F), "junk": _sb(4096, B), "zs": _sb(4096, F),
     "pT": ("psum", [128, 1536], F), "pS": ("psum", [128, 512], F), "pQ": ("psum", [128, 2048], F),
@@ -149,11 +154,10 @@ def build(T, topo, core, rank):
         return "Q%d" % k, T.pQ[:, 512 * k:512 * k + 512]
 
     tab = [T.tab0, T.tab1]; A = [T.A0, T.A1]; XR = [T.XR0, T.XR1]; XL = [T.XL0, T.XL1]
-    pT = T.pT; pS = T.pS; ES = T.ES; offU = [T.offU0, T.offU1]; offS = [T.offS0, T.offS1]; RR = T.RR; CK = T.CK
+    pT = T.pT; pS = T.pS; offU = [T.offU0, T.offU1]; offS = [T.offS0, T.offS1]; RR = T.RR; CK = T.CK
     half = lambda h: slice(128 * h, 128 * h + 128)
-    U0, E0, K0 = (640, 1024), (128, 1152), (384, 512)
+    U0, E0, K0 = (896, 1024), (128, 1152), (384, 512)
     UB, EB, KB = ("T1", "T2"), ("T0", "T2"), ("T0", "T1")
-    EC = (256, 128)
     reg = lambda lo, n=128: pT[:, lo:lo + n]
     blk = lambda nm, lo=0, hi=2048: ["%s.%d" % (nm, k) for k in range(lo // 256, hi // 256)]
 
@@ -179,7 +183,7 @@ def build(T, topo, core, rank):
     sel(128, ["mones"], ["nI"], T.nI[:], T.mones[:], [[-1, 128]], Al.is_equal, 0.0, 0, 1)
     ms(448, ["CK"], CK[0:64, :], 0.0)
     ms(64, ["CKc"], CK[32:33, 256:384], 4096 * YO, r=["CK"])
-    iota(256, ["CKd"], CK[0:1, 384:640], [[-128, 2], [1, 128]], 128, 0, r=["CK"])
+    iota(256, ["CKd"], CK[0:1, 384:640], [[1, 256]], 0, 0, r=["CK"])
     ms(64, ["CKf"], CK[0:1, 640:768], 16 * YO, r=["CK"]); ms(64, ["CKe"], CK[32:33, 640:768], -YO / 256, r=["CKf"])
     ms(64, ["CKg"], CK[0:1, 768:896], RC, r=["CK"])
     ms(288, ["SA0"], T.SA[0:32, :], 0.0)
@@ -207,23 +211,24 @@ def build(T, topo, core, rank):
     act(1, ["P0"], ["ccw"], c("cw"), T.POW[:, 11:12], Af.Identity, scale=8.0)
     act(1, ["P0"], ["cncw"], c("ncw"), T.POW[:, 11:12], Af.Identity, scale=-8.0)
     ms(72, ["WD0"], T.WD[:], 0.0)
-    iota(8, ["OH0"], T.OH[:], [[0, 8]], 1, 0)
-    sel(8, ["OH0"], ["OH1"], T.OH[:], T.OH[:], [[-16, 8]], Al.is_ge, 0.0, 0, 1)
-    sel(8, ["OH1"], ["OH"], T.OH[:], T.OH[:], [[16, 8]], Al.is_ge, 0.0, 15, -1)
+    for nm, out, x in (("OH", T.OH[:], 1), ("OHb", T.OHb[:], -8192), ("RR4", RR[:, 32:40], 256)):
+        iota(8, [nm + "0"], out, [[0, 8]], x, 0)
+        sel(8, [nm + "0"], [nm + "1"], out, out, [[-16, 8]], Al.is_ge, 0.0, 0, 1)
+        sel(8, [nm + "1"], [nm], out, out, [[16, 8]], Al.is_ge, 0.0, 15, -1)
     act(4, ["OH"], ["cod"], T.POW[:, 32:36], T.OH[:, 1:8:2], Af.Copy, acc=c("od"))
     if P["xo"] == "v":
         cp(1, ["cod"], ["odb"], T.odb[:, 0:1], c("od"))
     act(8, ["OH", "ccw", "WD0"], ["WD"], T.WD[:, 15:143:16], T.OH[:], Af.Identity, scale=c("cw"))
-    cp(256, ["imgi"], ["offI"], T.offI[:], T.imgi[:]); act(256, ["imgi"], ["imgf"], T.imgf[:], T.imgi[:], Af.Copy)
-    for k, w in enumerate(("cw", "ncw", -256.0, "cw", 256.0)):
+    cp(256, ["imgi"], ["offI"], T.offI[:], T.imgi[:]); act(256, ["imgi"], ["imgf"], T.imgf[:], T.imgi[:], Af.Identity, bias=-2048.0)
+    for k, w in enumerate(("cw", "ncw", -256.0, "cw")):
         act(8, ["OH", "ccw", "cncw"], ["RR%d" % k], RR[:, 8 * k:8 * k + 8], T.OH[:], Af.Identity, scale=c(w) if isinstance(w, str) else w)
     act(12, ["M16"], ["cdv"], T.POW[:, 36:48], T.M16[:, 4:16], Af.Identity, scale=-2.0 / 4096, acc=c("dv"))
     for nm, k, sc, bi in (("j4", 3, 4096.0, 0.0), ("b2", 2, 2.0 ** 20, c("j4"))):
         act(1, ["M16", "cj4"], ["c" + nm], c(nm), T.M16[:, k:k + 1], Af.Identity, bias=bi, scale=sc)
     act(1, ["cdv", "cb2"], ["cb"], c("b"), c("dv"), Af.Identity, bias=c("b2"), scale=2.0 ** 32)
-    act(8, ["OH"], ["OHb"], T.OHb[:], T.OH[:], Af.Identity, scale=-8192.0)
     act(128, ["Ib"], ["If"], T.If[:], T.Ib[:], Af.Copy)
-    act(128, ["Ib", "cdv"], ["DB"], T.DB[:], T.Ib[:], Af.Identity, scale=c("dv"))
+    sel(128, ["Ib"], ["DB0"], T.DB[:], T.Ib[:], [[-1, 128]], Al.not_equal, -2.0 / 4096, 0, 1)
+    sel(128, ["DB0"], ["DB"], T.DB[:], T.DB[:], [[0, 8], [1, 16]], Al.is_ge, 0.0, -4, 0)
     sel(128, ["Ib"], ["S01"], T.S01[:], T.Ib[:], [[0, 8], [-1, 16]], Al.is_ge, 0.0, 1, 0)
     rows = [[-16, 8], [0, 16]]
     for nm, src, k in (("Dp0", "ones", 0), ("Dp1", "ones", 1), ("Dm1", "mones", 1)):
@@ -231,7 +236,7 @@ def build(T, topo, core, rank):
     sel(128, ["Dp1"], ["D01"], T.D01[:], T.Dp1[:], rows, Al.not_equal, -1.0, 0, 1)
     sel(8, ["ones"], ["SL"], T.SL[:], T.ones[:, 0:8], [[-16, 8]], Al.is_equal, 0.0, -2, 1)
     ms(256, ["seg0"], T.seg[:], 0.0); ms(16, ["seg"], T.seg[:, 0:256:16], 2.0 ** 23, r=["seg0"])
-    iota(512, ["sez0"], T.sez[:], [[0, 512]], 0, 0); ms(2, ["sez"], T.sez[:, 0:512:256], 2.0 ** 40, r=["sez0"])
+    iota(512, ["sez0"], T.sez[:], [[0, 512]], 0, 0); sel(2, ["sez0"], ["sez"], T.sez[:, 0:512:256], T.sez[:, 0:512:256], [[0, 2]], Al.not_equal, 2.0 ** 40, 0, 0)
     act(16, ["M16"], ["MK4"], T.MK[:, 0:16], T.M16[:], Af.Copy)
     for s in range(4, 8):
         act(1 << s, ["MK%d" % s], ["MK%d" % (s + 1)], T.MK[:, 1 << s:2 << s], T.MK[:, 0:1 << s], Af.Copy)
@@ -310,9 +315,10 @@ def build(T, topo, core, rank):
     def column(h, start=False):
         return [(reg(K0[h]), T.ones[0:32, :], CK[0:32, 384 + 128 * h:512 + 128 * h], start, 128)]
 
-    def tr(b, src, lo, n, r0, more=()):
-        mm(blk(src) + ["RR%d" % k for k in range(r0, r0 + n)] + ["CKd", "ones"], b,
-           [(pT[:, lo + i:lo + 128 * n:16], T[src][:, i:2048:16], RR[:, 8 * r0:8 * (r0 + n)], False, 64) for i in range(16)] + list(more))
+    def tr(b, src, lo, n, r0, more=(), parts=None):
+        for l0, l1 in parts or (((0, 96), (96, 128)) if tag[0] in P["ts"].split() else ((0, 128),)):
+            mm(blk(src, 16 * l0, 16 * l1) + ["RR%d" % k for k in range(r0, r0 + n)] + ["CKd", "ones"], b,
+               [(pT[l0:l1, lo + i:lo + 128 * n:16], T[src][:, 16 * l0 + i:16 * l1:16], RR[:, 8 * r0:8 * (r0 + n)], False, min(64, l1 - l0)) for i in range(16)] + list(more) * (l1 == 128))
 
     def direct(h, src):
         for s in range(2):
@@ -322,12 +328,18 @@ def build(T, topo, core, rank):
     def const(lo, n, c0, rows, start=True):
         return (reg(lo, n), T.ones[0:rows, :], CK[0:rows, c0:c0 + n], start, n)
 
-    def turn(h, lo):
-        return (reg(U0[h]), ES[:, lo:lo + 128], T.If[:], True, 512)
+    def turn(h):
+        mm(["PF%d" % h, "Ib"], UB[h], [(reg(U0[h]), T.PF[:, half(h)], T.Ib[:], True, 128)])
 
-    def points(h):
-        tag[0] = "es" + "ab"[h]; n = 256 - 128 * h
-        act(n, [], ["ES%d" % h], ES[:, EC[h]:EC[h] + n], reg(E0[h], n), Af.Identity, bias=RC, b=[EB[h]])
+    def points(h, more):
+        tag[0] = "es" + "ab"[h]; sl = half(h); x = "%d" % h; raw = "pn" if tag[1] else "pm"
+        act(128, [], [raw + x], T[raw][:, sl], reg(E0[h]), Af.Identity, bias=RC + 2048, b=[EB[h]])
+        if more and h == 0:
+            act(128, [], ["run"], T.run[:], reg(256), Af.Identity, bias=RC, b=["T0"])
+        tag[0] = "nm" + "ab"[h]
+        if tag[1]:
+            ts(128, ["pn" + x], ["pm" + x], T.pm[:, sl], T.pn[:, sl], 4095, None, Al.bitwise_and)
+        act(128, ["pm" + x], ["PF" + x], T.PF[:, sl], T.pm[:, sl], Af.Identity, bias=-2048.0)
 
     def nstage(h, add, out, key, plain):
         o = reg(U0[h]); sl = half(h); b = [UB[h]]
@@ -340,27 +352,27 @@ def build(T, topo, core, rank):
             ts(128, ["ui%d" % h], ["uj%d" % h], T.uj[:, sl], T.ui[:, sl], 4095, None, Al.bitwise_and)
             shift(tag[0] in P["au"], 128, ["uj%d" % h], [key], out[:, sl], T.uj[:, sl], 0.0)
 
-    def reduce256(src, out, ra, banks):
+    def reduce256(h, src, out, ra, banks):
         for k, (lo, hi) in enumerate(cuts(4)):
             bk, pk = bank(banks[k])
-            mm(blk(src, lo, hi) + blk("y0", lo, hi) + ["Ib", "nI"], bk, [(pk, T.Ib[:], T[src][:, lo:hi], True, 512), (pk, T.nI[:], T.y0[:, lo:hi], False, 512)])
+            mm(blk(src, lo, hi) + blk("y%d" % h, lo, hi) + ["Ib", "nI"], bk, [(pk, T.Ib[:], T[src][:, lo:hi], True, 512), (pk, T.nI[:], T["y%d" % h][:, lo:hi], False, 512)])
             shift(k < ra, 512, [], blk(out, lo, hi), T[out][:, lo:hi], pk, -YO, b=[bk])
 
     def carries(h, src):
         tag[0] = "y" + "ab"[h]
-        for lo, hi in cuts(P["y"][h]):
-            ts((hi - lo) // 2, blk(src, lo, hi), blk("y%d" % h, lo, hi), T["y%d" % h][:, lo:hi], T[src][:, lo:hi], -YO - 127.5, None, Al.add)
+        for lo, hi, e in zip(P["y"][h], P["y"][h][1:], P["ye"][kind][h]):
+            shift(e == "a", (hi - lo) // (1 + (e == "v")), blk(src, lo, hi), blk("y%d" % h, lo, hi), T["y%d" % h][:, lo:hi], T[src][:, lo:hi], -YO - 127.5)
 
     for h in range(2):
         tag[0] = "i" + "ab"[h]
         gather(h, 2, T.tw[:], ["tw0", "tw1"], T.offI, ["offI"], "X%d0" % h)
     tag[0] = "ka"
-    mm(["CK", "ones", "imgf", "If"], "T0", [const(128, 384, 0, 32), (reg(E0[0]), T.imgf[:, half(0)], T.If[:], False, 512)])
+    mm(["CK", "ones", "imgf", "Ib"], "T0", [const(128, 384, 0, 32), (reg(E0[0]), T.imgf[:, half(0)], T.Ib[:], False, 128)])
     tr("T0", "X00", 256, 2, 1, column(0))
-    points(0)
+    points(0, True)
     tag[0] = "kb"
-    mm(["imgf", "If"], "T2", [(reg(E0[1]), T.imgf[:, half(1)], T.If[:], True, 512)])
-    points(1)
+    mm(["imgf", "Ib"], "T2", [(reg(E0[1]), T.imgf[:, half(1)], T.Ib[:], True, 128)])
+    points(1, True)
     tag[0] = "kb"
     mm(["CKd", "ones"], "T1", column(1, True))
     tr("T1", "X10", K0[1], 1, 2)
@@ -371,28 +383,29 @@ def build(T, topo, core, rank):
         keys = n < 6
         tag[1] = n
         Ak, Ao = "A%d" % cur, "A%d" % old
-        if n == 4:
-            tag[0] = "m"
-            reduce256("X0%d" % old, "X0%d" % cur, 4, "2323")
+        back = [n == 4, n == 3]
+        for h in range(2):
+            if back[h]:
+                tag[0] = "m"
+                reduce256(h, "X%d%d" % (h, old), "X%d%d" % (h, cur), 4, P["mb"][h])
         tag[0] = "tub"
-        mm(["ES1", "If"], UB[1], [turn(1, EC[1])])
+        turn(1)
         tag[0] = "scan"
         scan(256, ["seg"], ["Rm"], T.Rm[:], T.seg[:], reg(384, 256), ["T0", "T1"])
         ts(16, ["Rm"], ["oj"], T.oj[:], T.Rm[:, 15:256:16], 255, None, Al.bitwise_and)
         cp(16, ["oj"], ["offW"], T.offW[:], T.oj[:])
-        tt(256 * GC, ["ES0", "ES1", "offW", "MK8"], ["Wz"], T.Wz[:], ES[:, 128:384].indirect(T.offW[:]), T.MK[:], Al.mult)
+        tt(256 * GC, ["pm0", "pm1", "offW", "MK8"], ["Wz"], T.Wz[:], T.pm[:].indirect(T.offW[:]), T.MK[:], Al.mult)
         mm(["Wz", "OH"], "S", [(pS[:, 8 * h:8 * h + 8], T.Wz[:, half(h)], T.OH[:], True, 256) for h in range(2)])
-        ts(16, [], ["wi"], T.wi[:], pS[:, 0:16], 2048.0 if n > 1 else 0.0, None, Al.add, b=["S"])
-        ts(16, ["wi"], ["wj"], T.wj[:], T.wi[:], 4095, None, Al.bitwise_and)
-        cp(16, ["wj"], ["oO"], T.offO[:], T.wj[:])
+        cp(16, [], ["oO"], T.offO[:], pS[:, 0:16], b=["S"])
+        act(16, [], ["wj"], T.wj[:], pS[:, 0:16], Af.Copy, b=["S"])
         tag[0] = "look"
         shift(P["look"] == "a", 256 * GC, tabk(tb) + ["oO"], [Ak], A[cur][:], tab[tb][:, 0:4096].indirect(T.offO[:]), 0.0)
         tag[0] = "tua"
-        mm(["ES0", "If"], UB[0], [turn(0, EC[0])])
+        turn(0)
         for h in range(2):
             tag[0] = "go" + "ab"[h]
             mm(["Dp0", Ak], UB[h], [(reg(U0[h]), T.Dp0[:], A[cur][:, half(h)], False, 128)])
-            nstage(h, 2048 if n == 1 else 8192, T.offU0, "oU0.%d" % h, n > 1)
+            nstage(h, 4096, T.offU0, "oU0.%d" % h, n > 1)
         tag[0] = "xl"
         act(256 * GC, bitsr + ["oO", "cb"], ["XL0"], XL[0][:], T.bits[:].indirect(T.offO[:]), Af.Identity, bias=c("b"), scale=-2.0 ** 14)
         tag[0] = "xo"
@@ -436,7 +449,7 @@ def build(T, topo, core, rank):
         tag[0] = "list"
         mm(["Wn", "OHb", "If", "DUM"], "S", [(LS, T.If[:], T.DUM[:], True, 256)] + [(pS[:, 48 + 8 * h:56 + 8 * h], T.Wn[:, half(h)], T.OHb[:], False, 64) for h in range(2)])
         tt(16, ["wj"], ["t9"], tn(3), LS, T.wj[:], Al.max, b=["S"])
-        cp(16, ["t9"], ["oS%d" % cur], offS[cur][:], tn(3))
+        cp(16, ["t9"], ["offS%d" % cur], offS[cur][:], tn(3))
         if keys:
             tag[0] = "len"
             act(16, ["d"], ["z"], tn(0), tn(1), Af.Relu)
@@ -445,9 +458,16 @@ def build(T, topo, core, rank):
             tag[0] = "own"
             ownkeys()
         land = T["land%d" % ho]
-        if cur == 1:
+
+        def put(tb, off, val):
             tag[0] = "put"
-            cp(1000, ["oS1", "XR1"], tabk(tb), tab[tb][:].indirect(offS[1][:]), XR[1][:])
+            if P["pa"] and keys:
+                act(256, [val], ["V6"], T.V6[:], T[val][:], Af.Identity, bias=TO)
+                act(1000, [off, "V6"], tabk(tb), tab[tb][:].indirect(T[off][:]), T.V6[:], Af.Silu)
+            else:
+                cp(1000, [off, val], tabk(tb), tab[tb][:].indirect(T[off][:]), T[val][:])
+        if cur == 1:
+            put(tb, "offS1", "XR1")
             tag[0] = "ring"
             for q in range(3):
                 dma("s", 128, tabk(tb), ["cmp%d" % q], T.cmp[:, 256 * q:256 * q + 256], tab[tb][q:128:16, 0:4096])
@@ -458,21 +478,22 @@ def build(T, topo, core, rank):
                 unpack(land, "land%d." % ho + "%d", 1 - tb)
         else:
             tag[0] = "lo"
-            send(n - 2, 4, ["oS0"], ["lo%d" % n], T["lo%d" % n][:], offS[0][:])
+            send(n - 2, 4, ["offS0"], ["lo%d" % n], T["lo%d" % n][:], offS[0][:])
             tag[0] = "ring"
             if n == 6:
-                act(768, ["land2.0", "land2.1", "land2.2"], ["cmq0", "cmq1", "cmq2"], T.cmq[:], T.land2[:], Af.Identity, bias=2048.0)
+                for q in range(3):
+                    shift(P["ra"][q] == "a", 256, ["land2.%d" % q], ["cmq%d" % q], T.cmq[:, 256 * q:256 * q + 256], land[:, 256 * q:256 * q + 256], 2048.0)
                 unpack(T.cmq, "cmq%d", 1 - tb)
-            tag[0] = "put"
-            cp(1000, ["lo%d" % n, "lv%d" % n], tabk(1 - tb), tab[1 - tb][:].indirect(T["lo%d" % n][:]), T["lv%d" % n][:])
-        Xo, Xn = ["X%d%d" % (h, old) for h in range(2)], ["X%d%d" % (h, cur) for h in range(2)]
+            put(1 - tb, "lo%d" % n, "lv%d" % n)
+        Xn = ["X%d%d" % (h, cur) for h in range(2)]; Xo = [Xn[h] if back[h] else "X%d%d" % (h, old) for h in range(2)]
         plain = [n > 1 or q >= P["m1"] for q in range(2)]
         win = [(T.Hw[:], Hxr) if x else (T.Hw[:, 0:4096], Hr) for x in plain]
         for h in range(2):
             z = "ab"[h]; tag[0] = "op" + z
-            mm([Ak, "D01", "If", "ES0", "CKg", "ones"], UB[h], [const(U0[1], 128, 768, 32) if h else turn(0, 384), (reg(U0[h]), T.D01[:], A[cur][:, half(h)], False, 128)])
+            mm([Ak, "D01", "If", "CKg", "ones"] + ["run"] * (1 - h), UB[h],
+               [const(U0[1], 128, 768, 32) if h else (reg(U0[0]), T.run[:], T.If[:], True, 512), (reg(U0[h]), T.D01[:], A[cur][:, half(h)], False, 128)])
             tag[0] = "g0" + z
-            gather(h, P["g"][0][h], win[0][0], win[0][1], offU[0], ["oU0.%d" % h], "M%d" % h, None if h else Xn[0] if n == 4 else Xo[0])
+            gather(h, P["g"][0][h], win[0][0], win[0][1], offU[0], ["oU0.%d" % h], "M%d" % h, None if h else Xo[0])
             tag[0] = "d" + z
             direct(h, "M%d" % h)
             tag[0] = "off" + z
@@ -494,26 +515,25 @@ def build(T, topo, core, rank):
             tag[0] = "keya"
             if keys:
                 tr("T0", "y0", K0[0], 1, 4, column(0))
-        points(0)
+        points(0, keys)
         tag[0] = "oqb"
         mm([Ak, "Dm1"], "T2", [(reg(E0[1]), A[cur][:, half(1)], T.Dm1[:], True, 128)])
         tag[0] = "g1b"
         gather(1, P["g"][1][1], win[1][0], win[1][1], offU[1], ["oU1.1"], "G1")
         tag[0] = "trb"
         tr("T2", "G1", E0[1], 1, 0)
-        points(1)
+        points(1, keys)
         for k, (lo, hi) in enumerate(cuts(4)):
             tag[0] = "p"; bk, pk = bank(P["pb"][kind][k]); G = T.G1[:, lo:hi]; Y = T.y1[:, lo:hi]; yk = blk("y1", lo, hi); onv = keys and k >= P["xa"][kind]
-            mm(blk(Xo[1], lo, hi) + blk("M1", lo, hi) + ["Ib", "nI", "ones", "CKP"] + yk * (n == 4), bk,
-               [(pk, T.Ib[:], T[Xo[1]][:, lo:hi], True, 512), (pk, T.Ib[:], T.M1[:, lo:hi], False, 512)] + [(pk, T.nI[:], Y, False, 512)] * (n == 4) +
-               [(pk, T.ones[0:32, :], T.CKP[0:32, :], False, 512)] * (n == 4 and onv or not keys))
+            mm(blk(Xo[1], lo, hi) + blk("M1", lo, hi) + ["Ib"] + ["ones", "CKP"] * (not keys), bk,
+               [(pk, T.Ib[:], T[Xo[1]][:, lo:hi], True, 512), (pk, T.Ib[:], T.M1[:, lo:hi], False, 512)] + [(pk, T.ones[0:32, :], T.CKP[0:32, :], False, 512)] * (not keys))
             tag[0] = "x"
             if onv:
                 tt(512, blk("G1", lo, hi), blk(Xn[1], lo, hi), T[Xn[1]][:, lo:hi], pk, G, Al.add, b=[bk])
                 continue
             mm(blk("G1", lo, hi) + ["Ib"], bk, [(pk, T.Ib[:], G, False, 512)])
             if keys:
-                shift(True, 512, [], blk(Xn[1], lo, hi), T[Xn[1]][:, lo:hi], pk, -YO if n == 4 else 0.0, b=[bk])
+                act(512, [], blk(Xn[1], lo, hi), T[Xn[1]][:, lo:hi], pk, Af.Copy, b=[bk])
             else:
                 shift(True, 512, [], yk, Y, pk, -127.5, b=[bk])
                 tt(512, yk, blk("fo", 2048 + lo, 2048 + hi), T.fo[:, 2048 + lo:2048 + hi], pk, Y, Al.subtract, b=[bk])
@@ -521,16 +541,17 @@ def build(T, topo, core, rank):
             carries(1, Xn[1])
             tag[0] = "trx"
             mm(["CKc", "ones"], "T1", [const(K0[1], 128, 256, 64)])
-            tr("T1", Xn[1], K0[1], 1, 2)
-            tag[0] = "keyb"
-            tr("T1", "y1", K0[1], 1, 4, column(1))
+            for part in P["kp"]:
+                tag[0] = "trx"
+                tr("T1", Xn[1], K0[1], 1, 2, (), [part])
+                tag[0] = "keyb"
+                tr("T1", "y1", K0[1], 1, 4, column(1), [part])
         else:
             tag[0] = "f"
-            reduce256(Xn[0], "fo", P["rf"], P["pb"][kind][4:])
-            for h in range(2):
-                tag[0] = "img" + "ab"[h]
-                mm(["ES%d" % h, "If"], UB[h], [turn(h, EC[h])])
-                nstage(h, 2048, T.yi, "yi%d" % h, False)
+            reduce256(0, Xn[0], "fo", P["rf"], P["pb"][kind][4:])
+            tag[0] = "img"
+            turn(0); turn(1)
+            shift(P["ia"], 256, [], ["yi0", "yi1"], T.yi[:], reg(U0[0], 256), 2048.0, b=UB)
     tag[0] = "out"
     dma("s", 128, tabk(1), [], T.yent[:, 0:4096], T.tab1[0:128:16, 0:4096])
     dma("s", 128, tabk(1), [], T.yent[:, 4096:8192], T.tab1[1:128:16, 0:4096])
@@ -585,7 +606,7 @@ def first(ops, eng, dur, edges):
         k = (o["step"], o["tag"], o["e"]); seen[k] = seen.get(k, 0) + 1
         o["nm"] = o["tag"] + ("" if seen[k] == 1 else "." * o["tag"][-1].isdigit() + str(seen[k])); where[(o["step"], o["nm"], o["e"])] = n
     for e in START:
-        ends = [[where.get((int(x[0]), x[2:], e) if x[1] == ":" else (s, x, e)) for x in L.get(e, "").split()] for s, L in ((0, START), (6, END))]
+        ends = [[where.get((int(x[0]), x[2:], e) if ":" in x else (s, x, e)) for x in L.get(e, "").split()] for s, L in ((0, START), (6, END))]
         line = [where.get((2 * k + 2 + (x[0] == "o") - 2 * {"+": 1, "-": -1}.get(x[-1], 0), x[2:].rstrip("+-"), e)) for k in range(-2, 4) for x in ROUND.get(e, "").split()]
         line = [n for n in ends[0] + [n for n in line if n not in ends[0] + ends[1] and n is not None and ops[n]["step"]] + ends[1] if n is not None]
         before.update(zip(line[1:], line)); named.update(line)
@@ -602,7 +623,7 @@ def first(ops, eng, dur, edges):
             if not left[b]:
                 ready.append(b)
     for n in reversed(seq):
-        if n not in named and succ[n]:
+        if n not in named and succ[n] and eng[n] in "vap":
             st[n] = min(st[b] - d for b, d in succ[n]) - dur[n]
     for n in seq:
         st[n] = max([st[n]] + [st[a] + 1e-4 for a in pred[n]])

import math
import numpy
from concourse.mybir import AluOpType as Al, AxisListType, ActivationFunctionType as Af

F, B, H16, I, U = "float32", "bfloat16", "float16", "int32", "uint16"
P = {
    "g": ((2, 2), (3, 4)),
    "y": ((0, 1024, 2048), (0, 1024, 2048)),
    "pa": 0, "ra": "vvv", "mb": ("0101", "0123"), "ia": 0, "ts": "", "kp": ((0, 128),), "ye": (("vvvv", "vvvv"),) * 3,
    "zv": (2, 3, 4),
    "zo": ("76012345", "76012345", "70615243"),
    "zb": ("123010101", "123012301", "101230123"),
    "pb": ("2323", "0123", "01230101"),
    "xa": (1, 2, 0),
    "xo": "a", "au": "gob offb",
    "look": "v",
    "ha": "037",
    "ba": 8,
    "fv": 0,
    "rf": 4,
    "m1": 2,
}
CV, CA, CY, CP, CQ, SY, SX, GC = 0.05, 0.065, 0.00083, 0.00043, 0.035, 0.07, 0.19, 1.55
RATE = 300.0
WIDTH, SWEEPS, MOVES, HEAT, SEED = 16.0, 3, 12000, 0.08, 1
START = {
    "s": "tci tw0 imgi cI0 cI1 cI2 ow0 ow1 ow2",
    "g": "pi0 OH0 OH1 OH SA Ib CKd tf0 tf1 tf2 tf3 Dp0 SL G8 JB0 DB0 DB S01 Dp1 D01 Dm1 nI sez0 sez i16 DUM RR40 RR41 RR4 OHb0 OHb1 OHb CKP0 CKP tg0 tg1 tg2 tg3 tg4 tg5 tg6 tg7 cmq",
    "v": "SA0 ones pi1 P2 M16 CK WD0 P0 owni seg0 CKc seg offI bits9 bits10 bits11 bitt11 bits12 bitt12 mones Mz0 ui0 uj0 offK0 ia ui1 uj1 offK1 nmb ia2 H1 nma H2 1:scan 1:scan2 1:scan3 1:scan4 H4 "
         "1:scan5 1:look H5 1:gob 1:gob2 H6 1:goa 1:goa2 1:goa3 1:g0a",
    "a": "tw1 DL bits0 bits1 ccw bits2 WD bits3 cncw bits4 bits5 tch bits6 bits7 bits8 RR0 RR1 RR2 If imgf MK4 MK5 MK6 MK7 MK8 esb ib ib2 cmp0 H0 esa H3 H0.2 H7 H3.2 H7.2 1:xl 1:gob 1:g0b",
    "p": "Kt0 Kt1 Kt0.2 Kt0.3 Kt1.2 Kt1.3 kb Kw0 Kw1 ka kb2 ka2 kb3 H0 1:tub H3 1:scan 1:tua H7 1:gob 1:goa"}
END = {
    "v": "look goa g0a z7 z6 g0a2 z5 z4 offa win g1a win2 win3 ring list ring2 list2 ring3 g1a2 g1a3 ya x ya2 x2 put nma x3 nmb f x4 img",
    "a": "xl xo gob xr lv g0b z0 z0.2 z1 z1.2 z2 z2.2 z3 z3.2 g0b2 offb g1b g1b2 x g1b3 x2 g1b4 esa x3 esb f x4 nma f2 nmb f3 f4",
    "p": "goa gob xr at opa opb z7 z0 z6 z1 da z2 z5 z3 z4 db da2 db2 oqa list oqa2 p p2 x oqb p3 x2 p4 tra trb x3 f x4 f2 f3 img img2 f4"}
ROUND = {
    "v": "o:win3+ o:nmb+ o:nma+ e:scan e:scan2 o:list+ e:scan3 o:list2+ e:scan4 o:put+ e:scan5 e:look e:goa e:g0a e:z6 e:g0a2 e:z7 e:z5 e:offa e:win e:g1a3 e:g1a2 e:win2 e:g1a e:win3 e:x "
         "e:ya2 e:list e:ya e:list2 e:x2 e:yb2 e:yb e:nmb e:nma o:scan o:scan2 o:scan3 o:scan4 e:put o:scan5 o:look o:goa o:g0a o:g0a2 o:z7 o:z6 o:offa o:win o:g1a o:g1a2 o:g1a3 o:ya o:x "
         "o:ya2 o:yb o:x2 o:x3 o:yb2 o:win2",
    "a": "o:esa2+ e:m o:len+ e:m2 o:nma+ o:nmb+ e:m3 o:len2+ e:m4 o:own+ o:own2+ e:xl e:scan e:xo e:gob e:xr e:g0b2 e:z0 e:z1 e:z0.2 e:z1.2 e:g0b e:z4 e:z2 e:z3 e:z2.2 e:z3.2 e:offb e:z4.2 "
         "e:g1b3 e:g1b2 e:g1b e:g1b4 e:x e:x2 e:esb e:len e:esa e:esa2 e:nma e:nmb e:len2 o:m e:own2 e:own o:m2 o:m3 o:m4 o:xl o:scan o:xo o:gob o:xr o:g0b o:z1 o:z1.2 o:g0b2 o:z0 o:z0.2 o:z3 o:z3.2 o:offb "
         "o:z2 o:g1b o:g1b2 o:x o:z2.2 o:g1b3 o:g1b4 o:z5 o:z4 o:z4.2 o:z5.2 o:esb o:esa",
    "p": "e:m e:m2 e:m3 o:len+ e:m4 e:scan e:pv e:tub e:tua e:goa e:gob e:xr e:oqa e:opa e:z6 e:at e:z1 e:z0 e:da e:z7 e:opb e:z3 e:z4 e:z5 e:da2 e:z2 e:db e:db2 e:p2 e:p4 e:p3 e:trx e:oqb "
         "e:p e:oqa2 e:list e:tra e:x e:x2 e:trb e:keya e:trx2 e:keyb e:len o:m o:m2 o:tub o:tua o:scan o:m3 o:m4 o:pv o:gob o:goa o:xr o:at o:opb o:opa o:z7 o:z0 o:z1 o:oqa o:da o:z6 o:db o:z3 o:da2 o:db2 "
         "o:z2 o:p o:p2 o:trx o:oqb o:x o:z5 o:oqa2 o:tra o:p3 o:z4 o:p4 o:tra2 o:keya o:trb o:trx2 o:keyb o:list"}
MG = 12582912.0
TO = 2112.0
YO = 49152.0
RC = -255.0 / 512


def _sb(n, d):
    return ("sbuf", [128, n], d)


SCRATCH = {
    "tw": _sb(4096, B), "Hw": _sb(16384, B), "bits": _sb(4096, B), "tab0": _sb(4480, F), "tab1": _sb(4480, F),
    "X00": _sb(2048, H16), "X01": _sb(2048, H16), "X10": _sb(2048, H16), "X11": _sb(2048, H16), "M0": _sb(2048, H16), "M1": _sb(2048, B),
    "G0": _sb(2048, B), "G1": _sb(2048, B), "y0": _sb(2048, B), "y1": _sb(2048, B), "fo": _sb(4096, B), "CKP": _sb(512, B),
    "imgi": _sb(256, I), "imgf": _sb(256, H16), "offI": _sb(256, U), "tci": _sb(1024, I), "tch": _sb(1024, H16), "offK": _sb(256, U),
    "cmpI": _sb(768, I), "cmp": _sb(768, F), "cmq": _sb(768, F), "land0": _sb(768, F), "land1": _sb(768, F), "land2": _sb(768, F),
    "lv2": _sb(256, H16), "lv4": _sb(256, H16), "lv6": _sb(256, F), "lo2": _sb(16, U), "lo4": _sb(16, U), "lo6": _sb(16, U),
    "owni": _sb(256, I), "A0": _sb(256, H16), "A1": _sb(256, H16), "V6": _sb(256, F), "XR0": _sb(256, H16), "XR1": _sb(256, H16), "XL0": _sb(256, B), "XL1": _sb(256, B),
    "G8": _sb(16, F), "pi": _sb(32, I), "col": _sb(48, F), "odb": _sb(2, B), "POW": _sb(64, F), "i16": _sb(16, F), "M16": _sb(16, F), "SL": _sb(8, B), "DL": _sb(16, B),
    "Ib": _sb(128, B), "If": _sb(128, F), "nI": _sb(128, B), "ones": _sb(128, B), "mones": _sb(128, B),
    "Dp0": _sb(128, B), "Dp1": _sb(128, B), "Dm1": _sb(128, B), "D01": _sb(128, B), "S01": _sb(128, B), "DB": _sb(128, B),
    "WD": _sb(144, B), "SA": _sb(576, B), "RR": _sb(40, B), "CK": _sb(896, B), "seg": _sb(256, F), "sez": _sb(512, F), "JB": _sb(2, F), "DUM": _sb(16, F),
    "run": _sb(128, F), "pn": _sb(256, I), "pm": _sb(256, I), "PF": _sb(256, H16), "Rm": _sb(256, I), "oj": _sb(16, I), "offW": _sb(16, U),
    "wj": _sb(16, F), "Wz": _sb(256, F), "Wn": _sb(256, B), "MK": _sb(256, F), "MB": _sb(256, F), "offG": _sb(16, U), "OH": _sb(8, F), "Mz": _sb(256, H16),
    "offO": _sb(16, U), "offU0": _sb(256, U), "offU1": _sb(256, U), "offS0": _sb(16, U), "offS1": _sb(16, U),
    "ui": _sb(256, I), "uj": _sb(256, I), "yi": _sb(256, F), "OHb": _sb(8, B), "tn": _sb(64, F), "cnt": _sb(16, F), "junk": _sb(4096, B), "zs": _sb(4096, F),
    "pT": ("psum", [128, 1536], F), "pS": ("psum", [128, 512], F), "pQ": ("psum", [128, 2048], F),
}
SEMAPHORES = ["cv", "ca", "cp", "cg"] + ["d%d" % k for k in range(90)] + ["r%d" % k for k in range(18)]


def build(T, topo, core, rank):
    ops = []; tag = ["", 0]
    n4 = len(T.cores)
    nxt, prv = T.cores[(rank + 1) % n4], T.cores[(rank - 1) % n4]
    rid, pid = topo.addr(nxt)[0], topo.addr(nxt)[1]
    nout, nin = len(topo.engines(core, nxt)), len(topo.engines(prv, core))

    def op(e, t, r, w, fn, b=(), kind="c", lat=0.0, sem=None, kb=0.0):
        ops.append({"e": e, "t": t, "r": list(r), "w": list(w), "b": list(b), "fn": fn, "k": kind, "lat": lat, "sem": sem, "kb": kb,
                    "tag": tag[0] or (list(w) + list(b) + [""])[0], "step": tag[1]})

    def v(n, r, w, fn, b=()):
        op("v", CV + max(n, 64) * CY, r, w, fn, b)

    def gp(n, r, w, fn):
        op("g", 0.15 + 2 * n * CY, r, w, fn)

    def mm(r, b, lst):
        lst = [list(x) + [True] for x in lst]

        def fn(q):
            last = None
            for o, l, x, s0, c, s1 in lst:
                last = q.matmul(o, l, x, s0, s1)
            return last
        op("p", CQ + sum(m[4] for m in lst) * CP, r, [], fn, [b])
        ops[-1]["mm"] = lst

    def dma(e, kb, r, w, out, src):
        op(e, 0.1, r, w, lambda q: q.dma_start(out, src), kind="d", lat=1.3, kb=kb)

    def send(k, kb, r, w, dst, src):
        op("g", 0.3, r, ["snd%d" % k], lambda q, ls: q.remote_dma(dst, src, T.sem["r%d" % k], ls, pid, rid, topo.mask(core, nxt)), kind="s", lat=2.0 + kb / 80.0)
        op("x", 0.0, ["snd%d" % k], w, None, kind="x", lat=0.3, sem=("r%d" % k, nin))

    def ts(n, r, w, out, in0, s1, s2, o0, o1=None, b=()):
        if o1 is None:
            v(n, r, w, lambda q: q.tensor_scalar(out, in0, s1, None, o0), b)
        else:
            v(n, r, w, lambda q: q.tensor_scalar(out, in0, s1, s2, o0, o1), b)

    def tt(n, r, w, out, x, y, o, b=()):
        v(n, r, w, lambda q: q.tensor_tensor(out, x, y, o), b)

    def cp(n, r, w, out, x, b=()):
        v(n, r, w, lambda q: q.tensor_copy(out, x), b)

    def ms(n, w, out, c, r=()):
        v(n, r, w, lambda q: q.memset(out, c))

    def scan(n, r, w, out, seg, x, b):
        v(n, r, w, lambda q: q.tensor_tensor_scan(out, seg, x, 0.0, Al.add, Al.min), b)

    def act(n, r, w, out, x, f, bias=0.0, scale=1.0, b=(), acc=None):
        op("a", CA + max(n, 64) * CY + (0.02 if acc is not None else 0.0), r, w, lambda q: q.activation(out, x, f, bias=bias, scale=scale, accum_out=acc), b)

    def shift(scalar, n, r, w, out, x, add, b=()):
        plain = isinstance(add, float) and add == 0.0
        if scalar:
            act(n, r, w, out, x, Af.Copy if plain else Af.Identity, bias=add, b=b)
        elif not plain:
            ts(n, r, w, out, x, add, None, Al.add, b=b)
        else:
            cp(n, r, w, out, x, b=b)

    def iota(n, w, out, pat, base, cm, flt=True, r=()):
        if flt:
            gp(n, r, w, lambda q: q.iota(out, pat, base, cm, allow_small_or_imprecise_dtypes=True))
        else:
            gp(n, r, w, lambda q: q.iota(out, pat, base, cm))

    def sel(n, r, w, out, x, pat, cmp, fill, base, cm):
        gp(n, r, w, lambda q: q.affine_select(out, x, pat, cmp, fill, base, cm))

    def bank(k):
        k = int(k)
        return "Q%d" % k, T.pQ[:, 512 * k:512 * k + 512]

    tab = [T.tab0, T.tab1]; A = [T.A0, T.A1]; XR = [T.XR0, T.XR1]; XL = [T.XL0, T.XL1]
    pT = T.pT; pS = T.pS; offU = [T.offU0, T.offU1]; offS = [T.offS0, T.offS1]; RR = T.RR; CK = T.CK
    half = lambda h: slice(128 * h, 128 * h + 128)
    U0, E0, K0 = (896, 1024), (128, 1152), (384, 512)
    UB, EB, KB = ("T1", "T2"), ("T0", "T2"), ("T0", "T1")
    reg = lambda lo, n=128: pT[:, lo:lo + n]
    blk = lambda nm, lo=0, hi=2048: ["%s.%d" % (nm, k) for k in range(lo // 256, hi // 256)]

    def cuts(n, hi=2048):
        return [(256 * (hi // 256 * i // n), 256 * (hi // 256 * (i + 1) // n)) for i in range(n)]

    dma("s", 128, [], ["tci"], T.tci[0:32, :], T.turn[:])
    dma("s", 512, [], ["tw0"], T.tw[:, 0:2048], T.twist[:, 0:2048])
    dma("a", 512, [], ["tw1"], T.tw[:, 2048:4096], T.twist[:, 2048:4096])
    dma("s", 128, [], ["imgi"], T.imgi[:], T.img[:])
    ms(256, ["owni"], T.owni[:], 0)
    for q in range(2):
        dma("s", 128, [], ["cI%d" % q], T.cmpI[:, 256 * q:256 * q + 256], T.ent[:, 4096 * q:4096 * q + 4096])
        dma("s", 8, ["owni"], ["ow%d" % q], T.owni[q:128:16, :], T.own[:, 256 * q:256 * q + 256])
    dma("s", 128, [], ["cI2"], T.cmpI[:, 512:768], T.elen[:])
    dma("s", 8, ["owni"], ["ow2"], T.owni[2:128:16, :], T.olen[:])

    iota(16, ["pi0"], T.pi[:, 0:16], [[1, 16]], 128, -1, False)
    iota(16, ["i16"], T.i16[:], [[1, 16]], 0, 0)
    iota(16, ["G8"], T.G8[:], [[128, 2], [0, 8]], 0, 1)
    ms(64, ["ones"], T.ones[:], 1.0); ms(64, ["mones"], T.mones[:], -1.0)
    sel(128, ["ones"], ["Ib"], T.Ib[:], T.ones[:], [[-1, 128]], Al.is_equal, 0.0, 0, 1)
    sel(128, ["mones"], ["nI"], T.nI[:], T.mones[:], [[-1, 128]], Al.is_equal, 0.0, 0, 1)
    ms(448, ["CK"], CK[0:64, :], 0.0)
    ms(64, ["CKc"], CK[32:33, 256:384], 4096 * YO, r=["CK"])
    iota(256, ["CKd"], CK[0:1, 384:640], [[1, 256]], 0, 0, r=["CK"])
    ms(64, ["CKf"], CK[0:1, 640:768], 16 * YO, r=["CK"]); ms(64, ["CKe"], CK[32:33, 640:768], -YO / 256, r=["CKf"])
    ms(64, ["CKg"], CK[0:1, 768:896], RC, r=["CK"])
    ms(288, ["SA0"], T.SA[0:32, :], 0.0)
    sel(36, ["SA0"], ["SA"], T.SA[0:32, 15:576:16], T.SA[0:32, 15:576:16], [[1, 4], [4, 9]], Al.not_equal, -1.0, 0, -1)
    iota(2, ["JB0"], T.JB[:], [[128, 2]], -12 * 2 ** 19, 1)
    act(2, ["JB0"], ["JB"], T.JB[:], T.JB[:], Af.Identity, scale=4096.0)
    iota(16, ["DUM"], T.DUM[:], [[16, 16]], 4096, 1)
    fv = P["fv"]; fg = (4096 - fv) // 4
    for k in range(4):
        iota(fg, ["tf%d" % k], T.tab0[:, fg * k:fg * k + fg], [[0, fg]], 0, 0)
    if fv:
        ms(fv, ["tf4"], T.tab0[:, 4096 - fv:4096], 0.0)
    fill = [["tf%d" % k for k in range(5)], ["tg%d" % k for k in range(8)]]
    names = {}

    def c(nm):
        if nm not in names:
            names[nm] = len(names)
        return T.col[:, names[nm]:names[nm] + 1]

    ts(16, ["pi0"], ["pi1"], T.pi[:, 16:32], T.pi[:, 0:16], 15, None, Al.bitwise_and)
    ts(16, ["pi1"], ["M16"], T.M16[:], T.pi[:, 16:32], 0, None, Al.is_equal)
    ms(12, ["P2"], T.POW[:, 16:28], 0.5)
    v(12, ["P2", "M16"], ["P0"], lambda q: q.tensor_tensor_scan(T.POW[:, 0:12], T.POW[:, 16:28], T.M16[:, 4:16], 0.0, Al.mult, Al.add))
    act(1, ["P0"], ["ccw"], c("cw"), T.POW[:, 11:12], Af.Identity, scale=8.0)
    act(1, ["P0"], ["cncw"], c("ncw"), T.POW[:, 11:12], Af.Identity, scale=-8.0)
    ms(72, ["WD0"], T.WD[:], 0.0)
    for nm, out, x in (("OH", T.OH[:], 1), ("OHb", T.OHb[:], -8192), ("RR4", RR[:, 32:40], 256)):
        iota(8, [nm + "0"], out, [[0, 8]], x, 0)
        sel(8, [nm + "0"], [nm + "1"], out, out, [[-16, 8]], Al.is_ge, 0.0, 0, 1)
        sel(8, [nm + "1"], [nm], out, out, [[16, 8]], Al.is_ge, 0.0, 15, -1)
    act(4, ["OH"], ["cod"], T.POW[:, 32:36], T.OH[:, 1:8:2], Af.Copy, acc=c("od"))
    if P["xo"] == "v":
        cp(1, ["cod"], ["odb"], T.odb[:, 0:1], c("od"))
    act(8, ["OH", "ccw", "WD0"], ["WD"], T.WD[:, 15:143:16], T.OH[:], Af.Identity, scale=c("cw"))
    cp(256, ["imgi"], ["offI"], T.offI[:], T.imgi[:]); act(256, ["imgi"], ["imgf"], T.imgf[:], T.imgi[:], Af.Identity, bias=-2048.0)
    for k, w in enumerate(("cw", "ncw", -256.0, "cw")):
        act(8, ["OH", "ccw", "cncw"], ["RR%d" % k], RR[:, 8 * k:8 * k + 8], T.OH[:], Af.Identity, scale=c(w) if isinstance(w, str) else w)
    act(12, ["M16"], ["cdv"], T.POW[:, 36:48], T.M16[:, 4:16], Af.Identity, scale=-2.0 / 4096, acc=c("dv"))
    for nm, k, sc, bi in (("j4", 3, 4096.0, 0.0), ("b2", 2, 2.0 ** 20, c("j4"))):
        act(1, ["M16", "cj4"], ["c" + nm], c(nm), T.M16[:, k:k + 1], Af.Identity, bias=bi, scale=sc)
    act(1, ["cdv", "cb2"], ["cb"], c("b"), c("dv"), Af.Identity, bias=c("b2"), scale=2.0 ** 32)
    act(128, ["Ib"], ["If"], T.If[:], T.Ib[:], Af.Copy)
    sel(128, ["Ib"], ["DB0"], T.DB[:], T.Ib[:], [[-1, 128]], Al.not_equal, -2.0 / 4096, 0, 1)
    sel(128, ["DB0"], ["DB"], T.DB[:], T.DB[:], [[0, 8], [1, 16]], Al.is_ge, 0.0, -4, 0)
    sel(128, ["Ib"], ["S01"], T.S01[:], T.Ib[:], [[0, 8], [-1, 16]], Al.is_ge, 0.0, 1, 0)
    rows = [[-16, 8], [0, 16]]
    for nm, src, k in (("Dp0", "ones", 0), ("Dp1", "ones", 1), ("Dm1", "mones", 1)):
        sel(128, [src], [nm], T[nm][:], T[src][:], rows, Al.is_equal, 0.0, -k, 1)
    sel(128, ["Dp1"], ["D01"], T.D01[:], T.Dp1[:], rows, Al.not_equal, -1.0, 0, 1)
    sel(8, ["ones"], ["SL"], T.SL[:], T.ones[:, 0:8], [[-16, 8]], Al.is_equal, 0.0, -2, 1)
    ms(256, ["seg0"], T.seg[:], 0.0); ms(16, ["seg"], T.seg[:, 0:256:16], 2.0 ** 23, r=["seg0"])
    iota(512, ["sez0"], T.sez[:], [[0, 512]], 0, 0); sel(2, ["sez0"], ["sez"], T.sez[:, 0:512:256], T.sez[:, 0:512:256], [[0, 2]], Al.not_equal, 2.0 ** 40, 0, 0)
    act(16, ["M16"], ["MK4"], T.MK[:, 0:16], T.M16[:], Af.Copy)
    for s in range(4, 8):
        act(1 << s, ["MK%d" % s], ["MK%d" % (s + 1)], T.MK[:, 1 << s:2 << s], T.MK[:, 0:1 << s], Af.Copy)
    act(256, ["MK8"], ["MB"], T.MB[:], T.MK[:], Af.Identity, bias=8192.0, scale=-8192.0)
    act(16, ["i16"], ["offG"], T.offG[:], T.i16[:], Af.Copy)
    ms(128, ["Mz0"], T.Mz[:], 0.0)
    act(16, ["Mz0", "G8"], ["Mj"], T.Mz[:, 3:256:16], T.G8[:], Af.Copy)
    act(16, ["M16"], ["DL"], T.DL[:], T.M16[:], Af.Identity, scale=-256.0)
    act(1, ["M16"], ["bits0"], T.bits[:, 0:1], T.M16[:, 0:1], Af.Identity, scale=0.0)
    for s in range(12):
        n = 1 << s
        for j in range(2 if n > 512 else 1):
            m = n // 2 if n > 512 else n
            a = s < P["ba"]
            shift(a, m if a else m // 2, ["bits%d" % s, "bitt%d" % s, "DL"], ["bit%s%d" % ("st"[j], s + 1)], T.bits[:, n + j * m:n + j * m + m], T.bits[:, j * m:j * m + m], T.DL[:, 4 + s:5 + s])
    bitsr = ["bits12", "bitt12"]

    act(1024, ["tci"], ["tch"], T.tch[0:32, :], T.tci[0:32, :], Af.Identity, bias=-2048.0)
    for hh in range(2):
        bk, pk = bank(hh); tag[0] = "Kt%d" % hh
        mm(["CK", "SA"], bk, [(pk[:, 0:128], CK[0:32, 0:128], T.SA[0:32, 0:128], True, 128)])
        for a in range(2 * hh, 2 * hh + 2):
            mm(["tch", "SA"], bk, [(pk[:, 64 * (a % 2):64 * (a % 2) + 64], T.SA[0:32, 144 * a + 15 - r:144 * a + 143 - r], T.tch[0:32, r:1024:16], False, 64) for r in range(16)])
        tag[0] = "Kw%d" % hh
        mm(["tw%d" % hh, "WD"], bk, [(pk[:, 0:128], T.WD[:, 15 - r:143 - r], T.tw[:, 2048 * hh + r:2048 * hh + 2048:16], False, 128) for r in range(16)])
        tag[0] = ""
        ts(128, [], ["ui%d" % hh], T.ui[:, half(hh)], pk[:, 0:128], 2048 + RC, None, Al.add, b=[bk])
        ts(128, ["ui%d" % hh], ["uj%d" % hh], T.uj[:, half(hh)], T.ui[:, half(hh)], 4095, None, Al.bitwise_and)
        cp(128, ["uj%d" % hh], ["offK%d" % hh], T.offK[:, half(hh)], T.uj[:, half(hh)])
    iota(512, ["CKP0"], T.CKP[0:32, :], [[0, 512]], 0, 0); iota(512, ["CKP"], T.CKP[0:1, :], [[0, 512]], -int(YO), 0, r=["CKP0"])
    for k in range(8):
        iota(512, ["tg%d" % k], T.tab1[:, 512 * k:512 * k + 512], [[0, 512]], 0, 0)
    Hr = ["H%d" % i for i in range(8)]
    for s in range(8):
        sl = slice(512 * s, 512 * s + 512); bit = T.bits[:].indirect(T.offK[:, 32 * s:32 * s + 32]); tag[0] = "H%d" % s
        if str(s) not in P["ha"]:
            tt(512 * GC, bitsr + ["offK%d" % (s // 4), "tw%d" % (s // 4)], ["H%d" % s], T.Hw[:, sl], bit, T.tw[:, sl], Al.add)
        else:
            bk, pk = bank(2 + P["ha"].index(str(s)) % 2); lo = 512 * (s % 4); tmp = T["G%d" % (s // 4)][:, lo:lo + 512]; key = blk("G%d" % (s // 4), lo, lo + 512)
            act(512 * GC, bitsr + ["offK%d" % (s // 4)], key, tmp, bit, Af.Copy)
            mm(key + ["Ib", "tw%d" % (s // 4)], bk, [(pk, T.Ib[:], T.tw[:, sl], True, 512), (pk, T.Ib[:], tmp, False, 512)])
            act(512, [], ["H%d" % s], T.Hw[:, sl], pk, Af.Copy, b=[bk])
    tag[0] = ""
    for hh in range(4):
        for k in range(1, 4):
            dma("s", 256, Hr[2 * hh:2 * hh + 2], ["Hx%d.%d" % (k, hh)], T.Hw[:, 4096 * k + 1024 * hh:4096 * k + 1024 * hh + 1024], T.Hw[:, 1024 * hh:1024 * hh + 1024])
    Hxr = Hr + ["Hx%d.%d" % (k, hh) for k in range(1, 4) for hh in range(4)]

    act(768, ["cI0", "cI1", "cI2"], ["cmp0", "cmp1", "cmp2"], T.cmp[:], T.cmpI[:], Af.Identity, bias=-2048.0)

    def unpack(src, keys, tb):
        for q in range(3):
            dma("s", 128, [keys % q] + fill[tb], ["tab%d.%d" % (tb, q)], tab[tb][q:128:16, 0:4096], src[:, 256 * q:256 * q + 256])
    tabk = lambda tb: fill[tb] + ["tab%d.%d" % (tb, q) for q in range(3)]
    unpack(T.cmp, "cmp%d", 0)
    act(256, ["ow0", "ow1", "ow2"], ["A0"], T.A0[:], T.owni[:], Af.Identity, bias=-2048.0)
    tn = lambda k: T.tn[:, 16 * k:16 * k + 16]
    Mz = T.Mz[:, 2:256:16]
    tag[0] = "Mz"
    mm(["A0", "SL"], "S", [(pS[:, 8 * h:8 * h + 8], T.A0[:, half(h)], T.SL[:], True, 64) for h in range(2)])
    act(16, ["Mz0"], ["Mz"], Mz, pS[:, 0:16], Af.Copy, b=["S"])

    def ownkeys():
        for h in range(2):
            act(8, ["Mz", "JB"], ["kb%d" % h], T.tn[:, 32 + 8 * h:40 + 8 * h], T.Mz[:, 128 * h + 2:128 * h + 128:16], Af.Identity, bias=T.JB[:, h:h + 1], scale=2.0 ** 20)
    ownkeys()

    def gather(h, pieces, win, wr, off, offr, new, prev=None):
        for lo, hi in cuts(pieces):
            o = win.indirect(off[:, 128 * h + lo // 16:128 * h + hi // 16]); n = (hi - lo) * GC
            if prev:
                tt(n, wr + offr + blk(prev, lo, hi), blk(new, lo, hi), T[new][:, lo:hi], o, T[prev][:, lo:hi], Al.add)
            else:
                shift(h, n, wr + offr, blk(new, lo, hi), T[new][:, lo:hi], o, 0.0)

    def column(h, start=False):
        return [(reg(K0[h]), T.ones[0:32, :], CK[0:32, 384 + 128 * h:512 + 128 * h], start, 128)]

    def tr(b, src, lo, n, r0, more=(), parts=None):
        for l0, l1 in parts or (((0, 96), (96, 128)) if tag[0] in P["ts"].split() else ((0, 128),)):
            mm(blk(src, 16 * l0, 16 * l1) + ["RR%d" % k for k in range(r0, r0 + n)] + ["CKd", "ones"], b,
               [(pT[l0:l1, lo + i:lo + 128 * n:16], T[src][:, 16 * l0 + i:16 * l1:16], RR[:, 8 * r0:8 * (r0 + n)], False, min(64, l1 - l0)) for i in range(16)] + list(more) * (l1 == 128))

    def direct(h, src):
        for s in range(2):
            mm(blk(src, 1024 * s, 1024 * s + 1024) + ["WD"], UB[h],
               [(reg(U0[h] + 64 * s, 64), T.WD[:, 15 - i:143 - i], T[src][:, 1024 * s + i:1024 * s + 1024:16], False, 64) for i in range(16)])

    def const(lo, n, c0, rows, start=True):
        return (reg(lo, n), T.ones[0:rows, :], CK[0:rows, c0:c0 + n], start, n)

    def turn(h):
        mm(["PF%d" % h, "Ib"], UB[h], [(reg(U0[h]), T.PF[:, half(h)], T.Ib[:], True, 128)])

    def points(h, more):
        tag[0] = "es" + "ab"[h]; sl = half(h); x = "%d" % h; raw = "pn" if tag[1] else "pm"
        act(128, [], [raw + x], T[raw][:, sl], reg(E0[h]), Af.Identity, bias=RC + 2048, b=[EB[h]])
        if more and h == 0:
            act(128, [], ["run"], T.run[:], reg(256), Af.Identity, bias=RC, b=["T0"])
        tag[0] = "nm" + "ab"[h]
        if tag[1]:
            ts(128, ["pn" + x], ["pm" + x], T.pm[:, sl], T.pn[:, sl], 4095, None, Al.bitwise_and)
        act(128, ["pm" + x], ["PF" + x], T.PF[:, sl], T.pm[:, sl], Af.Identity, bias=-2048.0)

    def nstage(h, add, out, key, plain):
        o = reg(U0[h]); sl = half(h); b = [UB[h]]
        if plain and tag[0] in P["au"]:
            act(128, [], [key], out[:, sl], o, Af.Identity, bias=float(add), b=b)
        elif plain:
            ts(128, [], [key], out[:, sl], o, MG, MG - add, Al.add, Al.subtract, b=b)
        else:
            ts(128, [], ["ui%d" % h], T.ui[:, sl], o, float(add), None, Al.add, b=b)
            ts(128, ["ui%d" % h], ["uj%d" % h], T.uj[:, sl], T.ui[:, sl], 4095, None, Al.bitwise_and)
            shift(tag[0] in P["au"], 128, ["uj%d" % h], [key], out[:, sl], T.uj[:, sl], 0.0)

    def reduce256(h, src, out, ra, banks):
        for k, (lo, hi) in enumerate(cuts(4)):
            bk, pk = bank(banks[k])
            mm(blk(src, lo, hi) + blk("y%d" % h, lo, hi) + ["Ib", "nI"], bk, [(pk, T.Ib[:], T[src][:, lo:hi], True, 512), (pk, T.nI[:], T["y%d" % h][:, lo:hi], False, 512)])
            shift(k < ra, 512, [], blk(out, lo, hi), T[out][:, lo:hi], pk, -YO, b=[bk])

    def carries(h, src):
        tag[0] = "y" + "ab"[h]
        for lo, hi, e in zip(P["y"][h], P["y"][h][1:], P["ye"][kind][h]):
            shift(e == "a", (hi - lo) // (1 + (e == "v")), blk(src, lo, hi), blk("y%d" % h, lo, hi), T["y%d" % h][:, lo:hi], T[src][:, lo:hi], -YO - 127.5)

    for h in range(2):
        tag[0] = "i" + "ab"[h]
        gather(h, 2, T.tw[:], ["tw0", "tw1"], T.offI, ["offI"], "X%d0" % h)
    tag[0] = "ka"
    mm(["CK", "ones", "imgf", "Ib"], "T0", [const(128, 384, 0, 32), (reg(E0[0]), T.imgf[:, half(0)], T.Ib[:], False, 128)])
    tr("T0", "X00", 256, 2, 1, column(0))
    points(0, True)
    tag[0] = "kb"
    mm(["imgf", "Ib"], "T2", [(reg(E0[1]), T.imgf[:, half(1)], T.Ib[:], True, 128)])
    points(1, True)
    tag[0] = "kb"
    mm(["CKd", "ones"], "T1", column(1, True))
    tr("T1", "X10", K0[1], 1, 2)
    for n in range(1, 7):
        cur, old = n % 2, 1 - n % 2
        tb = ((n - 1) // 2) % 2; ho = (n - 1) // 2
        kind = 2 if n == 6 else 1 - cur
        keys = n < 6
        tag[1] = n
        Ak, Ao = "A%d" % cur, "A%d" % old
        back = [n == 4, n == 3]
        for h in range(2):
            if back[h]:
                tag[0] = "m"
                reduce256(h, "X%d%d" % (h, old), "X%d%d" % (h, cur), 4, P["mb"][h])
        tag[0] = "tub"
        turn(1)
        tag[0] = "scan"
        scan(256, ["seg"], ["Rm"], T.Rm[:], T.seg[:], reg(384, 256), ["T0", "T1"])
        ts(16, ["Rm"], ["oj"], T.oj[:], T.Rm[:, 15:256:16], 255, None, Al.bitwise_and)
        cp(16, ["oj"], ["offW"], T.offW[:], T.oj[:])
        tt(256 * GC, ["pm0", "pm1", "offW", "MK8"], ["Wz"], T.Wz[:], T.pm[:].indirect(T.offW[:]), T.MK[:], Al.mult)
        mm(["Wz", "OH"], "S", [(pS[:, 8 * h:8 * h + 8], T.Wz[:, half(h)], T.OH[:], True, 256) for h in range(2)])
        cp(16, [], ["oO"], T.offO[:], pS[:, 0:16], b=["S"])
        act(16, [], ["wj"], T.wj[:], pS[:, 0:16], Af.Copy, b=["S"])
        tag[0] = "look"
        shift(P["look"] == "a", 256 * GC, tabk(tb) + ["oO"], [Ak], A[cur][:], tab[tb][:, 0:4096].indirect(T.offO[:]), 0.0)
        tag[0] = "tua"
        turn(0)
        for h in range(2):
            tag[0] = "go" + "ab"[h]
            mm(["Dp0", Ak], UB[h], [(reg(U0[h]), T.Dp0[:], A[cur][:, half(h)], False, 128)])
            nstage(h, 4096, T.offU0, "oU0.%d" % h, n > 1)
        tag[0] = "xl"
        act(256 * GC, bitsr + ["oO", "cb"], ["XL0"], XL[0][:], T.bits[:].indirect(T.offO[:]), Af.Identity, bias=c("b"), scale=-2.0 ** 14)
        tag[0] = "xo"
        if P["xo"] == "v":
            ts(128, ["XL0", "odb"], ["XL1"], XL[1][:], XL[0][:], T.odb[:, 0:1], None, Al.mult)
        else:
            act(256, ["XL0", "cod"], ["XL1"], XL[1][:], XL[0][:], Af.Identity, scale=c("od"))
        tag[0] = "pv"; bk, pk = bank(P["zb"][kind][0]); pv = pk[:, 0:256]
        mm([Ao, "S01", "Mz", "Mj", "Ib"], bk, [(pv, T.S01[:], A[old][:], True, 256)] + [(pk[:, half(h)], T.Mz[:, half(h)], T.Ib[:], False, 128) for h in range(2)])
        tag[0] = "xr"
        mm(["XL0", "DB"], bk, [(pv, T.DB[:], XL[0][:], False, 256)])
        act(256, [], ["XR%d" % cur], XR[cur][:], pv, Af.Copy, b=[bk])
        tag[0] = "lv"
        if n == 6:
            shift(True, 256, [], ["V6"], T.V6[:], pv, 2048.0, b=[bk])
            send(n - 1, 128, ["V6"], ["lv6"], T.lv6[:], T.V6[:])
        elif cur == 0:
            send(n - 1, 64, ["XR0"], ["lv%d" % n], T["lv%d" % n][:], XR[0][:])
        tag[0] = "at"; AT, M2, LS = pS[:, 16:32], pS[:, 32:48], pS[:, 48:64]
        mm([Ak, "SL", "nI", "Mz"], "S", [(AT, T.nI[:], Mz, True, 64)] + [(pS[:, 16 + 8 * h:24 + 8 * h], A[cur][:, half(h)], T.SL[:], False, 64) for h in range(2)])
        zv = P["zv"][kind]; za = 16 - 2 * zv
        for k, zb in zip([int(x) for x in P["zo"][kind]], P["zb"][kind][1:]):
            tag[0] = "z%d" % k; bk, pk = bank(zb); lst = []
            for x in range(2):
                kz = 2 * k + x; r0 = 32 * (kz % 8 // 2); rs = slice(r0, r0 + 16 + 16 * x)
                lst.append((pk[:, 256 * x:256 * x + 256], XL[x][rs, half(kz // 8)], XR[cur][rs, :], True, 256))
            mm(["XL0", "XL1", "XR%d" % cur], bk, lst)
            if k >= 8 - zv:
                j = k - 8 + zv
                scan(512, ["sez"], ["mn%d" % k], T.zs[:, 512 * j:512 * j + 512], T.sez[:], pk, [bk])
            else:
                for x in range(2):
                    kz = 2 * k + x
                    act(256, ["kb%d" % (kz // 8)], ["cn%d" % kz], T.junk[:, 256 * kz:256 * kz + 256], pk[:, 256 * x:256 * x + 256], Af.Relu,
                        bias=T.tn[:, 32 + kz:33 + kz], scale=-1.0, b=[bk], acc=T.cnt[:, kz:kz + 1])
        tag[0] = "win"
        if zv:
            tt(16, ["kb0", "kb1"] + ["mn%d" % k for k in range(8 - zv, 8)], ["cn%d" % k for k in range(za, 16)], T.cnt[:, za:16], T.tn[:, 32 + za:48], T.zs[:, 255:512 * zv:256], Al.subtract)
        tt(16, ["cn%d" % k for k in range(16)], ["d"], tn(1), AT, T.cnt[:], Al.subtract, b=["S"])
        tt(256 * GC, ["d", "offG", "MB"], ["Wn"], T.Wn[:], tn(1).indirect(T.offG[:]), T.MB[:], Al.is_gt)
        tag[0] = "list"
        mm(["Wn", "OHb", "If", "DUM"], "S", [(LS, T.If[:], T.DUM[:], True, 256)] + [(pS[:, 48 + 8 * h:56 + 8 * h], T.Wn[:, half(h)], T.OHb[:], False, 64) for h in range(2)])
        tt(16, ["wj"], ["t9"], tn(3), LS, T.wj[:], Al.max, b=["S"])
        cp(16, ["t9"], ["offS%d" % cur], offS[cur][:], tn(3))
        if keys:
            tag[0] = "len"
            act(16, ["d"], ["z"], tn(0), tn(1), Af.Relu)
            mm(["z", "Mz", "If", "Ib", "ones"], "S", [(M2, T.If[:], tn(0), True, 256), (M2, T.Ib[:], Mz, False, 64), (M2, T.ones[0:2, :], T.ones[0:2, 0:16], False, 64)])
            act(16, [], ["Mz"], Mz, M2, Af.Copy, b=["S"])
            tag[0] = "own"
            ownkeys()
        land = T["land%d" % ho]

        def put(tb, off, val):
            tag[0] = "put"
            if P["pa"] and keys:
                act(256, [val], ["V6"], T.V6[:], T[val][:], Af.Identity, bias=TO)
                act(1000, [off, "V6"], tabk(tb), tab[tb][:].indirect(T[off][:]), T.V6[:], Af.Silu)
            else:
                cp(1000, [off, val], tabk(tb), tab[tb][:].indirect(T[off][:]), T[val][:])
        if cur == 1:
            put(tb, "offS1", "XR1")
            tag[0] = "ring"
            for q in range(3):
                dma("s", 128, tabk(tb), ["cmp%d" % q], T.cmp[:, 256 * q:256 * q + 256], tab[tb][q:128:16, 0:4096])
            for q in range(3):
                sl = slice(256 * q, 256 * q + 256); key = "land%d.%d" % (ho, q)
                send(6 + 3 * ho + q, 128, ["cmp%d" % q], [key], land[:, sl], T.cmp[:, sl])
            if n < 5:
                unpack(land, "land%d." % ho + "%d", 1 - tb)
        else:
            tag[0] = "lo"
            send(n - 2, 4, ["offS0"], ["lo%d" % n], T["lo%d" % n][:], offS[0][:])
            tag[0] = "ring"
            if n == 6:
                for q in range(3):
                    shift(P["ra"][q] == "a", 256, ["land2.%d" % q], ["cmq%d" % q], T.cmq[:, 256 * q:256 * q + 256], land[:, 256 * q:256 * q + 256], 2048.0)
                unpack(T.cmq, "cmq%d", 1 - tb)
            put(1 - tb, "lo%d" % n, "lv%d" % n)
        Xn = ["X%d%d" % (h, cur) for h in range(2)]; Xo = [Xn[h] if back[h] else "X%d%d" % (h, old) for h in range(2)]
        plain = [n > 1 or q >= P["m1"] for q in range(2)]
        win = [(T.Hw[:], Hxr) if x else (T.Hw[:, 0:4096], Hr) for x in plain]
        for h in range(2):
            z = "ab"[h]; tag[0] = "op" + z
            mm([Ak, "D01", "If", "CKg", "ones"] + ["run"] * (1 - h), UB[h],
               [const(U0[1], 128, 768, 32) if h else (reg(U0[0]), T.run[:], T.If[:], True, 512), (reg(U0[h]), T.D01[:], A[cur][:, half(h)], False, 128)])
            tag[0] = "g0" + z
            gather(h, P["g"][0][h], win[0][0], win[0][1], offU[0], ["oU0.%d" % h], "M%d" % h, None if h else Xo[0])
            tag[0] = "d" + z
            direct(h, "M%d" % h)
            tag[0] = "off" + z
            nstage(h, 8192, T.offU1, "oU1.%d" % h, plain[1])
        tag[0] = "oqa"
        mm(["CKc", "ones", Ak, "Dm1"], "T0", [const(128, 384 if keys else 128, 0, 64), (reg(128), A[cur][:, half(0)], T.Dm1[:], False, 128)])
        tr("T0", "M0", 128, 1, 1)
        tag[0] = "g1a"
        gather(0, P["g"][1][0], win[1][0], win[1][1], offU[1], ["oU1.0"], Xn[0], "M0")
        carries(0, Xn[0])
        tag[0] = "tra"
        if n == 3:
            mm(["CKe", "ones"], "T0", [const(256, 128, 640, 64, False)])
            tr("T0", "y0", 256, 2, 3)
            tag[0] = "keya"
            tr("T0", Xn[0], 128, 3, 0, column(0))
        else:
            tr("T0", Xn[0], 128, 3 if keys else 1, 0)
            tag[0] = "keya"
            if keys:
                tr("T0", "y0", K0[0], 1, 4, column(0))
        points(0, keys)
        tag[0] = "oqb"
        mm([Ak, "Dm1"], "T2", [(reg(E0[1]), A[cur][:, half(1)], T.Dm1[:], True, 128)])
        tag[0] = "g1b"
        gather(1, P["g"][1][1], win[1][0], win[1][1], offU[1], ["oU1.1"], "G1")
        tag[0] = "trb"
        tr("T2", "G1", E0[1], 1, 0)
        points(1, keys)
        for k, (lo, hi) in enumerate(cuts(4)):
            tag[0] = "p"; bk, pk = bank(P["pb"][kind][k]); G = T.G1[:, lo:hi]; Y = T.y1[:, lo:hi]; yk = blk("y1", lo, hi); onv = keys and k >= P["xa"][kind]
            mm(blk(Xo[1], lo, hi) + blk("M1", lo, hi) + ["Ib"] + ["ones", "CKP"] * (not keys), bk,
               [(pk, T.Ib[:], T[Xo[1]][:, lo:hi], True, 512), (pk, T.Ib[:], T.M1[:, lo:hi], False, 512)] + [(pk, T.ones[0:32, :], T.CKP[0:32, :], False, 512)] * (not keys))
            tag[0] = "x"
            if onv:
                tt(512, blk("G1", lo, hi), blk(Xn[1], lo, hi), T[Xn[1]][:, lo:hi], pk, G, Al.add, b=[bk])
                continue
            mm(blk("G1", lo, hi) + ["Ib"], bk, [(pk, T.Ib[:], G, False, 512)])
            if keys:
                act(512, [], blk(Xn[1], lo, hi), T[Xn[1]][:, lo:hi], pk, Af.Copy, b=[bk])
            else:
                shift(True, 512, [], yk, Y, pk, -127.5, b=[bk])
                tt(512, yk, blk("fo", 2048 + lo, 2048 + hi), T.fo[:, 2048 + lo:2048 + hi], pk, Y, Al.subtract, b=[bk])
        if keys:
            carries(1, Xn[1])
            tag[0] = "trx"
            mm(["CKc", "ones"], "T1", [const(K0[1], 128, 256, 64)])
            for part in P["kp"]:
                tag[0] = "trx"
                tr("T1", Xn[1], K0[1], 1, 2, (), [part])
                tag[0] = "keyb"
                tr("T1", "y1", K0[1], 1, 4, column(1), [part])
        else:
            tag[0] = "f"
            reduce256(0, Xn[0], "fo", P["rf"], P["pb"][kind][4:])
            tag[0] = "img"
            turn(0); turn(1)
            shift(P["ia"], 256, [], ["yi0", "yi1"], T.yi[:], reg(U0[0], 256), 2048.0, b=UB)
    tag[0] = "out"
    dma("s", 128, tabk(1), [], T.yent[:, 0:4096], T.tab1[0:128:16, 0:4096])
    dma("s", 128, tabk(1), [], T.yent[:, 4096:8192], T.tab1[1:128:16, 0:4096])
    dma("s", 128, tabk(1), [], T.yelen[:], T.tab1[2:128:16, 0:4096])
    dma("s", 128, ["yi0", "yi1"], [], T.yimg[:], T.yi[:])
    for k in range(8):
        dma("s", 128, blk("fo", 512 * k, 512 * k + 512), [], T.yf[:, 512 * k:512 * k + 512], T.fo[:, 512 * k:512 * k + 512])
    return ops, nout


def link(ops):
    lw, rd, lb, tail = {}, {}, {}, {}
    for n, o in enumerate(ops):
        dep = {}
        for k in o["r"]:
            if k in lw:
                dep[lw[k]] = True
        for k in o["w"]:
            for x in ([lw[k]] if k in lw else []) + rd.get(k, []):
                dep[x] = True
        for k in o["b"]:
            if k in lb:
                dep.setdefault(lb[k], False)
            lb[k] = n
            for x in o.get("mm", []):
                if not x[3]:
                    tail[k][5] = False
                tail[k] = x
        dep.pop(n, None)
        for k in o["r"]:
            rd.setdefault(k, []).append(n)
        for k in o["w"]:
            lw[k] = n; rd[k] = []
        o["dep"] = dep


def graph(ops):
    eng = [o["e"] for o in ops]; dur = [o["t"] for o in ops]; last = list(range(len(ops))); edges = []
    for n, o in enumerate(ops):
        if o["kb"]:
            last[n] = len(eng); eng.append("w"); dur.append(o["kb"] / RATE); edges.append((n, last[n], o["lat"] - 0.5))
    for n, o in enumerate(ops):
        for d, data in o["dep"].items():
            p = ops[d]; same = p["e"] == o["e"] and p["k"] == o["k"] == "c"
            edges.append((last[d], n, (0.5 if p["kb"] else p["lat"]) + (SX if not same else SY if data and o["e"] != "p" else 0.0)))
    return eng, dur, edges


def first(ops, eng, dur, edges):
    N = len(eng); seen = {}; where = {}; before = {}; named = set()
    for n, o in enumerate(ops):
        k = (o["step"], o["tag"], o["e"]); seen[k] = seen.get(k, 0) + 1
        o["nm"] = o["tag"] + ("" if seen[k] == 1 else "." * o["tag"][-1].isdigit() + str(seen[k])); where[(o["step"], o["nm"], o["e"])] = n
    for e in START:
        ends = [[where.get((int(x[0]), x[2:], e) if ":" in x else (s, x, e)) for x in L.get(e, "").split()] for s, L in ((0, START), (6, END))]
        line = [where.get((2 * k + 2 + (x[0] == "o") - 2 * {"+": 1, "-": -1}.get(x[-1], 0), x[2:].rstrip("+-"), e)) for k in range(-2, 4) for x in ROUND.get(e, "").split()]
        line = [n for n in ends[0] + [n for n in line if n not in ends[0] + ends[1] and n is not None and ops[n]["step"]] + ends[1] if n is not None]
        before.update(zip(line[1:], line)); named.update(line)
    succ = [[] for e in eng]; pred = [[] for e in eng]; left = [0] * N; st = [0.0] * N; free = {}; seq = []
    for a, b, d in edges:
        succ[a].append((b, d)); pred[b].append(a); left[b] += 1
    ready = [n for n in range(N) if not left[n]]; done = set()
    while ready:
        n = min(ready, key=lambda n: (n in before and before[n] not in done, st[n], n)); ready.remove(n); done.add(n); seq.append(n)
        if n in named:
            st[n] = max(st[n], free.get(eng[n], 0.0)); free[eng[n]] = st[n] + dur[n]
        for b, d in succ[n]:
            st[b] = max(st[b], st[n] + dur[n] + d); left[b] -= 1
            if not left[b]:
                ready.append(b)
    for n in reversed(seq):
        if n not in named and succ[n] and eng[n] in "vap":
            st[n] = min(st[b] - d for b, d in succ[n]) - dur[n]
    for n in seq:
        st[n] = max([st[n]] + [st[a] + 1e-4 for a in pred[n]])
    return st


def polish(eng, dur, edges, st):
    N = len(eng); gap = {}
    for a, b, d in edges:
        gap[(a, b)] = max(gap.get((a, b), 0.0), d + dur[a])
    succ = [[] for e in eng]; pred = [[] for e in eng]
    for (a, b), d in gap.items():
        succ[a].append((b, d)); pred[b].append((a, d))
    order = sorted(range(N), key=lambda n: (st[n], n)); rnd = numpy.random.RandomState(SEED)

    def heads():
        st = [0.0] * N; free = {}
        for n in order:
            st[n] = max([st[a] + d for a, d in pred[n]] + [free.get(eng[n], 0.0) * (eng[n] != "x")]); free[eng[n]] = st[n] + dur[n]
        return st
    for t0 in [WIDTH / 2 * k for s in range(SWEEPS) for k in range(int(300 / WIDTH))]:
        st = heads(); order.sort(key=lambda n: st[n]); tail = [0.0] * N; after = {}
        for n in reversed(order):
            tail[n] = max([tail[b] + d for b, d in succ[n]] + [dur[n] + after.get(eng[n], 0.0) * (eng[n] != "x")]); after[eng[n]] = tail[n]
        W = [n for n in order if t0 <= st[n] < t0 + WIDTH]
        if not W:
            continue
        i0 = order.index(W[0]); M = len(W); m = {n: i for i, n in enumerate(W)}; free = {}; after = {}; line = {}
        head = [max([st[a] + d for a, d in pred[n] if a not in m] + [0.0]) for n in W]
        rest = [max([tail[b] + d for b, d in succ[n] if b not in m] + [dur[n]]) for n in W]
        sc = [[(m[b], d) for b, d in succ[n] if b in m] for n in W]; wait = [sum(a in m for a, d in pred[n]) for n in W]; du = [dur[n] for n in W]
        for n in order[:i0]:
            free[eng[n]] = st[n] + dur[n]
        for n in reversed(order[i0 + M:]):
            after[eng[n]] = tail[n]
        for i, n in enumerate(W):
            if eng[n] != "x":
                line.setdefault(eng[n], []).append(i)
        nx = [-1] * M; pv = [-1] * M

        def relink(l):
            for j, i in enumerate(l):
                pv[i] = l[j - 1] if j else -1; nx[i] = l[j + 1] if j + 1 < len(l) else -1

        def run():
            left = [x + (p >= 0) for x, p in zip(wait, pv)]; s = list(head); by = [-1] * M
            for e, l in line.items():
                s[l[0]] = max(s[l[0]], free.get(e, 0.0))
            q = [i for i in range(M) if not left[i]]
            for i in q:
                t = s[i]
                for b, d in sc[i]:
                    if t + d > s[b]:
                        s[b] = t + d; by[b] = i
                    left[b] -= 1
                    if not left[b]:
                        q.append(b)
                b = nx[i]
                if b >= 0:
                    if t + du[i] >= s[b]:
                        s[b] = t + du[i]; by[b] = i
                    left[b] -= 1
                    if not left[b]:
                        q.append(b)
            if len(q) < M:
                return 1e9, q, []
            v, i = max([(s[i] + rest[i], i) for i in range(M)] + [(s[l[-1]] + du[l[-1]] + after.get(e, 0.0), l[-1]) for e, l in line.items()])
            on = []
            while by[i] >= 0:
                if pv[i] == by[i] and (W[by[i]], W[i]) not in gap:
                    on.append(i)
                i = by[i]
            return v, q, on
        for l in line.values():
            relink(l)
        cur, q, on = run(); best = (cur, q)
        for it, (u, k, up, z) in enumerate(rnd.random_sample((MOVES, 4)).tolist()):
            if not on:
                break
            x = on[int(u * len(on))]; l = line[eng[W[x]]]; i = l.index(x); k = (1, 1, 1, 2, 2, 3, 4, 6, 9)[int(9 * k)]; old = list(l)
            if up < 0.5:
                l.insert(max(i - k, 0), l.pop(i))
            else:
                l.insert(min(i - 1 + k, len(l) - 1), l.pop(i - 1))
            relink(l); v, q, o2 = run()
            if v - cur <= -(HEAT * (1 - it / MOVES) + 0.002) * math.log(z + 1e-12):
                cur, on = v, o2; best = min(best, (v, q))
            else:
                l[:] = old; relink(l)
        order[i0:i0 + M] = [W[i] for i in best[1]]
    return heads()


KEPT = []


def schedule(ops):
    if not KEPT:
        eng, dur, edges = graph(ops)
        st = polish(eng, dur, edges, first(ops, eng, dur, edges))
        KEPT.append((st, max(t + d for t, d in zip(st, dur)) + 0.5))
    st, end = KEPT[0]
    for n, o in enumerate(ops):
        o["st"] = st[n]
    return sorted(range(len(ops)), key=lambda n: (st[n], n)), end


def rank_program(g, core, T, topo):
    rank = T.rank_of(core)
    if rank is None:
        return
    ops, nout = build(T, topo, core, rank)
    link(ops)
    order, end = schedule(ops)
    Q = {"g": g, "v": g.vector, "a": g.scalar, "p": g.tensor, "s": g.sync}
    cnt = {"v": 0, "a": 0, "p": 0, "g": 0}; seen = {e: {} for e in Q}; nd = [0]; total = {}
    for n in order:
        o = ops[n]; e = o["e"]
        if o["k"] == "x":
            total[o["sem"][0]] = o["sem"][1]
            continue
        need = {}
        for d, data in o["dep"].items():
            p = ops[d]
            if p["k"] == "c" and p["e"] == e and o["k"] == "c" and (e == "p" or not data):
                continue
            s, val = p["sem"]
            need[s] = max(need.get(s, 0), val)
        for s, val in need.items():
            if seen[e].get(s, 0) < val:
                Q[e].wait_ge(T.sem[s], val); seen[e][s] = val
        if o["k"] == "c":
            cnt[e] += 1; o["sem"] = ("c" + e, cnt[e])
            o["fn"](Q[e]).then_inc(T.sem["c" + e], 1)
        else:
            s = "d%d" % nd[0]; nd[0] += 1
            if o["k"] == "d":
                o["sem"] = (s, 16); o["fn"](Q[e]).then_inc(T.sem[s], 16)
            else:
                o["sem"] = (s, nout); o["fn"](Q[e], T.sem[s])
        total[o["sem"][0]] = o["sem"][1]
    for s, val in total.items():
        g.wait_ge(T.sem[s], val)
